import numpy as np
import ml_dtypes


def mxq(x, axis, fmt="e4m3"):
    dtype, down = {"e4m3": (ml_dtypes.float8_e4m3fn, 7), "e5m2": (ml_dtypes.float8_e5m2, 14)}[fmt]
    v = np.moveaxis(np.asarray(x, np.float32).astype(ml_dtypes.bfloat16).astype(np.float64), axis, -1)
    blocks = v.reshape(v.shape[:-1] + (-1, 32))
    amax = np.abs(blocks).max(-1, keepdims=True)
    byte = np.maximum(np.where(amax > 0, np.frexp(amax)[1] - 1 + 127, 0) - down, 1)
    scale = np.exp2(byte - 127.0)
    codes = (blocks / scale).astype(np.float32).astype(dtype).astype(np.float64)
    return np.moveaxis((codes * scale).reshape(v.shape), -1, axis)


WIDE = False


def mx_kscale(k):
    if not WIDE:
        return np.ones(k)
    levels = np.array([10, -10, 5, -5, 0])
    if k % 512:
        return np.exp2(np.random.permutation(np.resize(levels, k // 32))).repeat(32)
    a = np.empty((k // 512, 16))
    for p in range(k // 512):
        a[p, :8] = np.random.permutation(np.resize(levels, 8))
        for g in range(8):
            far = levels[np.abs(levels - a[p, g]) >= 10]
            a[p, g + 8] = far[np.random.randint(len(far))]
    return np.exp2(a.ravel()).repeat(32)


def f64(x):
    return np.asarray(x).astype(np.float64)


def striped(idx):
    return np.tile(idx.reshape(-1, 16).T, (8, 1)).astype(np.uint16)


def unstriped(offs):
    return offs[:16].T.reshape(-1).astype(np.int64)


E2M1 = np.array([0.0, 0.5, 1.0, 1.5, 2.0, 3.0, 4.0, 6.0, -0.0, -0.5, -1.0, -1.5, -2.0, -3.0, -4.0, -6.0])


def pack_weight(w, fmt):
    k, n = w.shape
    w = f64(np.asarray(w, np.float32).astype(ml_dtypes.bfloat16)).reshape(k // 32, 32, n)
    amax = np.abs(w).max(1)
    if fmt == "e4m3":
        byte = np.frexp(amax)[1] - 1 + 127 - 7
    else:
        mant, ex = np.frexp(amax / 6.0)
        byte = np.where(mant > 0.5, ex, ex - 1) + 127
    byte = np.clip(np.where(amax > 0, byte, 1), 1, 254)
    scaled = (w * np.exp2(127.0 - byte)[:, None, :]).reshape(k, n).astype(np.float32)
    by_word = np.ascontiguousarray(scaled.reshape(k // 512, 128, 4, n).transpose(0, 1, 3, 2))
    if fmt == "e4m3":
        words = by_word.astype(ml_dtypes.float8_e4m3fn).view(np.uint8)
    else:
        c = by_word.astype(ml_dtypes.float4_e2m1fn).view(np.uint8) & 0xF
        words = (c[..., 0::2] | (c[..., 1::2] << 4)).reshape(k // 512, 128, 2 * n)
    return np.ascontiguousarray(words), np.ascontiguousarray(byte.astype(np.uint8).reshape(k // 512, 16, n))


def unpack_weight(words, scales, fmt):
    g, _, n = scales.shape
    words = np.ascontiguousarray(words).reshape(g, 128, n, -1)
    if fmt == "e4m3":
        vals = words.view(ml_dtypes.float8_e4m3fn).astype(np.float64)
    else:
        nib = np.empty((g, 128, n, 4), np.uint8)
        nib[..., 0::2] = words & 0xF
        nib[..., 1::2] = words >> 4
        vals = E2M1[nib]
    vals = vals * np.repeat(np.exp2(scales.astype(np.float64) - 127.0), 8, axis=1)[..., None]
    return vals.transpose(0, 1, 3, 2).reshape(g * 512, n)


def gelu(v):
    return 0.5 * v * (1.0 + np.tanh(np.sqrt(2.0 / np.pi) * (v + 0.044715 * v**3)))


def bf(x):
    return np.asarray(x, np.float32).astype(ml_dtypes.bfloat16)


def planes(Y):
    n, m = Y.shape
    b = f64(bf(Y)).reshape(n // 32, 32, m)
    amax = np.abs(b).max(1)
    byte = np.clip(np.where(amax > 0, np.frexp(amax)[1] - 1 + 127 - 7, 1), 1, 254)
    codes = (b * np.exp2(127.0 - byte)[:, None, :]).reshape(n, m).astype(np.float32).astype(ml_dtypes.float8_e4m3fn).view(np.uint8)
    words = codes.reshape(n // 512, 128, 4, m).transpose(0, 1, 3, 2)
    return np.ascontiguousarray(words), np.ascontiguousarray(byte.astype(np.uint8).reshape(n // 512, 16, m))


K, H, N, T, S, T2 = 1024, 1024, 768, 2048, 512, 1024

def setup_inputs():
    n = np.random.standard_normal
    s = mx_kscale(K)[:, None]
    u = mx_kscale(H)[:, None]
    tab_words, tab_scales = pack_weight(n((K, T)) * s, "e4m3")
    w2_words, w2_scales = pack_weight(n((K, H)) / np.sqrt(K) / s, "e2m1")
    w4_words, w4_scales = pack_weight(n((H, N)) / np.sqrt(H) / u, "e2m1")
    return {
        "tab_words": tab_words, "tab_scales": tab_scales,
        "offs": striped(np.random.permutation(T)[:S]),
        "offs2": striped(np.random.permutation(T2)[:S]),
        "w1": (n((K, H)) / np.sqrt(K) / s * u.T).astype(np.float32),
        "w2_words": w2_words, "w2_scales": w2_scales,
        "wgs": np.exp(0.3 * n((128, S))).astype(np.float32),
        "page0": (n((H, T2)) * u).astype(np.float32),
        "w3": (n((H, N)) / np.sqrt(H) / u).astype(np.float32),
        "w4_words": w4_words, "w4_scales": w4_scales,
        "prev": n((N, T2)).astype(np.float32),
    }

def reference(tab_words, tab_scales, offs, offs2, w1, w2_words, w2_scales, wgs, page0, w3, w4_words, w4_scales, prev):
    v = unpack_weight(tab_words, tab_scales, "e4m3")[:, unstriped(offs)]
    taste = mxq(f64(w1), 0, "e4m3").T @ v
    recent = unpack_weight(w2_words, w2_scales, "e2m1").T @ v
    h = taste * recent
    page = f64(page0).copy()
    page[:, unstriped(offs2)] = np.tile(f64(wgs), (H // 128, 1)) * h
    words, scales = planes(page)
    pq = mxq(page, 0, "e4m3")
    gate = 1.0 / (1.0 + np.exp(-(mxq(f64(w3), 0, "e4m3").T @ pq)))
    fresh = unpack_weight(w4_words, w4_scales, "e2m1").T @ pq
    old = f64(prev)
    y = old + gate * (fresh - old)
    return y, page, words, scales

@@ -1,0 +1,340 @@
+from contextlib import ExitStack
+
+import concourse.mybir as mybir
+from concourse.masks import make_identity
+
+K, H, N, T, S, T2 = 1024, 1024, 768, 2048, 512, 1024
+FLOPS = 2 * (2 * K * H * S) + 2 * (2 * H * N * T2)
+
+F32 = mybir.dt.float32
+BF16 = mybir.dt.bfloat16
+I32 = mybir.dt.int32
+U32 = mybir.dt.uint32
+U16 = mybir.dt.uint16
+U8 = mybir.dt.uint8
+FP8X4 = mybir.dt.float8_e4m3fn_x4
+FP4X4 = mybir.dt.float4_e2m1fn_x4
+MULT = mybir.AluOpType.mult
+SUB = mybir.AluOpType.subtract
+SIGMOID = mybir.ActivationFunctionType.Sigmoid
+
+P = 128
+PACK = 4
+K_PASS = P * PACK
+PASSES = K // K_PASS
+BANK = 512
+ROW_TILES = H // P
+TILES_PER_PASS = K_PASS // P
+HALVES = T2 // BANK
+OUT_TILES = N // P
+W1_CHUNKS = (128, 128, 256, 256, 256)
+W3_CHUNK = 256
+
+
+def tile_list_shelf_suggester_kernel(
+    tc, tab_words, tab_scales, offs, offs2, w1, w2_words, w2_scales, wgs, page0, w3, w4_words, w4_scales, prev,
+    out_0, out_1, out_2, out_3,
+):
+    nc = tc.nc
+    with ExitStack() as ctx:
+        keep = ctx.enter_context(tc.tile_pool(name="keep", bufs=1))
+        psum = ctx.enter_context(tc.psum_pool(name="psum", bufs=1))
+
+        def sbuf(name, shape, dtype, tag=None):
+            return keep.tile(shape, dtype, name=name, tag=tag or name, align_bytes=64)
+
+        banks = [psum.tile([P, BANK], F32, name=f"bank{i}") for i in range(8)]
+
+        pick_list = keep.tile([P, S // 16], U16, name="pick_list")
+        put_list = keep.tile([P, S // 16], U16, name="put_list")
+        identity = sbuf("identity", [P, P], F32)
+        table_words = [sbuf(f"table_words{a}", [P, T], I32) for a in range(PASSES)]
+        table_scales = sbuf("table_scales", [P, PASSES, T], U8)
+        picked_words = [sbuf(f"picked_words{a}", [P, S], U32) for a in range(PASSES)]
+        picked_scales = [sbuf(f"picked_scales{a}", [P, S], U8) for a in range(PASSES)]
+        w2_codes = [sbuf(f"w2_codes{g}", [P, PASSES, 2 * K_PASS], U8) for g in range(PASSES)]
+        w2_plane = sbuf("w2_plane", [P, PASSES, H], U8)
+        w4_codes = sbuf("w4_codes", [P, PASSES, 2 * N], U8)
+        w4_plane = sbuf("w4_plane", [P, PASSES, N], U8)
+        weights = sbuf("weights", [P, S], F32)
+        page = [sbuf(f"page{b}", [P, T2], F32) for b in range(ROW_TILES)]
+        widths = list(W1_CHUNKS) + [W3_CHUNK] * (N // W3_CHUNK)
+        raw = [
+            [sbuf(f"raw{u}_0", [P, PACK, w], F32, tag=f"slot{u - 1}" if u >= 2 else None), sbuf(f"raw{u}_1", [P, PACK, w], F32)]
+            for u, w in enumerate(widths)
+        ]
+        w1_raw, w3_raw = raw[: len(W1_CHUNKS)], raw[len(W1_CHUNKS) :]
+        old = [sbuf(f"old{c}", [P, W3_CHUNK // P, T2], F32) for c in range(N // W3_CHUNK)]
+        staged = [sbuf(f"staged{i}", [P, PASSES * W3_CHUNK * PACK], BF16) for i in range(2)]
+        w1_codes, w3_codes, page_codes = {}, {}, {}
+        w1_plane = [sbuf(f"w1_plane{c}", [P, PASSES * w], U8) for c, w in enumerate(W1_CHUNKS)]
+        w3_plane = [sbuf(f"w3_plane{c}", [P, PASSES * W3_CHUNK], U8) for c in range(N // W3_CHUNK)]
+        recent = {}
+        product = [sbuf(f"product{i}", [P, S], F32) for i in range(2)]
+        turned = [[sbuf(f"turned{g}_{h}", [P, PACK * K_PASS], BF16) for h in range(HALVES)] for g in range(PASSES)]
+        grouped = [sbuf(f"grouped{h}", [P, BANK * PACK], BF16) for h in range(HALVES)]
+        page_plane = sbuf("page_plane", [P, PASSES, T2], U8)
+        rest = [sbuf(f"rest{i}", [P, BANK], F32) for i in range(3)]
+        step = [sbuf(f"step{i}", [P, BANK], F32) for i in range(3)]
+
+        nc.vector.memset(table_scales[:].bitcast(I32), 0)
+        nc.vector.memset(w2_plane[:].bitcast(I32), 0)
+        nc.gpsimd.memset(w4_plane[:].bitcast(I32), 0)
+        make_identity(nc, identity[:])
+
+        def load_plane(plane, scales):
+            rows = scales.bitcast(I32)
+            for q in range(4):
+                nc.sync.dma_start(
+                    out=plane[32 * q : 32 * q + 4].bitcast(I32),
+                    in_=rows[:, 4 * q : 4 * q + 4, :].rearrange("a r n -> r a n"),
+                )
+
+        def load_weight(pair, w, first, passes=range(PASSES)):
+            for a in passes:
+                width = pair[a].shape[2]
+                rows = w[a * K_PASS : (a + 1) * K_PASS, first : first + width]
+                nc.sync.dma_start(out=pair[a][:], in_=rows.rearrange("(p j) c -> p j c", j=PACK))
+
+        def load_w1(c, passes=range(PASSES)):
+            load_weight(w1_raw[c], w1, sum(W1_CHUNKS[:c]), passes)
+
+        def load_unit(u, a):
+            if u < len(W1_CHUNKS):
+                load_w1(u, (a,))
+            else:
+                load_weight(raw[u], w3, (u - len(W1_CHUNKS)) * W3_CHUNK, (a,))
+
+        def load_table_words(a, pieces):
+            words = tab_words[a].rearrange("p t i -> p (t i)").bitcast(I32)
+            for i in range(pieces):
+                cols = slice(i * T // pieces, (i + 1) * T // pieces)
+                nc.sync.dma_start(out=table_words[a][:, cols], in_=words[:, cols])
+
+        def load_w2(g):
+            words = w2_words.bitcast(I32)[:, :, g * K_PASS // 2 : (g + 1) * K_PASS // 2]
+            nc.sync.dma_start(out=w2_codes[g][:].bitcast(I32), in_=words.rearrange("a p n -> p a n"))
+
+        def load_page(b):
+            nc.sync.dma_start(out=page[b][:], in_=page0[b * P : (b + 1) * P, :])
+
+        def load_old(c):
+            rows = prev[c * W3_CHUNK : (c + 1) * W3_CHUNK, :]
+            nc.sync.dma_start(out=old[c][:], in_=rows.rearrange("(i p) m -> p i m", p=P))
+
+        nc.sync.dma_start(pick_list[:], offs)
+        nc.sync.dma_start(put_list[:], offs2)
+        load_w1(0, (0,))
+        load_table_words(0, 4)
+        load_w2(0)
+        load_plane(table_scales, tab_scales)
+        load_table_words(1, 1)
+        load_plane(w2_plane, w2_scales)
+        load_w1(0, (1,))
+        load_w1(1)
+        nc.sync.dma_start(out=weights[:], in_=wgs)
+        load_page(0)
+        load_w1(2)
+        for u in range(3, len(widths)):
+            if u == len(W1_CHUNKS):
+                load_w2(1)
+            load_unit(u, 0)
+            load_page(u - 2)
+            load_unit(u, 1)
+        nc.sync.dma_start(out=w4_codes[:].bitcast(I32), in_=w4_words.bitcast(I32).rearrange("a p n -> p a n"))
+        load_plane(w4_plane, w4_scales)
+        load_page(6)
+        load_page(7)
+        load_old(0)
+        load_old(1)
+        load_old(2)
+
+        def stage_weight(unit, passes=range(PASSES)):
+            width = widths[unit]
+            stage = staged[unit % len(staged)]
+            for a in passes:
+                dst = stage[:, a * width * PACK : (a + 1) * width * PACK].rearrange("p (c i j) -> p c j i", i=4, j=PACK)
+                nc.scalar.copy(out=dst, in_=raw[unit][a][:].rearrange("p j (c i) -> p c j i", i=4))
+
+        def quantize_weight(unit, plane, tag):
+            words = plane.shape[1]
+            codes = sbuf(f"codes{unit}", [P, words], U32, tag=tag)
+            stage = staged[unit % len(staged)]
+            nc.vector.quantize_mx(out=codes[:].bitcast(FP8X4), scales=plane[:], in_=stage[:, : words * PACK])
+            return codes
+
+        def w1_place(b):
+            c = max(i for i in range(len(W1_CHUNKS)) if sum(W1_CHUNKS[:i]) <= b * P)
+            return c, b * P - sum(W1_CHUNKS[:c])
+
+        def recent_product(b):
+            bank = banks[2 + 4 * (b % 2)]
+            g, col = divmod(b * P, K_PASS)
+            for a in range(PASSES):
+                nc.tensor.matmul_mx(
+                    out=bank[:],
+                    lhsT=w2_codes[g][:, a, 2 * col : 2 * (col + P)].bitcast(FP4X4),
+                    lhsT_scale=w2_plane[:, a, b * P : (b + 1) * P],
+                    rhs=picked_words[a][:].bitcast(FP8X4), rhs_scale=picked_scales[a][:],
+                    start=(a == 0), stop=(a == PASSES - 1),
+                )
+            recent[b] = sbuf(f"recent{b}", [P, S], F32, tag=f"slot{b}")
+            nc.scalar.copy(out=recent[b][:], in_=bank[:])
+
+        def taste_product(b):
+            c, first = w1_place(b)
+            for a in range(PASSES):
+                w1_cols = slice(a * W1_CHUNKS[c] + first, a * W1_CHUNKS[c] + first + P)
+                nc.tensor.matmul_mx(
+                    out=banks[b % 2][:],
+                    lhsT=w1_codes[c][:, w1_cols].bitcast(FP8X4),
+                    lhsT_scale=w1_plane[c][:, w1_cols],
+                    rhs=picked_words[a][:].bitcast(FP8X4), rhs_scale=picked_scales[a][:],
+                    start=(a == 0), stop=(a == PASSES - 1),
+                )
+
+        def multiply(b):
+            nc.vector.tensor_tensor(out=product[b % 2][:], in0=banks[b % 2][:], in1=recent[b][:], op=MULT)
+
+        def scatter(b):
+            nc.vector.tensor_tensor(page[b][:].indirect(put_list[:]), product[b % 2][:], weights[:], MULT)
+            nc.sync.dma_start(out=out_1[b * P : (b + 1) * P, :], in_=page[b][:])
+
+        def turn_page(b, engines):
+            g, q = divmod(b, TILES_PER_PASS)
+            for h in range(HALVES):
+                bank = banks[2 + 4 * (b % 2) + h]
+                for j in range(4):
+                    col = h * BANK + j * P
+                    nc.tensor.transpose(bank[:, j * P : (j + 1) * P], page[b][:, col : col + P], identity[:])
+                dst = turned[g][h][:].rearrange("m (j u p e) -> m j u p e", j=4, u=2, e=2)[:, :, :, 32 * q : 32 * (q + 1), :]
+                engines[h](out=dst, in_=bank[:].rearrange("m (j p u e) -> m j u p e", j=4, u=2, e=2))
+
+        def regroup_page(g, h, engines):
+            words = turned[g][h][:].bitcast(F32)
+            for s in range(2):
+                bank = banks[4 + 2 * g * h + s]
+                for i in range(4):
+                    col = (4 * s + i) * P
+                    nc.tensor.transpose(bank[:, i * P : (i + 1) * P], words[:, col : col + P], identity[:])
+                dst = grouped[h][:].bitcast(F32)[:, s * BANK : (s + 1) * BANK].rearrange("p (j m u) -> p j m u", j=2, u=2)
+                engines[s](out=dst, in_=bank[:].rearrange("p (j u m) -> p j m u", j=2, u=2))
+
+        def quantize_page(g, h):
+            cols = slice(h * BANK, (h + 1) * BANK)
+            nc.vector.quantize_mx(out=page_codes[g][:, cols].bitcast(FP8X4), scales=page_plane[:, g, cols], in_=grouped[h][:])
+
+        def store_codes(g):
+            nc.sync.dma_start(out=out_2[g].rearrange("p m t -> p (m t)").bitcast(I32), in_=page_codes[g][:].bitcast(I32))
+
+        units = [(n, h) for c in range(N // W3_CHUNK) for h in range(HALVES) for n in (2 * c, 2 * c + 1)]
+
+        def second_pass(i, g):
+            n, h = units[i]
+            cols = slice(h * BANK, (h + 1) * BANK)
+            moving = page_codes[g][:, cols].bitcast(FP8X4)
+            w3_cols = slice(g * W3_CHUNK + n % 2 * P, g * W3_CHUNK + (n % 2 + 1) * P)
+            nc.tensor.matmul_mx(
+                out=banks[2 * i % 8][:],
+                lhsT=w3_codes[n // 2][:, w3_cols].bitcast(FP8X4),
+                lhsT_scale=w3_plane[n // 2][:, w3_cols],
+                rhs=moving, rhs_scale=page_plane[:, g, cols],
+                start=(g == 0), stop=(g == PASSES - 1),
+            )
+            nc.tensor.matmul_mx(
+                out=banks[(2 * i + 1) % 8][:],
+                lhsT=w4_codes[:, g, 2 * n * P : 2 * (n + 1) * P].bitcast(FP4X4),
+                lhsT_scale=w4_plane[:, g, n * P : (n + 1) * P],
+                rhs=moving, rhs_scale=page_plane[:, g, cols],
+                start=(g == 0), stop=(g == PASSES - 1),
+            )
+
+        def scores(i):
+            n, h = units[i]
+            return old[n // 2][:, n % 2, h * BANK : (h + 1) * BANK]
+
+        def blend_begin(i):
+            ring = i % len(step)
+            nc.scalar.activation(out=rest[ring][:], in_=banks[2 * i % 8][:], func=SIGMOID, scale=-1.0)
+            nc.vector.tensor_tensor(out=step[ring][:], in0=banks[(2 * i + 1) % 8][:], in1=scores(i), op=SUB)
+            engine = nc.vector if i == len(units) - 1 else nc.gpsimd
+            engine.tensor_tensor(out=step[ring][:], in0=step[ring][:], in1=rest[ring][:], op=MULT)
+
+        def blend_end(i):
+            n, h = units[i]
+            nc.vector.tensor_tensor(out=scores(i), in0=banks[(2 * i + 1) % 8][:], in1=step[i % len(step)][:], op=SUB)
+            nc.sync.dma_start(out=out_0[n * P : (n + 1) * P, h * BANK : (h + 1) * BANK], in_=scores(i))
+
+        on_scalar = (nc.scalar.copy, nc.scalar.copy)
+        shared = (nc.scalar.copy, nc.vector.tensor_copy)
+
+        n_w1 = len(W1_CHUNKS)
+        planes = w1_plane + w3_plane
+        w1_codes[0] = sbuf("codes0", [P, PASSES * P], U32)
+        for a in range(PASSES):
+            cols = slice(a * P, (a + 1) * P)
+            stage_weight(0, (a,))
+            nc.vector.tensor_copy(picked_scales[a][:], table_scales[:, a, :].indirect(pick_list[:]))
+            nc.vector.tensor_copy(picked_words[a][:], table_words[a][:].bitcast(U32).indirect(pick_list[:]))
+            nc.vector.quantize_mx(
+                out=w1_codes[0][:, cols].bitcast(FP8X4), scales=planes[0][:, cols],
+                in_=staged[0][:, a * K_PASS : (a + 1) * K_PASS],
+            )
+        last = ROW_TILES - 1
+        stage_weight(1)
+        recent_product(0)
+        taste_product(0)
+        stage_weight(2, (0,))
+        recent_product(1)
+        stage_weight(2, (1,))
+        for b in range(ROW_TILES):
+            multiply(b)
+            unit = b + 1
+            if unit < len(widths):
+                codes = quantize_weight(unit, planes[unit], None)
+                if unit < n_w1:
+                    w1_codes[unit] = codes
+                else:
+                    w3_codes[unit - n_w1] = codes
+            if b == last - 1:
+                page_codes[0] = sbuf("page_codes0", [P, T2], U32, tag=f"slot{b}")
+                for h in range(HALVES):
+                    quantize_page(0, h)
+                store_codes(0)
+            scatter(b)
+            if b < last:
+                taste_product(b + 1)
+            if b + 3 < len(widths):
+                stage_weight(b + 3, (0,))
+            if b + 2 < ROW_TILES:
+                recent_product(b + 2)
+            if b + 3 < len(widths):
+                stage_weight(b + 3, (1,))
+            if b == last:
+                second_pass(0, 0)
+                second_pass(1, 0)
+            turn_page(b, shared if b == last else on_scalar)
+            if b == TILES_PER_PASS:
+                for h in range(HALVES):
+                    regroup_page(0, h, on_scalar)
+
+        page_codes[1] = sbuf("page_codes1", [P, T2], U32)
+        for h in range(HALVES):
+            regroup_page(1, h, shared)
+            quantize_page(1, h)
+        store_codes(1)
+        scale_rows = out_3.bitcast(I32)
+        for q in range(4):
+            nc.sync.dma_start(
+                out=scale_rows[:, 4 * q : 4 * q + 4, :].rearrange("g r m -> r g m"),
+                in_=page_plane[32 * q : 32 * q + 4].bitcast(I32),
+            )
+
+        for i in range(len(units)):
+            if i >= 2:
+                second_pass(i, 0)
+            second_pass(i, 1)
+            blend_begin(i)
+            if i >= 1:
+                blend_end(i - 1)
+        blend_end(len(units) - 1)

@@ -27,7 +27,7 @@ ROW_TILES = H // P
 TILES_PER_PASS = K_PASS // P
 HALVES = T2 // BANK
 OUT_TILES = N // P
-W1_CHUNKS = (128, 128, 256, 256, 256)
+W1_CHUNKS = (256, 256, 256, 256)
 W3_CHUNK = 256
 
 
@@ -59,23 +59,28 @@ def tile_list_shelf_suggester_kernel(
         weights = sbuf("weights", [P, S], F32)
         page = [sbuf(f"page{b}", [P, T2], F32) for b in range(ROW_TILES)]
         widths = list(W1_CHUNKS) + [W3_CHUNK] * (N // W3_CHUNK)
-        raw = [
-            [sbuf(f"raw{u}_0", [P, PACK, w], F32, tag=f"slot{u - 1}" if u >= 2 else None), sbuf(f"raw{u}_1", [P, PACK, w], F32)]
-            for u, w in enumerate(widths)
+        first_tile = [sum(W1_CHUNKS[:c]) // P for c in range(len(W1_CHUNKS))]
+        w1_raw = [
+            [sbuf(f"raw{c}_0", [P, PACK, w], F32), sbuf(f"raw{c}_1", [P, PACK, w], F32, tag=f"slot{first_tile[c] - 1}")]
+            for c, w in enumerate(W1_CHUNKS)
         ]
-        w1_raw, w3_raw = raw[: len(W1_CHUNKS)], raw[len(W1_CHUNKS) :]
+        w3_first = [sbuf(f"w3_first{a}", [P, PACK, W3_CHUNK], F32) for a in range(PASSES)]
+        w3_rest = [sbuf(f"w3_rest{a}", [P, PACK, N - W3_CHUNK], F32) for a in range(PASSES)]
+        raw = [[t[:] for t in pair] for pair in w1_raw + [w3_first]] + [
+            [t[:, :, c * W3_CHUNK : (c + 1) * W3_CHUNK] for t in w3_rest] for c in range(N // W3_CHUNK - 1)
+        ]
         old = [sbuf(f"old{c}", [P, W3_CHUNK // P, T2], F32) for c in range(N // W3_CHUNK)]
-        staged = [sbuf(f"staged{i}", [P, PASSES * W3_CHUNK * PACK], BF16) for i in range(2)]
-        w1_codes, w3_codes, page_codes = {}, {}, {}
+        ring = [sbuf(f"staged{i}", [P, PASSES * W3_CHUNK * PACK], BF16) for i in range(2)]
+        staged = {u: ring[i % 2] for i, u in enumerate((0, 1, 4, 2, 3, 5, 6))}
+        w1_codes, w3_codes = {}, {}
+        page_codes = [sbuf(f"page_codes{g}", [P, T2], U32) for g in range(PASSES)]
         w1_plane = [sbuf(f"w1_plane{c}", [P, PASSES * w], U8) for c, w in enumerate(W1_CHUNKS)]
         w3_plane = [sbuf(f"w3_plane{c}", [P, PASSES * W3_CHUNK], U8) for c in range(N // W3_CHUNK)]
-        recent = {}
-        product = [sbuf(f"product{i}", [P, S], F32) for i in range(2)]
+        taste = {}
+        product = [sbuf(f"product{i}", [P, S], F32) for i in range(ROW_TILES)]
         turned = [[sbuf(f"turned{g}_{h}", [P, PACK * K_PASS], BF16) for h in range(HALVES)] for g in range(PASSES)]
         grouped = [sbuf(f"grouped{h}", [P, BANK * PACK], BF16) for h in range(HALVES)]
         page_plane = sbuf("page_plane", [P, PASSES, T2], U8)
-        rest = [sbuf(f"rest{i}", [P, BANK], F32) for i in range(3)]
-        step = [sbuf(f"step{i}", [P, BANK], F32) for i in range(3)]
 
         nc.vector.memset(table_scales[:].bitcast(I32), 0)
         nc.vector.memset(w2_plane[:].bitcast(I32), 0)
@@ -99,17 +104,8 @@ def tile_list_shelf_suggester_kernel(
         def load_w1(c, passes=range(PASSES)):
             load_weight(w1_raw[c], w1, sum(W1_CHUNKS[:c]), passes)
 
-        def load_unit(u, a):
-            if u < len(W1_CHUNKS):
-                load_w1(u, (a,))
-            else:
-                load_weight(raw[u], w3, (u - len(W1_CHUNKS)) * W3_CHUNK, (a,))
-
-        def load_table_words(a, pieces):
-            words = tab_words[a].rearrange("p t i -> p (t i)").bitcast(I32)
-            for i in range(pieces):
-                cols = slice(i * T // pieces, (i + 1) * T // pieces)
-                nc.sync.dma_start(out=table_words[a][:, cols], in_=words[:, cols])
+        def load_table_words(a):
+            nc.sync.dma_start(out=table_words[a][:], in_=tab_words[a].rearrange("p t i -> p (t i)").bitcast(I32))
 
         def load_w2(g):
             words = w2_words.bitcast(I32)[:, :, g * K_PASS // 2 : (g + 1) * K_PASS // 2]
@@ -124,42 +120,45 @@ def tile_list_shelf_suggester_kernel(
 
         nc.sync.dma_start(pick_list[:], offs)
         nc.sync.dma_start(put_list[:], offs2)
+        load_table_words(0)
         load_w1(0, (0,))
-        load_table_words(0, 4)
         load_w2(0)
         load_plane(table_scales, tab_scales)
-        load_table_words(1, 1)
-        load_plane(w2_plane, w2_scales)
         load_w1(0, (1,))
-        load_w1(1)
+        load_table_words(1)
+        load_plane(w2_plane, w2_scales)
         nc.sync.dma_start(out=weights[:], in_=wgs)
         load_page(0)
+        load_w1(1)
+        load_page(1)
+        load_weight(w3_first, w3, 0)
+        load_page(2)
         load_w1(2)
-        for u in range(3, len(widths)):
-            if u == len(W1_CHUNKS):
-                load_w2(1)
-            load_unit(u, 0)
-            load_page(u - 2)
-            load_unit(u, 1)
+        load_page(3)
+        load_w2(1)
+        load_page(4)
+        load_w1(3)
+        load_weight(w3_rest, w3, W3_CHUNK)
+        load_page(5)
+        load_page(6)
         nc.sync.dma_start(out=w4_codes[:].bitcast(I32), in_=w4_words.bitcast(I32).rearrange("a p n -> p a n"))
         load_plane(w4_plane, w4_scales)
-        load_page(6)
-        load_page(7)
         load_old(0)
         load_old(1)
+        load_page(7)
         load_old(2)
 
         def stage_weight(unit, passes=range(PASSES)):
             width = widths[unit]
-            stage = staged[unit % len(staged)]
+            stage = staged[unit]
             for a in passes:
                 dst = stage[:, a * width * PACK : (a + 1) * width * PACK].rearrange("p (c i j) -> p c j i", i=4, j=PACK)
-                nc.scalar.copy(out=dst, in_=raw[unit][a][:].rearrange("p j (c i) -> p c j i", i=4))
+                nc.scalar.copy(out=dst, in_=raw[unit][a].rearrange("p j (c i) -> p c j i", i=4))
 
         def quantize_weight(unit, plane, tag):
             words = plane.shape[1]
             codes = sbuf(f"codes{unit}", [P, words], U32, tag=tag)
-            stage = staged[unit % len(staged)]
+            stage = staged[unit]
             nc.vector.quantize_mx(out=codes[:].bitcast(FP8X4), scales=plane[:], in_=stage[:, : words * PACK])
             return codes
 
@@ -167,8 +166,12 @@ def tile_list_shelf_suggester_kernel(
             c = max(i for i in range(len(W1_CHUNKS)) if sum(W1_CHUNKS[:i]) <= b * P)
             return c, b * P - sum(W1_CHUNKS[:c])
 
+        def bank_pair(b):
+            first = 4 if b == ROW_TILES - 1 else 6 - 4 * (b % 2)
+            return banks[first : first + 2]
+
         def recent_product(b):
-            bank = banks[2 + 4 * (b % 2)]
+            bank = banks[(0, 1, 4, 5)[b % 4]]
             g, col = divmod(b * P, K_PASS)
             for a in range(PASSES):
                 nc.tensor.matmul_mx(
@@ -178,32 +181,35 @@ def tile_list_shelf_suggester_kernel(
                     rhs=picked_words[a][:].bitcast(FP8X4), rhs_scale=picked_scales[a][:],
                     start=(a == 0), stop=(a == PASSES - 1),
                 )
-            recent[b] = sbuf(f"recent{b}", [P, S], F32, tag=f"slot{b}")
-            nc.scalar.copy(out=recent[b][:], in_=bank[:])
 
         def taste_product(b):
             c, first = w1_place(b)
-            for a in range(PASSES):
-                w1_cols = slice(a * W1_CHUNKS[c] + first, a * W1_CHUNKS[c] + first + P)
-                nc.tensor.matmul_mx(
-                    out=banks[b % 2][:],
-                    lhsT=w1_codes[c][:, w1_cols].bitcast(FP8X4),
-                    lhsT_scale=w1_plane[c][:, w1_cols],
-                    rhs=picked_words[a][:].bitcast(FP8X4), rhs_scale=picked_scales[a][:],
-                    start=(a == 0), stop=(a == PASSES - 1),
-                )
+            taste[b] = sbuf(f"taste{b}", [P, S], F32, tag=f"slot{b}")
+            for h in range(2):
+                picks = slice(h * S // 2, (h + 1) * S // 2)
+                bank = bank_pair(b)[h]
+                for a in range(PASSES):
+                    w1_cols = slice(a * W1_CHUNKS[c] + first, a * W1_CHUNKS[c] + first + P)
+                    nc.tensor.matmul_mx(
+                        out=bank[:, : S // 2],
+                        lhsT=w1_codes[c][:, w1_cols].bitcast(FP8X4),
+                        lhsT_scale=w1_plane[c][:, w1_cols],
+                        rhs=picked_words[a][:, picks].bitcast(FP8X4), rhs_scale=picked_scales[a][:, picks],
+                        start=(a == 0), stop=(a == PASSES - 1),
+                    )
+                nc.scalar.copy(out=taste[b][:, picks], in_=bank[:, : S // 2])
 
         def multiply(b):
-            nc.vector.tensor_tensor(out=product[b % 2][:], in0=banks[b % 2][:], in1=recent[b][:], op=MULT)
+            nc.vector.tensor_tensor(out=product[b % len(product)][:], in0=banks[(0, 1, 4, 5)[b % 4]][:], in1=weights[:], op=MULT)
 
         def scatter(b):
-            nc.vector.tensor_tensor(page[b][:].indirect(put_list[:]), product[b % 2][:], weights[:], MULT)
+            nc.vector.tensor_tensor(page[b][:].indirect(put_list[:]), product[b % len(product)][:], taste[b][:], MULT)
             nc.sync.dma_start(out=out_1[b * P : (b + 1) * P, :], in_=page[b][:])
 
         def turn_page(b, engines):
             g, q = divmod(b, TILES_PER_PASS)
             for h in range(HALVES):
-                bank = banks[2 + 4 * (b % 2) + h]
+                bank = bank_pair(b + 1)[h]
                 for j in range(4):
                     col = h * BANK + j * P
                     nc.tensor.transpose(bank[:, j * P : (j + 1) * P], page[b][:, col : col + P], identity[:])
@@ -213,7 +219,7 @@ def tile_list_shelf_suggester_kernel(
         def regroup_page(g, h, engines):
             words = turned[g][h][:].bitcast(F32)
             for s in range(2):
-                bank = banks[4 + 2 * g * h + s]
+                bank = banks[4 + 2 * h + s] if g else banks[2 - 2 * h + s]
                 for i in range(4):
                     col = (4 * s + i) * P
                     nc.tensor.transpose(bank[:, i * P : (i + 1) * P], words[:, col : col + P], identity[:])
@@ -229,20 +235,26 @@ def tile_list_shelf_suggester_kernel(
 
         units = [(n, h) for c in range(N // W3_CHUNK) for h in range(HALVES) for n in (2 * c, 2 * c + 1)]
 
+        def gate_bank(i):
+            return banks[2 * i % 8]
+
+        def fresh_bank(i):
+            return banks[(2 * i + 1) % 8]
+
         def second_pass(i, g):
             n, h = units[i]
             cols = slice(h * BANK, (h + 1) * BANK)
             moving = page_codes[g][:, cols].bitcast(FP8X4)
             w3_cols = slice(g * W3_CHUNK + n % 2 * P, g * W3_CHUNK + (n % 2 + 1) * P)
             nc.tensor.matmul_mx(
-                out=banks[2 * i % 8][:],
+                out=gate_bank(i)[:],
                 lhsT=w3_codes[n // 2][:, w3_cols].bitcast(FP8X4),
                 lhsT_scale=w3_plane[n // 2][:, w3_cols],
                 rhs=moving, rhs_scale=page_plane[:, g, cols],
                 start=(g == 0), stop=(g == PASSES - 1),
             )
             nc.tensor.matmul_mx(
-                out=banks[(2 * i + 1) % 8][:],
+                out=fresh_bank(i)[:],
                 lhsT=w4_codes[:, g, 2 * n * P : 2 * (n + 1) * P].bitcast(FP4X4),
                 lhsT_scale=w4_plane[:, g, n * P : (n + 1) * P],
                 rhs=moving, rhs_scale=page_plane[:, g, cols],
@@ -254,74 +266,70 @@ def tile_list_shelf_suggester_kernel(
             return old[n // 2][:, n % 2, h * BANK : (h + 1) * BANK]
 
         def blend_begin(i):
-            ring = i % len(step)
-            nc.scalar.activation(out=rest[ring][:], in_=banks[2 * i % 8][:], func=SIGMOID, scale=-1.0)
-            nc.vector.tensor_tensor(out=step[ring][:], in0=banks[(2 * i + 1) % 8][:], in1=scores(i), op=SUB)
-            engine = nc.vector if i == len(units) - 1 else nc.gpsimd
-            engine.tensor_tensor(out=step[ring][:], in0=step[ring][:], in1=rest[ring][:], op=MULT)
+            slot = i % len(step)
+            nc.scalar.activation(out=rest[slot][:], in_=gate_bank(i)[:], func=SIGMOID, scale=-1.0)
+            nc.vector.tensor_tensor(out=step[slot][:], in0=fresh_bank(i)[:], in1=scores(i), op=SUB)
+            engine = nc.vector if i in (0, len(units) - 1) else nc.gpsimd
+            engine.tensor_tensor(out=step[slot][:], in0=step[slot][:], in1=rest[slot][:], op=MULT)
 
         def blend_end(i):
             n, h = units[i]
-            nc.vector.tensor_tensor(out=scores(i), in0=banks[(2 * i + 1) % 8][:], in1=step[i % len(step)][:], op=SUB)
+            nc.vector.tensor_tensor(out=scores(i), in0=fresh_bank(i)[:], in1=step[i % len(step)][:], op=SUB)
             nc.sync.dma_start(out=out_0[n * P : (n + 1) * P, h * BANK : (h + 1) * BANK], in_=scores(i))
 
         on_scalar = (nc.scalar.copy, nc.scalar.copy)
-        shared = (nc.scalar.copy, nc.vector.tensor_copy)
+        shared = (nc.vector.tensor_copy, nc.scalar.copy)
 
         n_w1 = len(W1_CHUNKS)
         planes = w1_plane + w3_plane
-        w1_codes[0] = sbuf("codes0", [P, PASSES * P], U32)
+        stage_weight(0)
+        w1_codes[0] = quantize_weight(0, planes[0], None)
         for a in range(PASSES):
-            cols = slice(a * P, (a + 1) * P)
-            stage_weight(0, (a,))
             nc.vector.tensor_copy(picked_scales[a][:], table_scales[:, a, :].indirect(pick_list[:]))
             nc.vector.tensor_copy(picked_words[a][:], table_words[a][:].bitcast(U32).indirect(pick_list[:]))
-            nc.vector.quantize_mx(
-                out=w1_codes[0][:, cols].bitcast(FP8X4), scales=planes[0][:, cols],
-                in_=staged[0][:, a * K_PASS : (a + 1) * K_PASS],
-            )
         last = ROW_TILES - 1
-        stage_weight(1)
         recent_product(0)
         taste_product(0)
-        stage_weight(2, (0,))
-        recent_product(1)
-        stage_weight(2, (1,))
+        multiply(0)
+        stage_weight(1)
         for b in range(ROW_TILES):
-            multiply(b)
-            unit = b + 1
-            if unit < len(widths):
-                codes = quantize_weight(unit, planes[unit], None)
-                if unit < n_w1:
-                    w1_codes[unit] = codes
-                else:
-                    w3_codes[unit - n_w1] = codes
-            if b == last - 1:
-                page_codes[0] = sbuf("page_codes0", [P, T2], U32, tag=f"slot{b}")
+            if b + 1 in first_tile:
+                c = first_tile.index(b + 1)
+                w1_codes[c] = quantize_weight(c, planes[c], None)
+            if b == 2:
+                w3_codes[0] = quantize_weight(n_w1, planes[n_w1], None)
+            if b == last:
                 for h in range(HALVES):
                     quantize_page(0, h)
                 store_codes(0)
             scatter(b)
+            if b in (0, 2):
+                for ahead in range(max(1, 2 * b), 2 * b + TILES_PER_PASS):
+                    recent_product(ahead)
+                    multiply(ahead)
+            if b == 1:
+                stage_weight(n_w1)
+            if b + 2 in first_tile[2:]:
+                stage_weight(first_tile.index(b + 2))
             if b < last:
                 taste_product(b + 1)
-            if b + 3 < len(widths):
-                stage_weight(b + 3, (0,))
-            if b + 2 < ROW_TILES:
-                recent_product(b + 2)
-            if b + 3 < len(widths):
-                stage_weight(b + 3, (1,))
-            if b == last:
-                second_pass(0, 0)
-                second_pass(1, 0)
-            turn_page(b, shared if b == last else on_scalar)
-            if b == TILES_PER_PASS:
+            if b == last - 2:
                 for h in range(HALVES):
                     regroup_page(0, h, on_scalar)
+            if b >= last - 1:
+                stage_weight(n_w1 + 2 + b - last)
+            if b >= 1:
+                turn_page(b - 1, on_scalar)
+        second_pass(0, 0)
+        second_pass(1, 0)
+        turn_page(last, shared)
 
-        page_codes[1] = sbuf("page_codes1", [P, T2], U32)
-        for h in range(HALVES):
-            regroup_page(1, h, shared)
-            quantize_page(1, h)
+        w3_codes[1] = quantize_weight(n_w1 + 1, planes[n_w1 + 1], f"slot{last}")
+        regroup_page(1, 0, shared)
+        quantize_page(1, 0)
+        regroup_page(1, 1, on_scalar)
+        quantize_page(1, 1)
+        w3_codes[2] = quantize_weight(n_w1 + 2, planes[n_w1 + 2], "grouped0")
         store_codes(1)
         scale_rows = out_3.bitcast(I32)
         for q in range(4):
@@ -330,6 +338,8 @@ def tile_list_shelf_suggester_kernel(
                 in_=page_plane[32 * q : 32 * q + 4].bitcast(I32),
             )
 
+        rest = [sbuf(f"rest{i}", [P, BANK], F32, tag=f"raw{i}_0") for i in range(4)]
+        step = [sbuf(f"step{i}", [P, BANK], F32, tag=f"product{i}") for i in range(4)]
         for i in range(len(units)):
             if i >= 2:
                 second_pass(i, 0)

@@ -58,24 +58,18 @@ def tile_list_shelf_suggester_kernel(
         w4_plane = sbuf("w4_plane", [P, PASSES, N], U8)
         weights = sbuf("weights", [P, S], F32)
         page = [sbuf(f"page{b}", [P, T2], F32) for b in range(ROW_TILES)]
-        widths = list(W1_CHUNKS) + [W3_CHUNK] * (N // W3_CHUNK)
         first_tile = [sum(W1_CHUNKS[:c]) // P for c in range(len(W1_CHUNKS))]
         w1_raw = [
             [sbuf(f"raw{c}_0", [P, PACK, w], F32), sbuf(f"raw{c}_1", [P, PACK, w], F32, tag=f"slot{first_tile[c] - 1}")]
             for c, w in enumerate(W1_CHUNKS)
         ]
-        w3_first = [sbuf(f"w3_first{a}", [P, PACK, W3_CHUNK], F32) for a in range(PASSES)]
-        w3_rest = [sbuf(f"w3_rest{a}", [P, PACK, N - W3_CHUNK], F32) for a in range(PASSES)]
-        raw = [[t[:] for t in pair] for pair in w1_raw + [w3_first]] + [
-            [t[:, :, c * W3_CHUNK : (c + 1) * W3_CHUNK] for t in w3_rest] for c in range(N // W3_CHUNK - 1)
-        ]
-        old = [sbuf(f"old{c}", [P, W3_CHUNK // P, T2], F32) for c in range(N // W3_CHUNK)]
+        w3_early = [sbuf(f"w3_early{a}", [P, PACK, 2 * W3_CHUNK], F32) for a in range(PASSES)]
+        w3_late = [sbuf(f"w3_late{a}", [P, PACK, W3_CHUNK], F32) for a in range(PASSES)]
+        old = [sbuf(f"old{c}", [P, W3_CHUNK // P, T2], F32) for c in range(N // W3_CHUNK - 1)]
         ring = [sbuf(f"staged{i}", [P, PASSES * W3_CHUNK * PACK], BF16) for i in range(2)]
-        staged = {u: ring[i % 2] for i, u in enumerate((0, 1, 4, 2, 3, 5, 6))}
-        w1_codes, w3_codes = {}, {}
-        page_codes = [sbuf(f"page_codes{g}", [P, T2], U32) for g in range(PASSES)]
+        w1_codes, w3_codes, page_codes = {}, {}, {}
         w1_plane = [sbuf(f"w1_plane{c}", [P, PASSES * w], U8) for c, w in enumerate(W1_CHUNKS)]
-        w3_plane = [sbuf(f"w3_plane{c}", [P, PASSES * W3_CHUNK], U8) for c in range(N // W3_CHUNK)]
+        w3_plane = [sbuf(f"w3_plane{a}", [P, N], U8) for a in range(PASSES)]
         taste = {}
         product = [sbuf(f"product{i}", [P, S], F32) for i in range(ROW_TILES)]
         turned = [[sbuf(f"turned{g}_{h}", [P, PACK * K_PASS], BF16) for h in range(HALVES)] for g in range(PASSES)]
@@ -124,56 +118,69 @@ def tile_list_shelf_suggester_kernel(
         load_w1(0, (0,))
         load_w2(0)
         load_plane(table_scales, tab_scales)
-        load_w1(0, (1,))
         load_table_words(1)
         load_plane(w2_plane, w2_scales)
+        load_w1(0, (1,))
         nc.sync.dma_start(out=weights[:], in_=wgs)
         load_page(0)
+        load_w2(1)
         load_w1(1)
         load_page(1)
-        load_weight(w3_first, w3, 0)
-        load_page(2)
         load_w1(2)
-        load_page(3)
-        load_w2(1)
-        load_page(4)
+        load_page(2)
         load_w1(3)
-        load_weight(w3_rest, w3, W3_CHUNK)
+        load_page(3)
+        load_weight(w3_early, w3, 0, (0,))
+        load_page(4)
+        load_weight(w3_early, w3, 0, (1,))
         load_page(5)
+        load_old(0)
         load_page(6)
         nc.sync.dma_start(out=w4_codes[:].bitcast(I32), in_=w4_words.bitcast(I32).rearrange("a p n -> p a n"))
         load_plane(w4_plane, w4_scales)
-        load_old(0)
-        load_old(1)
+        load_weight(w3_late, w3, 2 * W3_CHUNK)
         load_page(7)
-        load_old(2)
+        load_old(1)
 
-        def stage_weight(unit, passes=range(PASSES)):
-            width = widths[unit]
-            stage = staged[unit]
-            for a in passes:
-                dst = stage[:, a * width * PACK : (a + 1) * width * PACK].rearrange("p (c i j) -> p c j i", i=4, j=PACK)
-                nc.scalar.copy(out=dst, in_=raw[unit][a].rearrange("p j (c i) -> p c j i", i=4))
+        def stage(dst, src):
+            nc.scalar.copy(
+                out=dst.rearrange("p (c i j) -> p c j i", i=4, j=PACK), in_=src.rearrange("p j (c i) -> p c j i", i=4)
+            )
 
-        def quantize_weight(unit, plane, tag):
-            words = plane.shape[1]
-            codes = sbuf(f"codes{unit}", [P, words], U32, tag=tag)
-            stage = staged[unit]
-            nc.vector.quantize_mx(out=codes[:].bitcast(FP8X4), scales=plane[:], in_=stage[:, : words * PACK])
-            return codes
+        def stage_w1(c):
+            width = W1_CHUNKS[c]
+            for a in range(PASSES):
+                stage(ring[c % 2][:, a * width * PACK : (a + 1) * width * PACK], w1_raw[c][a][:])
+
+        def quantize_w1(c, pieces):
+            words = PASSES * W1_CHUNKS[c]
+            w1_codes[c] = sbuf(f"w1_codes{c}", [P, words], U32)
+            for i in range(pieces):
+                cols = slice(i * words // pieces, (i + 1) * words // pieces)
+                nc.vector.quantize_mx(
+                    out=w1_codes[c][:, cols].bitcast(FP8X4), scales=w1_plane[c][:, cols],
+                    in_=ring[c % 2][:, cols.start * PACK : cols.stop * PACK],
+                )
+
+        def quantize_w3(a, first, count, staged, tag):
+            codes = sbuf(f"w3_codes{a}_{first}", [P, count * W3_CHUNK], U32, tag=tag)
+            cols = slice(first * W3_CHUNK, (first + count) * W3_CHUNK)
+            nc.vector.quantize_mx(out=codes[:].bitcast(FP8X4), scales=w3_plane[a][:, cols], in_=staged)
+            for c in range(count):
+                w3_codes[a, first + c] = codes[:, c * W3_CHUNK : (c + 1) * W3_CHUNK]
 
         def w1_place(b):
             c = max(i for i in range(len(W1_CHUNKS)) if sum(W1_CHUNKS[:i]) <= b * P)
             return c, b * P - sum(W1_CHUNKS[:c])
 
         def bank_pair(b):
-            first = 4 if b == ROW_TILES - 1 else 6 - 4 * (b % 2)
+            first = 2 - 2 * (b % 2)
             return banks[first : first + 2]
 
-        def recent_product(b):
+        def recent_product(b, passes=range(PASSES)):
             bank = banks[(0, 1, 4, 5)[b % 4]]
             g, col = divmod(b * P, K_PASS)
-            for a in range(PASSES):
+            for a in passes:
                 nc.tensor.matmul_mx(
                     out=bank[:],
                     lhsT=w2_codes[g][:, a, 2 * col : 2 * (col + P)].bitcast(FP4X4),
@@ -185,19 +192,17 @@ def tile_list_shelf_suggester_kernel(
         def taste_product(b):
             c, first = w1_place(b)
             taste[b] = sbuf(f"taste{b}", [P, S], F32, tag=f"slot{b}")
-            for h in range(2):
-                picks = slice(h * S // 2, (h + 1) * S // 2)
-                bank = bank_pair(b)[h]
-                for a in range(PASSES):
-                    w1_cols = slice(a * W1_CHUNKS[c] + first, a * W1_CHUNKS[c] + first + P)
-                    nc.tensor.matmul_mx(
-                        out=bank[:, : S // 2],
-                        lhsT=w1_codes[c][:, w1_cols].bitcast(FP8X4),
-                        lhsT_scale=w1_plane[c][:, w1_cols],
-                        rhs=picked_words[a][:, picks].bitcast(FP8X4), rhs_scale=picked_scales[a][:, picks],
-                        start=(a == 0), stop=(a == PASSES - 1),
-                    )
-                nc.scalar.copy(out=taste[b][:, picks], in_=bank[:, : S // 2])
+            bank = banks[6 + b % 2]
+            for a in range(PASSES):
+                w1_cols = slice(a * W1_CHUNKS[c] + first, a * W1_CHUNKS[c] + first + P)
+                nc.tensor.matmul_mx(
+                    out=bank[:],
+                    lhsT=w1_codes[c][:, w1_cols].bitcast(FP8X4),
+                    lhsT_scale=w1_plane[c][:, w1_cols],
+                    rhs=picked_words[a][:].bitcast(FP8X4), rhs_scale=picked_scales[a][:],
+                    start=(a == 0), stop=(a == PASSES - 1),
+                )
+            nc.scalar.copy(out=taste[b][:], in_=bank[:])
 
         def multiply(b):
             nc.vector.tensor_tensor(out=product[b % len(product)][:], in0=banks[(0, 1, 4, 5)[b % 4]][:], in1=weights[:], op=MULT)
@@ -209,7 +214,7 @@ def tile_list_shelf_suggester_kernel(
         def turn_page(b, engines):
             g, q = divmod(b, TILES_PER_PASS)
             for h in range(HALVES):
-                bank = bank_pair(b + 1)[h]
+                bank = bank_pair(b)[h]
                 for j in range(4):
                     col = h * BANK + j * P
                     nc.tensor.transpose(bank[:, j * P : (j + 1) * P], page[b][:, col : col + P], identity[:])
@@ -219,45 +224,45 @@ def tile_list_shelf_suggester_kernel(
         def regroup_page(g, h, engines):
             words = turned[g][h][:].bitcast(F32)
             for s in range(2):
-                bank = banks[4 + 2 * h + s] if g else banks[2 - 2 * h + s]
+                bank = banks[(2, 0)[h] + s] if g else banks[(4, 6)[h] + s]
                 for i in range(4):
                     col = (4 * s + i) * P
                     nc.tensor.transpose(bank[:, i * P : (i + 1) * P], words[:, col : col + P], identity[:])
                 dst = grouped[h][:].bitcast(F32)[:, s * BANK : (s + 1) * BANK].rearrange("p (j m u) -> p j m u", j=2, u=2)
                 engines[s](out=dst, in_=bank[:].rearrange("p (j u m) -> p j m u", j=2, u=2))
 
-        def quantize_page(g, h):
+        def quantize_page(g, h, tag=None):
             cols = slice(h * BANK, (h + 1) * BANK)
-            nc.vector.quantize_mx(out=page_codes[g][:, cols].bitcast(FP8X4), scales=page_plane[:, g, cols], in_=grouped[h][:])
-
-        def store_codes(g):
-            nc.sync.dma_start(out=out_2[g].rearrange("p m t -> p (m t)").bitcast(I32), in_=page_codes[g][:].bitcast(I32))
+            page_codes[g, h] = sbuf(f"page_codes{g}_{h}", [P, BANK], U32, tag=tag)
+            nc.vector.quantize_mx(out=page_codes[g, h][:].bitcast(FP8X4), scales=page_plane[:, g, cols], in_=grouped[h][:])
+            words = out_2[g].rearrange("p m t -> p (m t)").bitcast(I32)
+            nc.sync.dma_start(out=words[:, cols], in_=page_codes[g, h][:].bitcast(I32))
 
         units = [(n, h) for c in range(N // W3_CHUNK) for h in range(HALVES) for n in (2 * c, 2 * c + 1)]
 
         def gate_bank(i):
-            return banks[2 * i % 8]
+            return banks[(4, 6, 2)[i % 3]]
 
         def fresh_bank(i):
-            return banks[(2 * i + 1) % 8]
+            return banks[(5, 7, 3, 0, 1)[i % 5]]
 
-        def second_pass(i, g):
+        def gate_pass(i, g):
             n, h = units[i]
-            cols = slice(h * BANK, (h + 1) * BANK)
-            moving = page_codes[g][:, cols].bitcast(FP8X4)
-            w3_cols = slice(g * W3_CHUNK + n % 2 * P, g * W3_CHUNK + (n % 2 + 1) * P)
             nc.tensor.matmul_mx(
                 out=gate_bank(i)[:],
-                lhsT=w3_codes[n // 2][:, w3_cols].bitcast(FP8X4),
-                lhsT_scale=w3_plane[n // 2][:, w3_cols],
-                rhs=moving, rhs_scale=page_plane[:, g, cols],
+                lhsT=w3_codes[g, n // 2][:, n % 2 * P : (n % 2 + 1) * P].bitcast(FP8X4),
+                lhsT_scale=w3_plane[g][:, n * P : (n + 1) * P],
+                rhs=page_codes[g, h][:].bitcast(FP8X4), rhs_scale=page_plane[:, g, h * BANK : (h + 1) * BANK],
                 start=(g == 0), stop=(g == PASSES - 1),
             )
+
+        def fresh_pass(i, g):
+            n, h = units[i]
             nc.tensor.matmul_mx(
                 out=fresh_bank(i)[:],
                 lhsT=w4_codes[:, g, 2 * n * P : 2 * (n + 1) * P].bitcast(FP4X4),
                 lhsT_scale=w4_plane[:, g, n * P : (n + 1) * P],
-                rhs=moving, rhs_scale=page_plane[:, g, cols],
+                rhs=page_codes[g, h][:].bitcast(FP8X4), rhs_scale=page_plane[:, g, h * BANK : (h + 1) * BANK],
                 start=(g == 0), stop=(g == PASSES - 1),
             )
 
@@ -267,10 +272,10 @@ def tile_list_shelf_suggester_kernel(
 
         def blend_begin(i):
             slot = i % len(step)
-            nc.scalar.activation(out=rest[slot][:], in_=gate_bank(i)[:], func=SIGMOID, scale=-1.0)
+            nc.scalar.activation(out=rest[i % len(rest)][:], in_=gate_bank(i)[:], func=SIGMOID, scale=-1.0)
             nc.vector.tensor_tensor(out=step[slot][:], in0=fresh_bank(i)[:], in1=scores(i), op=SUB)
             engine = nc.vector if i in (0, len(units) - 1) else nc.gpsimd
-            engine.tensor_tensor(out=step[slot][:], in0=step[slot][:], in1=rest[slot][:], op=MULT)
+            engine.tensor_tensor(out=step[slot][:], in0=step[slot][:], in1=rest[i % len(rest)][:], op=MULT)
 
         def blend_end(i):
             n, h = units[i]
@@ -280,57 +285,65 @@ def tile_list_shelf_suggester_kernel(
         on_scalar = (nc.scalar.copy, nc.scalar.copy)
         shared = (nc.vector.tensor_copy, nc.scalar.copy)
 
-        n_w1 = len(W1_CHUNKS)
-        planes = w1_plane + w3_plane
-        stage_weight(0)
-        w1_codes[0] = quantize_weight(0, planes[0], None)
+        last = ROW_TILES - 1
+        piece = W3_CHUNK * PACK
+        nc.vector.tensor_copy(picked_words[0][:], table_words[0][:].bitcast(U32).indirect(pick_list[:]))
         for a in range(PASSES):
             nc.vector.tensor_copy(picked_scales[a][:], table_scales[:, a, :].indirect(pick_list[:]))
-            nc.vector.tensor_copy(picked_words[a][:], table_words[a][:].bitcast(U32).indirect(pick_list[:]))
-        last = ROW_TILES - 1
-        recent_product(0)
+        nc.vector.tensor_copy(picked_words[1][:], table_words[1][:].bitcast(U32).indirect(pick_list[:]))
+        old.append(sbuf("old2", [P, W3_CHUNK // P, T2], F32, tag="table_words0"))
+        load_old(2)
+        w3_staged = sbuf("w3_staged", [P, PASSES * 2 * piece], BF16, tag="table_words1")
+        stage_w1(0)
+        quantize_w1(0, PASSES)
         taste_product(0)
-        multiply(0)
-        stage_weight(1)
-        for b in range(ROW_TILES):
-            if b + 1 in first_tile:
-                c = first_tile.index(b + 1)
-                w1_codes[c] = quantize_weight(c, planes[c], None)
-            if b == 2:
-                w3_codes[0] = quantize_weight(n_w1, planes[n_w1], None)
+        for b in range(TILES_PER_PASS):
+            recent_product(b)
+            multiply(b)
+        stage_w1(1)
+        taste_product(1)
+        scatter(0)
+        for c in range(1, len(W1_CHUNKS)):
+            quantize_w1(c, 1)
+            taste_product(2 * c)
+            if c + 1 < len(W1_CHUNKS):
+                stage_w1(c + 1)
+            taste_product(2 * c + 1)
+            if c == 1:
+                for b in range(TILES_PER_PASS, ROW_TILES):
+                    recent_product(b)
+                    multiply(b)
+            scatter(c)
+            turn_page(c - 1, on_scalar)
+        turn_page(TILES_PER_PASS - 1, on_scalar)
+        for b in range(TILES_PER_PASS, ROW_TILES):
+            if b == last - 1:
+                quantize_w3(0, 0, 1, w3_staged[:, :piece], f"product{b - 1}")
             if b == last:
-                for h in range(HALVES):
-                    quantize_page(0, h)
-                store_codes(0)
+                quantize_page(0, 0, f"product{b - 1}")
             scatter(b)
-            if b in (0, 2):
-                for ahead in range(max(1, 2 * b), 2 * b + TILES_PER_PASS):
-                    recent_product(ahead)
-                    multiply(ahead)
-            if b == 1:
-                stage_weight(n_w1)
-            if b + 2 in first_tile[2:]:
-                stage_weight(first_tile.index(b + 2))
-            if b < last:
-                taste_product(b + 1)
-            if b == last - 2:
+            if b == TILES_PER_PASS:
                 for h in range(HALVES):
                     regroup_page(0, h, on_scalar)
-            if b >= last - 1:
-                stage_weight(n_w1 + 2 + b - last)
-            if b >= 1:
-                turn_page(b - 1, on_scalar)
-        second_pass(0, 0)
-        second_pass(1, 0)
+            if b < TILES_PER_PASS + PASSES:
+                a = b - TILES_PER_PASS
+                for c in range(2):
+                    cols = slice(c * W3_CHUNK, (c + 1) * W3_CHUNK)
+                    stage(w3_staged[:, (2 * a + c) * piece : (2 * a + c + 1) * piece], w3_early[a][:, :, cols])
+            if b < last:
+                turn_page(b, on_scalar)
+        for i in range(2):
+            gate_pass(i, 0)
+            fresh_pass(i, 0)
         turn_page(last, shared)
 
-        w3_codes[1] = quantize_weight(n_w1 + 1, planes[n_w1 + 1], f"slot{last}")
+        quantize_w3(1, 0, 2, w3_staged[:, 2 * piece :], f"slot{last}")
+        quantize_w3(0, 1, 1, w3_staged[:, piece : 2 * piece], f"product{last}")
+        quantize_page(0, 1, "table_words1")
         regroup_page(1, 0, shared)
         quantize_page(1, 0)
         regroup_page(1, 1, on_scalar)
         quantize_page(1, 1)
-        w3_codes[2] = quantize_weight(n_w1 + 2, planes[n_w1 + 2], "grouped0")
-        store_codes(1)
         scale_rows = out_3.bitcast(I32)
         for q in range(4):
             nc.sync.dma_start(
@@ -339,12 +352,20 @@ def tile_list_shelf_suggester_kernel(
             )
 
         rest = [sbuf(f"rest{i}", [P, BANK], F32, tag=f"raw{i}_0") for i in range(4)]
-        step = [sbuf(f"step{i}", [P, BANK], F32, tag=f"product{i}") for i in range(4)]
+        step = [sbuf(f"step{i}", [P, BANK], F32, tag=f"product{i}") for i in range(5)]
         for i in range(len(units)):
-            if i >= 2:
-                second_pass(i, 0)
-            second_pass(i, 1)
+            for one_pass in (fresh_pass, gate_pass):
+                for g in range(0 if i >= 2 else 1, PASSES):
+                    one_pass(i, g)
             blend_begin(i)
-            if i >= 1:
-                blend_end(i - 1)
+            if i == 0:
+                late_staged = sbuf("late_staged", [P, PASSES * piece], BF16, tag="grouped1")
+            if i in (0, 2):
+                stage(late_staged[:, i // 2 * piece : (i // 2 + 1) * piece], w3_late[i // 2][:])
+            if i in (3, 5):
+                a = (i - 3) // 2
+                quantize_w3(a, 2, 1, late_staged[:, a * piece : (a + 1) * piece], None)
+            if i >= 2:
+                blend_end(i - 2)
+        blend_end(len(units) - 2)
         blend_end(len(units) - 1)

@@ -60,7 +60,7 @@ def tile_list_shelf_suggester_kernel(
         page = [sbuf(f"page{b}", [P, T2], F32) for b in range(ROW_TILES)]
         first_tile = [sum(W1_CHUNKS[:c]) // P for c in range(len(W1_CHUNKS))]
         w1_raw = [
-            [sbuf(f"raw{c}_0", [P, PACK, w], F32), sbuf(f"raw{c}_1", [P, PACK, w], F32, tag=f"slot{first_tile[c] - 1}")]
+            [sbuf(f"raw{c}_0", [P, PACK, w], F32), sbuf(f"raw{c}_1", [P, PACK, w], F32, tag=f"slot{(-1, 1, -2, 3)[c]}")]
             for c, w in enumerate(W1_CHUNKS)
         ]
         w3_early = [sbuf(f"w3_early{a}", [P, PACK, 2 * W3_CHUNK], F32) for a in range(PASSES)]
@@ -69,17 +69,20 @@ def tile_list_shelf_suggester_kernel(
         ring = [sbuf(f"staged{i}", [P, PASSES * W3_CHUNK * PACK], BF16) for i in range(2)]
         w1_codes, w3_codes, page_codes = {}, {}, {}
         w1_plane = [sbuf(f"w1_plane{c}", [P, PASSES * w], U8) for c, w in enumerate(W1_CHUNKS)]
-        w3_plane = [sbuf(f"w3_plane{a}", [P, N], U8) for a in range(PASSES)]
+        w3_plane = [sbuf(f"w3_plane{c}", [P, PASSES * W3_CHUNK], U8) for c in range(N // W3_CHUNK)]
         taste = {}
         product = [sbuf(f"product{i}", [P, S], F32) for i in range(ROW_TILES)]
         turned = [[sbuf(f"turned{g}_{h}", [P, PACK * K_PASS], BF16) for h in range(HALVES)] for g in range(PASSES)]
-        grouped = [sbuf(f"grouped{h}", [P, BANK * PACK], BF16) for h in range(HALVES)]
+        grouped = {}
         page_plane = sbuf("page_plane", [P, PASSES, T2], U8)
 
         nc.vector.memset(table_scales[:].bitcast(I32), 0)
         nc.vector.memset(w2_plane[:].bitcast(I32), 0)
         nc.gpsimd.memset(w4_plane[:].bitcast(I32), 0)
         make_identity(nc, identity[:])
+
+        warm = sbuf("warm", [P, 1], F32)
+        nc.scalar.activation(out=warm[:], in_=identity[:, 0:1], func=SIGMOID)
 
         def load_plane(plane, scales):
             rows = scales.bitcast(I32)
@@ -99,7 +102,11 @@ def tile_list_shelf_suggester_kernel(
             load_weight(w1_raw[c], w1, sum(W1_CHUNKS[:c]), passes)
 
         def load_table_words(a):
-            nc.sync.dma_start(out=table_words[a][:], in_=tab_words[a].rearrange("p t i -> p (t i)").bitcast(I32))
+            words = tab_words[a].rearrange("p t i -> p (t i)").bitcast(I32)
+            pieces = 1 if a else 4
+            for i in range(pieces):
+                cols = slice(i * T // pieces, (i + 1) * T // pieces)
+                nc.sync.dma_start(out=table_words[a][:, cols], in_=words[:, cols])
 
         def load_w2(g):
             words = w2_words.bitcast(I32)[:, :, g * K_PASS // 2 : (g + 1) * K_PASS // 2]
@@ -113,22 +120,23 @@ def tile_list_shelf_suggester_kernel(
             nc.sync.dma_start(out=old[c][:], in_=rows.rearrange("(i p) m -> p i m", p=P))
 
         nc.sync.dma_start(pick_list[:], offs)
-        nc.sync.dma_start(put_list[:], offs2)
         load_table_words(0)
-        load_w1(0, (0,))
-        load_w2(0)
         load_plane(table_scales, tab_scales)
-        load_table_words(1)
+        load_w2(0)
         load_plane(w2_plane, w2_scales)
-        load_w1(0, (1,))
+        load_table_words(1)
         nc.sync.dma_start(out=weights[:], in_=wgs)
-        load_page(0)
+        load_w1(0, (0,))
         load_w2(1)
+        load_w1(0, (1,))
+        nc.sync.dma_start(put_list[:], offs2)
+        load_page(0)
         load_w1(1)
+        load_w1(2, (0,))
         load_page(1)
-        load_w1(2)
-        load_page(2)
+        load_w1(2, (1,))
         load_w1(3)
+        load_page(2)
         load_page(3)
         load_weight(w3_early, w3, 0, (0,))
         load_page(4)
@@ -142,8 +150,8 @@ def tile_list_shelf_suggester_kernel(
         load_page(7)
         load_old(1)
 
-        def stage(dst, src):
-            nc.scalar.copy(
+        def stage(dst, src, copy=nc.scalar.copy):
+            copy(
                 out=dst.rearrange("p (c i j) -> p c j i", i=4, j=PACK), in_=src.rearrange("p j (c i) -> p c j i", i=4)
             )
 
@@ -162,12 +170,12 @@ def tile_list_shelf_suggester_kernel(
                     in_=ring[c % 2][:, cols.start * PACK : cols.stop * PACK],
                 )
 
-        def quantize_w3(a, first, count, staged, tag):
-            codes = sbuf(f"w3_codes{a}_{first}", [P, count * W3_CHUNK], U32, tag=tag)
-            cols = slice(first * W3_CHUNK, (first + count) * W3_CHUNK)
-            nc.vector.quantize_mx(out=codes[:].bitcast(FP8X4), scales=w3_plane[a][:, cols], in_=staged)
-            for c in range(count):
-                w3_codes[a, first + c] = codes[:, c * W3_CHUNK : (c + 1) * W3_CHUNK]
+        def quantize_w3(c, staged, tag):
+            w3_codes[c] = sbuf(f"w3_codes{c}", [P, PASSES * W3_CHUNK], U32, tag=tag)
+            words = PASSES * W3_CHUNK // len(staged)
+            for i, part in enumerate(staged):
+                cols = slice(i * words, (i + 1) * words)
+                nc.vector.quantize_mx(out=w3_codes[c][:, cols].bitcast(FP8X4), scales=w3_plane[c][:, cols], in_=part[:])
 
         def w1_place(b):
             c = max(i for i in range(len(W1_CHUNKS)) if sum(W1_CHUNKS[:i]) <= b * P)
@@ -191,8 +199,8 @@ def tile_list_shelf_suggester_kernel(
 
         def taste_product(b):
             c, first = w1_place(b)
-            taste[b] = sbuf(f"taste{b}", [P, S], F32, tag=f"slot{b}")
-            bank = banks[6 + b % 2]
+            taste[b] = sbuf(f"taste{b}", [P, S], F32, tag="raw3_0" if b == 4 else f"slot{b}")
+            bank = banks[(6, 7, 2, 3, 0, 1, 6, 7)[b]]
             for a in range(PASSES):
                 w1_cols = slice(a * W1_CHUNKS[c] + first, a * W1_CHUNKS[c] + first + P)
                 nc.tensor.matmul_mx(
@@ -202,9 +210,15 @@ def tile_list_shelf_suggester_kernel(
                     rhs=picked_words[a][:].bitcast(FP8X4), rhs_scale=picked_scales[a][:],
                     start=(a == 0), stop=(a == PASSES - 1),
                 )
-            nc.scalar.copy(out=taste[b][:], in_=bank[:])
+            if b == 0:
+                nc.vector.tensor_tensor(out=taste[b][:], in0=bank[:], in1=weights[:], op=MULT)
+            else:
+                nc.scalar.copy(out=taste[b][:], in_=bank[:])
 
         def multiply(b):
+            if b == 0:
+                nc.scalar.copy(out=product[b][:], in_=banks[0][:])
+                return
             nc.vector.tensor_tensor(out=product[b % len(product)][:], in0=banks[(0, 1, 4, 5)[b % 4]][:], in1=weights[:], op=MULT)
 
         def scatter(b):
@@ -223,35 +237,37 @@ def tile_list_shelf_suggester_kernel(
 
         def regroup_page(g, h, engines):
             words = turned[g][h][:].bitcast(F32)
+            grouped[g, h] = sbuf(f"grouped{g}_{h}", [P, BANK * PACK], BF16, tag=(("slot-1", "slot1"), ("slot2", "slot3"))[g][h])
             for s in range(2):
-                bank = banks[(2, 0)[h] + s] if g else banks[(4, 6)[h] + s]
+                bank = banks[4 + 2 * h + s]
                 for i in range(4):
                     col = (4 * s + i) * P
                     nc.tensor.transpose(bank[:, i * P : (i + 1) * P], words[:, col : col + P], identity[:])
-                dst = grouped[h][:].bitcast(F32)[:, s * BANK : (s + 1) * BANK].rearrange("p (j m u) -> p j m u", j=2, u=2)
+                dst = grouped[g, h][:].bitcast(F32)[:, s * BANK : (s + 1) * BANK].rearrange("p (j m u) -> p j m u", j=2, u=2)
                 engines[s](out=dst, in_=bank[:].rearrange("p (j u m) -> p j m u", j=2, u=2))
 
         def quantize_page(g, h, tag=None):
             cols = slice(h * BANK, (h + 1) * BANK)
             page_codes[g, h] = sbuf(f"page_codes{g}_{h}", [P, BANK], U32, tag=tag)
-            nc.vector.quantize_mx(out=page_codes[g, h][:].bitcast(FP8X4), scales=page_plane[:, g, cols], in_=grouped[h][:])
+            nc.vector.quantize_mx(out=page_codes[g, h][:].bitcast(FP8X4), scales=page_plane[:, g, cols], in_=grouped[g, h][:])
             words = out_2[g].rearrange("p m t -> p (m t)").bitcast(I32)
             nc.sync.dma_start(out=words[:, cols], in_=page_codes[g, h][:].bitcast(I32))
 
         units = [(n, h) for c in range(N // W3_CHUNK) for h in range(HALVES) for n in (2 * c, 2 * c + 1)]
 
         def gate_bank(i):
-            return banks[(4, 6, 2)[i % 3]]
+            return banks[(2, 0, 4)[i % 3]]
 
         def fresh_bank(i):
-            return banks[(5, 7, 3, 0, 1)[i % 5]]
+            return banks[(3, 1, 5, 6, 7)[i % 5]]
 
         def gate_pass(i, g):
             n, h = units[i]
+            w3_cols = slice(g * W3_CHUNK + n % 2 * P, g * W3_CHUNK + (n % 2 + 1) * P)
             nc.tensor.matmul_mx(
                 out=gate_bank(i)[:],
-                lhsT=w3_codes[g, n // 2][:, n % 2 * P : (n % 2 + 1) * P].bitcast(FP8X4),
-                lhsT_scale=w3_plane[g][:, n * P : (n + 1) * P],
+                lhsT=w3_codes[n // 2][:, w3_cols].bitcast(FP8X4),
+                lhsT_scale=w3_plane[n // 2][:, w3_cols],
                 rhs=page_codes[g, h][:].bitcast(FP8X4), rhs_scale=page_plane[:, g, h * BANK : (h + 1) * BANK],
                 start=(g == 0), stop=(g == PASSES - 1),
             )
@@ -293,7 +309,7 @@ def tile_list_shelf_suggester_kernel(
         nc.vector.tensor_copy(picked_words[1][:], table_words[1][:].bitcast(U32).indirect(pick_list[:]))
         old.append(sbuf("old2", [P, W3_CHUNK // P, T2], F32, tag="table_words0"))
         load_old(2)
-        w3_staged = sbuf("w3_staged", [P, PASSES * 2 * piece], BF16, tag="table_words1")
+        w3_staged = sbuf("w3_staged", [P, PASSES * piece], BF16, tag="table_words1")
         stage_w1(0)
         quantize_w1(0, PASSES)
         taste_product(0)
@@ -303,47 +319,46 @@ def tile_list_shelf_suggester_kernel(
         stage_w1(1)
         taste_product(1)
         scatter(0)
-        for c in range(1, len(W1_CHUNKS)):
-            quantize_w1(c, 1)
-            taste_product(2 * c)
-            if c + 1 < len(W1_CHUNKS):
-                stage_w1(c + 1)
-            taste_product(2 * c + 1)
-            if c == 1:
-                for b in range(TILES_PER_PASS, ROW_TILES):
-                    recent_product(b)
-                    multiply(b)
-            scatter(c)
-            turn_page(c - 1, on_scalar)
-        turn_page(TILES_PER_PASS - 1, on_scalar)
         for b in range(TILES_PER_PASS, ROW_TILES):
-            if b == last - 1:
-                quantize_w3(0, 0, 1, w3_staged[:, :piece], f"product{b - 1}")
-            if b == last:
-                quantize_page(0, 0, f"product{b - 1}")
+            recent_product(b)
+            multiply(b)
+        tastes = {1: (2,), 2: (3, 4, 5), 3: (6, 7)}
+        for b in range(1, ROW_TILES):
+            if b < len(W1_CHUNKS):
+                quantize_w1(b, 1)
+                if b + 1 < len(W1_CHUNKS):
+                    stage_w1(b + 1)
+                for ahead in tastes[b]:
+                    taste_product(ahead)
             scatter(b)
-            if b == TILES_PER_PASS:
+            if b == TILES_PER_PASS + 1:
                 for h in range(HALVES):
                     regroup_page(0, h, on_scalar)
-            if b < TILES_PER_PASS + PASSES:
+            if b in (TILES_PER_PASS, TILES_PER_PASS + 1):
                 a = b - TILES_PER_PASS
-                for c in range(2):
-                    cols = slice(c * W3_CHUNK, (c + 1) * W3_CHUNK)
-                    stage(w3_staged[:, (2 * a + c) * piece : (2 * a + c + 1) * piece], w3_early[a][:, :, cols])
-            if b < last:
-                turn_page(b, on_scalar)
-        for i in range(2):
-            gate_pass(i, 0)
-            fresh_pass(i, 0)
-        turn_page(last, shared)
-
-        quantize_w3(1, 0, 2, w3_staged[:, 2 * piece :], f"slot{last}")
-        quantize_w3(0, 1, 1, w3_staged[:, piece : 2 * piece], f"product{last}")
+                stage(w3_staged[:, a * piece : (a + 1) * piece], w3_early[a][:, :, :W3_CHUNK])
+            for done in {1: (), 2: (0, 1)}.get(b, (b - 1,)):
+                turn_page(done, on_scalar)
+        mid_staged = [sbuf("mid_staged0", [P, piece], BF16, tag=f"slot{last - 1}")]
+        stage(mid_staged[0][:], w3_early[0][:, :, W3_CHUNK:])
+        for repeat in range(3):
+            nc.tensor.matmul_mx(
+                out=bank_pair(last)[1][:], lhsT=w1_codes[0][:, :P].bitcast(FP8X4), lhsT_scale=w1_plane[0][:, :P],
+                rhs=picked_words[0][:].bitcast(FP8X4), rhs_scale=picked_scales[0][:], start=True, stop=True,
+            )
+        quantize_w3(0, [w3_staged], f"slot{last}")
+        quantize_page(0, 0, f"product{last}")
+        turn_page(last, on_scalar)
+        gate_pass(0, 0)
+        fresh_pass(0, 0)
         quantize_page(0, 1, "table_words1")
         regroup_page(1, 0, shared)
         quantize_page(1, 0)
         regroup_page(1, 1, on_scalar)
         quantize_page(1, 1)
+        mid_staged.append(sbuf("mid_staged1", [P, piece], BF16, tag="slot-1"))
+        stage(mid_staged[1][:], w3_early[1][:, :, W3_CHUNK:], nc.vector.tensor_copy)
+        quantize_w3(1, mid_staged, None)
         scale_rows = out_3.bitcast(I32)
         for q in range(4):
             nc.sync.dma_start(
@@ -355,16 +370,15 @@ def tile_list_shelf_suggester_kernel(
         step = [sbuf(f"step{i}", [P, BANK], F32, tag=f"product{i}") for i in range(5)]
         for i in range(len(units)):
             for one_pass in (fresh_pass, gate_pass):
-                for g in range(0 if i >= 2 else 1, PASSES):
+                for g in range(1 if i == 0 else 0, PASSES):
                     one_pass(i, g)
             blend_begin(i)
             if i == 0:
-                late_staged = sbuf("late_staged", [P, PASSES * piece], BF16, tag="grouped1")
-            if i in (0, 2):
-                stage(late_staged[:, i // 2 * piece : (i // 2 + 1) * piece], w3_late[i // 2][:])
-            if i in (3, 5):
-                a = (i - 3) // 2
-                quantize_w3(a, 2, 1, late_staged[:, a * piece : (a + 1) * piece], None)
+                late_staged = sbuf("late_staged", [P, PASSES * piece], BF16, tag="slot2")
+            if i in (2, 3):
+                stage(late_staged[:, (i - 2) * piece : (i - 1) * piece], w3_late[i - 2][:])
+            if i == 4:
+                quantize_w3(2, [late_staged], None)
             if i >= 2:
                 blend_end(i - 2)
         blend_end(len(units) - 2)

@@ -358,7 +358,7 @@ def tile_list_shelf_suggester_kernel(
         quantize_page(1, 1)
         mid_staged.append(sbuf("mid_staged1", [P, piece], BF16, tag="slot-1"))
         stage(mid_staged[1][:], w3_early[1][:, :, W3_CHUNK:], nc.vector.tensor_copy)
-        quantize_w3(1, mid_staged, None)
+        quantize_w3(1, mid_staged, "slot1")
         scale_rows = out_3.bitcast(I32)
         for q in range(4):
             nc.sync.dma_start(

@@ -63,8 +63,7 @@ def tile_list_shelf_suggester_kernel(
             [sbuf(f"raw{c}_0", [P, PACK, w], F32), sbuf(f"raw{c}_1", [P, PACK, w], F32, tag=f"slot{(-1, 1, -2, 3)[c]}")]
             for c, w in enumerate(W1_CHUNKS)
         ]
-        w3_early = [sbuf(f"w3_early{a}", [P, PACK, 2 * W3_CHUNK], F32) for a in range(PASSES)]
-        w3_late = [sbuf(f"w3_late{a}", [P, PACK, W3_CHUNK], F32) for a in range(PASSES)]
+        w3_early = [sbuf(f"w3_early{a}", [P, PACK, N], F32) for a in range(PASSES)]
         old = [sbuf(f"old{c}", [P, W3_CHUNK // P, T2], F32) for c in range(N // W3_CHUNK - 1)]
         ring = [sbuf(f"staged{i}", [P, PASSES * W3_CHUNK * PACK], BF16) for i in range(2)]
         w1_codes, w3_codes, page_codes = {}, {}, {}
@@ -138,16 +137,15 @@ def tile_list_shelf_suggester_kernel(
         load_w1(3)
         load_page(2)
         load_page(3)
-        load_weight(w3_early, w3, 0, (0,))
         load_page(4)
-        load_weight(w3_early, w3, 0, (1,))
+        load_weight(w3_early, w3, 0, (0,))
         load_page(5)
-        load_old(0)
+        load_weight(w3_early, w3, 0, (1,))
         load_page(6)
+        load_page(7)
         nc.sync.dma_start(out=w4_codes[:].bitcast(I32), in_=w4_words.bitcast(I32).rearrange("a p n -> p a n"))
         load_plane(w4_plane, w4_scales)
-        load_weight(w3_late, w3, 2 * W3_CHUNK)
-        load_page(7)
+        load_old(0)
         load_old(1)
 
         def stage(dst, src, copy=nc.scalar.copy):
@@ -290,7 +288,7 @@ def tile_list_shelf_suggester_kernel(
             slot = i % len(step)
             nc.scalar.activation(out=rest[i % len(rest)][:], in_=gate_bank(i)[:], func=SIGMOID, scale=-1.0)
             nc.vector.tensor_tensor(out=step[slot][:], in0=fresh_bank(i)[:], in1=scores(i), op=SUB)
-            engine = nc.vector if i in (0, len(units) - 1) else nc.gpsimd
+            engine = nc.vector if i in (1, len(units) - 1) else nc.gpsimd
             engine.tensor_tensor(out=step[slot][:], in0=step[slot][:], in1=rest[i % len(rest)][:], op=MULT)
 
         def blend_end(i):
@@ -340,10 +338,10 @@ def tile_list_shelf_suggester_kernel(
             for done in {1: (), 2: (0, 1)}.get(b, (b - 1,)):
                 turn_page(done, on_scalar)
         mid_staged = [sbuf("mid_staged0", [P, piece], BF16, tag=f"slot{last - 1}")]
-        stage(mid_staged[0][:], w3_early[0][:, :, W3_CHUNK:])
+        stage(mid_staged[0][:], w3_early[0][:, :, W3_CHUNK : 2 * W3_CHUNK])
         for repeat in range(3):
             nc.tensor.matmul_mx(
-                out=bank_pair(last)[1][:], lhsT=w1_codes[0][:, :P].bitcast(FP8X4), lhsT_scale=w1_plane[0][:, :P],
+                out=bank_pair(last)[0][:], lhsT=w1_codes[0][:, :P].bitcast(FP8X4), lhsT_scale=w1_plane[0][:, :P],
                 rhs=picked_words[0][:].bitcast(FP8X4), rhs_scale=picked_scales[0][:], start=True, stop=True,
             )
         quantize_w3(0, [w3_staged], f"slot{last}")
@@ -357,8 +355,12 @@ def tile_list_shelf_suggester_kernel(
         regroup_page(1, 1, on_scalar)
         quantize_page(1, 1)
         mid_staged.append(sbuf("mid_staged1", [P, piece], BF16, tag="slot-1"))
-        stage(mid_staged[1][:], w3_early[1][:, :, W3_CHUNK:], nc.vector.tensor_copy)
+        stage(mid_staged[1][:], w3_early[1][:, :, W3_CHUNK : 2 * W3_CHUNK], nc.vector.tensor_copy)
         quantize_w3(1, mid_staged, "slot1")
+        late_staged = sbuf("late_staged", [P, PASSES * piece], BF16)
+        for a in range(PASSES):
+            stage(late_staged[:, a * piece : (a + 1) * piece], w3_early[a][:, :, 2 * W3_CHUNK :])
+        quantize_w3(2, [late_staged], "slot2")
         scale_rows = out_3.bitcast(I32)
         for q in range(4):
             nc.sync.dma_start(
@@ -373,12 +375,6 @@ def tile_list_shelf_suggester_kernel(
                 for g in range(1 if i == 0 else 0, PASSES):
                     one_pass(i, g)
             blend_begin(i)
-            if i == 0:
-                late_staged = sbuf("late_staged", [P, PASSES * piece], BF16, tag="slot2")
-            if i in (2, 3):
-                stage(late_staged[:, (i - 2) * piece : (i - 1) * piece], w3_late[i - 2][:])
-            if i == 4:
-                quantize_w3(2, [late_staged], None)
             if i >= 2:
                 blend_end(i - 2)
         blend_end(len(units) - 2)

@@ -26,9 +26,14 @@ BANK = 512
 ROW_TILES = H // P
 TILES_PER_PASS = K_PASS // P
 HALVES = T2 // BANK
-OUT_TILES = N // P
-W1_CHUNKS = (256, 256, 256, 256)
-W3_CHUNK = 256
+CHUNK = 256
+W1_CHUNKS = H // CHUNK
+W3_CHUNKS = N // CHUNK
+CHUNK_VALUES = CHUNK * PACK
+FIRST_TABLE_LOADS = 4
+RESTS = 4
+STEPS = 5
+END_LAG = 2
 
 
 def tile_list_shelf_suggester_kernel(
@@ -58,22 +63,20 @@ def tile_list_shelf_suggester_kernel(
         w4_plane = sbuf("w4_plane", [P, PASSES, N], U8)
         weights = sbuf("weights", [P, S], F32)
         page = [sbuf(f"page{b}", [P, T2], F32) for b in range(ROW_TILES)]
-        first_tile = [sum(W1_CHUNKS[:c]) // P for c in range(len(W1_CHUNKS))]
-        w1_raw = [
-            [sbuf(f"raw{c}_0", [P, PACK, w], F32), sbuf(f"raw{c}_1", [P, PACK, w], F32, tag=f"slot{(-1, 1, -2, 3)[c]}")]
-            for c, w in enumerate(W1_CHUNKS)
-        ]
-        w3_early = [sbuf(f"w3_early{a}", [P, PACK, N], F32) for a in range(PASSES)]
-        old = [sbuf(f"old{c}", [P, W3_CHUNK // P, T2], F32) for c in range(N // W3_CHUNK - 1)]
-        ring = [sbuf(f"staged{i}", [P, PASSES * W3_CHUNK * PACK], BF16) for i in range(2)]
-        w1_codes, w3_codes, page_codes = {}, {}, {}
-        w1_plane = [sbuf(f"w1_plane{c}", [P, PASSES * w], U8) for c, w in enumerate(W1_CHUNKS)]
-        w3_plane = [sbuf(f"w3_plane{c}", [P, PASSES * W3_CHUNK], U8) for c in range(N // W3_CHUNK)]
-        taste = {}
-        product = [sbuf(f"product{i}", [P, S], F32) for i in range(ROW_TILES)]
+        w1_raw = [[sbuf(f"w1_raw{c}_{a}", [P, PACK, CHUNK], F32) for a in range(PASSES)] for c in range(W1_CHUNKS)]
+        w3_raw = [sbuf(f"w3_raw{a}", [P, PACK, N], F32) for a in range(PASSES)]
+        old = [sbuf(f"old{c}", [P, CHUNK // P, T2], F32) for c in range(W3_CHUNKS - 1)]
+        w1_staged = [sbuf(f"w1_staged{i}", [P, PASSES * CHUNK_VALUES], BF16) for i in range(2)]
+        w1_plane = [sbuf(f"w1_plane{c}", [P, PASSES * CHUNK], U8) for c in range(W1_CHUNKS)]
+        w3_plane = [sbuf(f"w3_plane{c}", [P, PASSES * CHUNK], U8) for c in range(W3_CHUNKS)]
+        recent = [sbuf(f"recent{b}", [P, S], F32) for b in range(ROW_TILES)]
         turned = [[sbuf(f"turned{g}_{h}", [P, PACK * K_PASS], BF16) for h in range(HALVES)] for g in range(PASSES)]
-        grouped = {}
         page_plane = sbuf("page_plane", [P, PASSES, T2], U8)
+        w1_codes, w3_codes, page_codes, taste, grouped = {}, {}, {}, {}, {}
+
+        taste_tag = {b: f"taste{b}" for b in range(ROW_TILES)}
+        taste_tag.update({1: "w1_raw1_1", 3: "w1_raw3_1", 4: "w1_raw3_0"})
+        grouped_tag = {(0, 0): "w1_raw0_1", (0, 1): taste_tag[1], (1, 0): taste_tag[2], (1, 1): taste_tag[3]}
 
         nc.vector.memset(table_scales[:].bitcast(I32), 0)
         nc.vector.memset(w2_plane[:].bitcast(I32), 0)
@@ -91,20 +94,20 @@ def tile_list_shelf_suggester_kernel(
                     in_=rows[:, 4 * q : 4 * q + 4, :].rearrange("a r n -> r a n"),
                 )
 
-        def load_weight(pair, w, first, passes=range(PASSES)):
-            for a in passes:
-                width = pair[a].shape[2]
-                rows = w[a * K_PASS : (a + 1) * K_PASS, first : first + width]
-                nc.sync.dma_start(out=pair[a][:], in_=rows.rearrange("(p j) c -> p j c", j=PACK))
+        def load_pass(tile, w, a, first):
+            rows = w[a * K_PASS : (a + 1) * K_PASS, first : first + tile.shape[2]]
+            nc.sync.dma_start(out=tile[:], in_=rows.rearrange("(p j) c -> p j c", j=PACK))
 
-        def load_w1(c, passes=range(PASSES)):
-            load_weight(w1_raw[c], w1, sum(W1_CHUNKS[:c]), passes)
+        def load_w1(c, a):
+            load_pass(w1_raw[c][a], w1, a, c * CHUNK)
 
-        def load_table_words(a):
+        def load_w3(a):
+            load_pass(w3_raw[a], w3, a, 0)
+
+        def load_table_words(a, loads):
             words = tab_words[a].rearrange("p t i -> p (t i)").bitcast(I32)
-            pieces = 1 if a else 4
-            for i in range(pieces):
-                cols = slice(i * T // pieces, (i + 1) * T // pieces)
+            for i in range(loads):
+                cols = slice(i * T // loads, (i + 1) * T // loads)
                 nc.sync.dma_start(out=table_words[a][:, cols], in_=words[:, cols])
 
         def load_w2(g):
@@ -115,32 +118,34 @@ def tile_list_shelf_suggester_kernel(
             nc.sync.dma_start(out=page[b][:], in_=page0[b * P : (b + 1) * P, :])
 
         def load_old(c):
-            rows = prev[c * W3_CHUNK : (c + 1) * W3_CHUNK, :]
+            rows = prev[c * CHUNK : (c + 1) * CHUNK, :]
             nc.sync.dma_start(out=old[c][:], in_=rows.rearrange("(i p) m -> p i m", p=P))
 
         nc.sync.dma_start(pick_list[:], offs)
-        load_table_words(0)
+        load_table_words(0, FIRST_TABLE_LOADS)
         load_plane(table_scales, tab_scales)
         load_w2(0)
         load_plane(w2_plane, w2_scales)
-        load_table_words(1)
+        load_table_words(1, 1)
         nc.sync.dma_start(out=weights[:], in_=wgs)
-        load_w1(0, (0,))
+        load_w1(0, 0)
         load_w2(1)
-        load_w1(0, (1,))
+        load_w1(0, 1)
         nc.sync.dma_start(put_list[:], offs2)
         load_page(0)
-        load_w1(1)
-        load_w1(2, (0,))
+        load_w1(1, 0)
+        load_w1(1, 1)
+        load_w1(2, 0)
         load_page(1)
-        load_w1(2, (1,))
-        load_w1(3)
+        load_w1(2, 1)
+        load_w1(3, 0)
+        load_w1(3, 1)
         load_page(2)
         load_page(3)
         load_page(4)
-        load_weight(w3_early, w3, 0, (0,))
+        load_w3(0)
         load_page(5)
-        load_weight(w3_early, w3, 0, (1,))
+        load_w3(1)
         load_page(6)
         load_page(7)
         nc.sync.dma_start(out=w4_codes[:].bitcast(I32), in_=w4_words.bitcast(I32).rearrange("a p n -> p a n"))
@@ -148,45 +153,44 @@ def tile_list_shelf_suggester_kernel(
         load_old(0)
         load_old(1)
 
-        def stage(dst, src, copy=nc.scalar.copy):
-            copy(
-                out=dst.rearrange("p (c i j) -> p c j i", i=4, j=PACK), in_=src.rearrange("p j (c i) -> p c j i", i=4)
-            )
+        def stage(dst, src, copy):
+            copy(out=dst.rearrange("p (c i j) -> p c j i", i=4, j=PACK), in_=src.rearrange("p j (c i) -> p c j i", i=4))
+
+        def pass_part(staged, a):
+            return staged[:, a * CHUNK_VALUES : (a + 1) * CHUNK_VALUES]
 
         def stage_w1(c):
-            width = W1_CHUNKS[c]
             for a in range(PASSES):
-                stage(ring[c % 2][:, a * width * PACK : (a + 1) * width * PACK], w1_raw[c][a][:])
+                stage(pass_part(w1_staged[c % 2], a), w1_raw[c][a][:], nc.scalar.copy)
 
-        def quantize_w1(c, pieces):
-            words = PASSES * W1_CHUNKS[c]
-            w1_codes[c] = sbuf(f"w1_codes{c}", [P, words], U32)
-            for i in range(pieces):
-                cols = slice(i * words // pieces, (i + 1) * words // pieces)
-                nc.vector.quantize_mx(
-                    out=w1_codes[c][:, cols].bitcast(FP8X4), scales=w1_plane[c][:, cols],
-                    in_=ring[c % 2][:, cols.start * PACK : cols.stop * PACK],
-                )
+        def stage_w3(dst, c, a, copy):
+            stage(dst, w3_raw[a][:, :, c * CHUNK : (c + 1) * CHUNK], copy)
 
-        def quantize_w3(c, staged, tag):
-            w3_codes[c] = sbuf(f"w3_codes{c}", [P, PASSES * W3_CHUNK], U32, tag=tag)
-            words = PASSES * W3_CHUNK // len(staged)
-            for i, part in enumerate(staged):
+        def quantize_chunk(codes, plane, parts):
+            words = PASSES * CHUNK // len(parts)
+            for i, part in enumerate(parts):
                 cols = slice(i * words, (i + 1) * words)
-                nc.vector.quantize_mx(out=w3_codes[c][:, cols].bitcast(FP8X4), scales=w3_plane[c][:, cols], in_=part[:])
+                nc.vector.quantize_mx(out=codes[:, cols].bitcast(FP8X4), scales=plane[:, cols], in_=part)
 
-        def w1_place(b):
-            c = max(i for i in range(len(W1_CHUNKS)) if sum(W1_CHUNKS[:i]) <= b * P)
-            return c, b * P - sum(W1_CHUNKS[:c])
+        def quantize_w1(c, parts):
+            w1_codes[c] = sbuf(f"w1_codes{c}", [P, PASSES * CHUNK], U32)
+            quantize_chunk(w1_codes[c], w1_plane[c], parts)
 
-        def bank_pair(b):
-            first = 2 - 2 * (b % 2)
-            return banks[first : first + 2]
+        def quantize_w3(c, parts, tag):
+            w3_codes[c] = sbuf(f"w3_codes{c}", [P, PASSES * CHUNK], U32, tag=tag)
+            quantize_chunk(w3_codes[c], w3_plane[c], parts)
 
-        def recent_product(b, passes=range(PASSES)):
+        def chunk_columns(tile, a):
+            first = a * CHUNK + tile % 2 * P
+            return slice(first, first + P)
+
+        def weigh(dst, bank):
+            nc.vector.tensor_tensor(out=dst[:], in0=bank[:], in1=weights[:], op=MULT)
+
+        def recent_product(b):
             bank = banks[(0, 1, 4, 5)[b % 4]]
             g, col = divmod(b * P, K_PASS)
-            for a in passes:
+            for a in range(PASSES):
                 nc.tensor.matmul_mx(
                     out=bank[:],
                     lhsT=w2_codes[g][:, a, 2 * col : 2 * (col + P)].bitcast(FP4X4),
@@ -194,55 +198,55 @@ def tile_list_shelf_suggester_kernel(
                     rhs=picked_words[a][:].bitcast(FP8X4), rhs_scale=picked_scales[a][:],
                     start=(a == 0), stop=(a == PASSES - 1),
                 )
+            if b == 0:
+                nc.scalar.copy(out=recent[b][:], in_=bank[:])
+            else:
+                weigh(recent[b], bank)
 
         def taste_product(b):
-            c, first = w1_place(b)
-            taste[b] = sbuf(f"taste{b}", [P, S], F32, tag="raw3_0" if b == 4 else f"slot{b}")
+            taste[b] = sbuf(f"taste{b}", [P, S], F32, tag=taste_tag[b])
             bank = banks[(6, 7, 2, 3, 0, 1, 6, 7)[b]]
             for a in range(PASSES):
-                w1_cols = slice(a * W1_CHUNKS[c] + first, a * W1_CHUNKS[c] + first + P)
+                cols = chunk_columns(b, a)
                 nc.tensor.matmul_mx(
                     out=bank[:],
-                    lhsT=w1_codes[c][:, w1_cols].bitcast(FP8X4),
-                    lhsT_scale=w1_plane[c][:, w1_cols],
+                    lhsT=w1_codes[b // 2][:, cols].bitcast(FP8X4), lhsT_scale=w1_plane[b // 2][:, cols],
                     rhs=picked_words[a][:].bitcast(FP8X4), rhs_scale=picked_scales[a][:],
                     start=(a == 0), stop=(a == PASSES - 1),
                 )
             if b == 0:
-                nc.vector.tensor_tensor(out=taste[b][:], in0=bank[:], in1=weights[:], op=MULT)
+                weigh(taste[b], bank)
             else:
                 nc.scalar.copy(out=taste[b][:], in_=bank[:])
 
-        def multiply(b):
-            if b == 0:
-                nc.scalar.copy(out=product[b][:], in_=banks[0][:])
-                return
-            nc.vector.tensor_tensor(out=product[b % len(product)][:], in0=banks[(0, 1, 4, 5)[b % 4]][:], in1=weights[:], op=MULT)
-
         def scatter(b):
-            nc.vector.tensor_tensor(page[b][:].indirect(put_list[:]), product[b % len(product)][:], taste[b][:], MULT)
+            nc.vector.tensor_tensor(page[b][:].indirect(put_list[:]), recent[b][:], taste[b][:], MULT)
             nc.sync.dma_start(out=out_1[b * P : (b + 1) * P, :], in_=page[b][:])
 
-        def turn_page(b, engines):
+        def turn_banks(b):
+            first = 2 - 2 * (b % 2)
+            return banks[first : first + 2]
+
+        def turn_page(b):
             g, q = divmod(b, TILES_PER_PASS)
             for h in range(HALVES):
-                bank = bank_pair(b)[h]
+                bank = turn_banks(b)[h]
                 for j in range(4):
                     col = h * BANK + j * P
                     nc.tensor.transpose(bank[:, j * P : (j + 1) * P], page[b][:, col : col + P], identity[:])
                 dst = turned[g][h][:].rearrange("m (j u p e) -> m j u p e", j=4, u=2, e=2)[:, :, :, 32 * q : 32 * (q + 1), :]
-                engines[h](out=dst, in_=bank[:].rearrange("m (j p u e) -> m j u p e", j=4, u=2, e=2))
+                nc.scalar.copy(out=dst, in_=bank[:].rearrange("m (j p u e) -> m j u p e", j=4, u=2, e=2))
 
-        def regroup_page(g, h, engines):
+        def regroup_page(g, h, copies):
             words = turned[g][h][:].bitcast(F32)
-            grouped[g, h] = sbuf(f"grouped{g}_{h}", [P, BANK * PACK], BF16, tag=(("slot-1", "slot1"), ("slot2", "slot3"))[g][h])
+            grouped[g, h] = sbuf(f"grouped{g}_{h}", [P, BANK * PACK], BF16, tag=grouped_tag[g, h])
             for s in range(2):
                 bank = banks[4 + 2 * h + s]
                 for i in range(4):
                     col = (4 * s + i) * P
                     nc.tensor.transpose(bank[:, i * P : (i + 1) * P], words[:, col : col + P], identity[:])
                 dst = grouped[g, h][:].bitcast(F32)[:, s * BANK : (s + 1) * BANK].rearrange("p (j m u) -> p j m u", j=2, u=2)
-                engines[s](out=dst, in_=bank[:].rearrange("p (j u m) -> p j m u", j=2, u=2))
+                copies[s](out=dst, in_=bank[:].rearrange("p (j u m) -> p j m u", j=2, u=2))
 
         def quantize_page(g, h, tag=None):
             cols = slice(h * BANK, (h + 1) * BANK)
@@ -251,27 +255,26 @@ def tile_list_shelf_suggester_kernel(
             words = out_2[g].rearrange("p m t -> p (m t)").bitcast(I32)
             nc.sync.dma_start(out=words[:, cols], in_=page_codes[g, h][:].bitcast(I32))
 
-        units = [(n, h) for c in range(N // W3_CHUNK) for h in range(HALVES) for n in (2 * c, 2 * c + 1)]
+        pieces = [(n, h) for c in range(W3_CHUNKS) for h in range(HALVES) for n in (2 * c, 2 * c + 1)]
 
         def gate_bank(i):
             return banks[(2, 0, 4)[i % 3]]
 
         def fresh_bank(i):
-            return banks[(3, 1, 5, 6, 7)[i % 5]]
+            return banks[(3, 1, 5, 6, 7)[i % STEPS]]
 
         def gate_pass(i, g):
-            n, h = units[i]
-            w3_cols = slice(g * W3_CHUNK + n % 2 * P, g * W3_CHUNK + (n % 2 + 1) * P)
+            n, h = pieces[i]
+            cols = chunk_columns(n, g)
             nc.tensor.matmul_mx(
                 out=gate_bank(i)[:],
-                lhsT=w3_codes[n // 2][:, w3_cols].bitcast(FP8X4),
-                lhsT_scale=w3_plane[n // 2][:, w3_cols],
+                lhsT=w3_codes[n // 2][:, cols].bitcast(FP8X4), lhsT_scale=w3_plane[n // 2][:, cols],
                 rhs=page_codes[g, h][:].bitcast(FP8X4), rhs_scale=page_plane[:, g, h * BANK : (h + 1) * BANK],
                 start=(g == 0), stop=(g == PASSES - 1),
             )
 
         def fresh_pass(i, g):
-            n, h = units[i]
+            n, h = pieces[i]
             nc.tensor.matmul_mx(
                 out=fresh_bank(i)[:],
                 lhsT=w4_codes[:, g, 2 * n * P : 2 * (n + 1) * P].bitcast(FP4X4),
@@ -281,72 +284,76 @@ def tile_list_shelf_suggester_kernel(
             )
 
         def scores(i):
-            n, h = units[i]
+            n, h = pieces[i]
             return old[n // 2][:, n % 2, h * BANK : (h + 1) * BANK]
 
         def blend_begin(i):
-            slot = i % len(step)
-            nc.scalar.activation(out=rest[i % len(rest)][:], in_=gate_bank(i)[:], func=SIGMOID, scale=-1.0)
-            nc.vector.tensor_tensor(out=step[slot][:], in0=fresh_bank(i)[:], in1=scores(i), op=SUB)
-            engine = nc.vector if i in (1, len(units) - 1) else nc.gpsimd
-            engine.tensor_tensor(out=step[slot][:], in0=step[slot][:], in1=rest[i % len(rest)][:], op=MULT)
+            nc.scalar.activation(out=rest[i % RESTS][:], in_=gate_bank(i)[:], func=SIGMOID, scale=-1.0)
+            nc.vector.tensor_tensor(out=step[i % STEPS][:], in0=fresh_bank(i)[:], in1=scores(i), op=SUB)
+            engine = nc.vector if i in (1, len(pieces) - 1) else nc.gpsimd
+            engine.tensor_tensor(out=step[i % STEPS][:], in0=step[i % STEPS][:], in1=rest[i % RESTS][:], op=MULT)
 
         def blend_end(i):
-            n, h = units[i]
-            nc.vector.tensor_tensor(out=scores(i), in0=fresh_bank(i)[:], in1=step[i % len(step)][:], op=SUB)
+            n, h = pieces[i]
+            nc.vector.tensor_tensor(out=scores(i), in0=fresh_bank(i)[:], in1=step[i % STEPS][:], op=SUB)
             nc.sync.dma_start(out=out_0[n * P : (n + 1) * P, h * BANK : (h + 1) * BANK], in_=scores(i))
 
         on_scalar = (nc.scalar.copy, nc.scalar.copy)
         shared = (nc.vector.tensor_copy, nc.scalar.copy)
-
         last = ROW_TILES - 1
-        piece = W3_CHUNK * PACK
+
         nc.vector.tensor_copy(picked_words[0][:], table_words[0][:].bitcast(U32).indirect(pick_list[:]))
         for a in range(PASSES):
             nc.vector.tensor_copy(picked_scales[a][:], table_scales[:, a, :].indirect(pick_list[:]))
         nc.vector.tensor_copy(picked_words[1][:], table_words[1][:].bitcast(U32).indirect(pick_list[:]))
-        old.append(sbuf("old2", [P, W3_CHUNK // P, T2], F32, tag="table_words0"))
+        old.append(sbuf("old2", [P, CHUNK // P, T2], F32, tag="table_words0"))
         load_old(2)
-        w3_staged = sbuf("w3_staged", [P, PASSES * piece], BF16, tag="table_words1")
+        w3_first = sbuf("w3_first", [P, PASSES * CHUNK_VALUES], BF16, tag="table_words1")
         stage_w1(0)
-        quantize_w1(0, PASSES)
+        quantize_w1(0, [pass_part(w1_staged[0], a) for a in range(PASSES)])
         taste_product(0)
         for b in range(TILES_PER_PASS):
             recent_product(b)
-            multiply(b)
         stage_w1(1)
         taste_product(1)
         scatter(0)
         for b in range(TILES_PER_PASS, ROW_TILES):
             recent_product(b)
-            multiply(b)
-        tastes = {1: (2,), 2: (3, 4, 5), 3: (6, 7)}
-        for b in range(1, ROW_TILES):
-            if b < len(W1_CHUNKS):
-                quantize_w1(b, 1)
-                if b + 1 < len(W1_CHUNKS):
-                    stage_w1(b + 1)
-                for ahead in tastes[b]:
-                    taste_product(ahead)
+
+        quantize_w1(1, [w1_staged[1][:]])
+        stage_w1(2)
+        taste_product(2)
+        scatter(1)
+        quantize_w1(2, [w1_staged[0][:]])
+        stage_w1(3)
+        for b in (3, 4, 5):
+            taste_product(b)
+        scatter(2)
+        turn_page(0)
+        turn_page(1)
+        quantize_w1(3, [w1_staged[1][:]])
+        for b in (6, 7):
+            taste_product(b)
+        scatter(3)
+        turn_page(2)
+
+        scatter(4)
+        stage_w3(pass_part(w3_first, 0), 0, 0, nc.scalar.copy)
+        turn_page(3)
+        scatter(5)
+        for h in range(HALVES):
+            regroup_page(0, h, on_scalar)
+        stage_w3(pass_part(w3_first, 1), 0, 1, nc.scalar.copy)
+        turn_page(4)
+        for b in (6, 7):
             scatter(b)
-            if b == TILES_PER_PASS + 1:
-                for h in range(HALVES):
-                    regroup_page(0, h, on_scalar)
-            if b in (TILES_PER_PASS, TILES_PER_PASS + 1):
-                a = b - TILES_PER_PASS
-                stage(w3_staged[:, a * piece : (a + 1) * piece], w3_early[a][:, :, :W3_CHUNK])
-            for done in {1: (), 2: (0, 1)}.get(b, (b - 1,)):
-                turn_page(done, on_scalar)
-        mid_staged = [sbuf("mid_staged0", [P, piece], BF16, tag=f"slot{last - 1}")]
-        stage(mid_staged[0][:], w3_early[0][:, :, W3_CHUNK : 2 * W3_CHUNK])
-        for repeat in range(3):
-            nc.tensor.matmul_mx(
-                out=bank_pair(last)[0][:], lhsT=w1_codes[0][:, :P].bitcast(FP8X4), lhsT_scale=w1_plane[0][:, :P],
-                rhs=picked_words[0][:].bitcast(FP8X4), rhs_scale=picked_scales[0][:], start=True, stop=True,
-            )
-        quantize_w3(0, [w3_staged], f"slot{last}")
-        quantize_page(0, 0, f"product{last}")
-        turn_page(last, on_scalar)
+            turn_page(b - 1)
+        w3_middle = [sbuf("w3_middle0", [P, CHUNK_VALUES], BF16, tag=taste_tag[last - 1])]
+        stage_w3(w3_middle[0][:], 1, 0, nc.scalar.copy)
+
+        quantize_w3(0, [w3_first[:]], taste_tag[last])
+        quantize_page(0, 0, f"recent{last}")
+        turn_page(last)
         gate_pass(0, 0)
         fresh_pass(0, 0)
         quantize_page(0, 1, "table_words1")
@@ -354,13 +361,13 @@ def tile_list_shelf_suggester_kernel(
         quantize_page(1, 0)
         regroup_page(1, 1, on_scalar)
         quantize_page(1, 1)
-        mid_staged.append(sbuf("mid_staged1", [P, piece], BF16, tag="slot-1"))
-        stage(mid_staged[1][:], w3_early[1][:, :, W3_CHUNK : 2 * W3_CHUNK], nc.vector.tensor_copy)
-        quantize_w3(1, mid_staged, "slot1")
-        late_staged = sbuf("late_staged", [P, PASSES * piece], BF16)
+        w3_middle.append(sbuf("w3_middle1", [P, CHUNK_VALUES], BF16, tag=grouped_tag[0, 0]))
+        stage_w3(w3_middle[1][:], 1, 1, nc.vector.tensor_copy)
+        quantize_w3(1, [t[:] for t in w3_middle], grouped_tag[0, 1])
+        w3_last = sbuf("w3_last", [P, PASSES * CHUNK_VALUES], BF16)
         for a in range(PASSES):
-            stage(late_staged[:, a * piece : (a + 1) * piece], w3_early[a][:, :, 2 * W3_CHUNK :])
-        quantize_w3(2, [late_staged], "slot2")
+            stage_w3(pass_part(w3_last, a), 2, a, nc.scalar.copy)
+        quantize_w3(2, [w3_last[:]], grouped_tag[1, 0])
         scale_rows = out_3.bitcast(I32)
         for q in range(4):
             nc.sync.dma_start(
@@ -368,14 +375,14 @@ def tile_list_shelf_suggester_kernel(
                 in_=page_plane[32 * q : 32 * q + 4].bitcast(I32),
             )
 
-        rest = [sbuf(f"rest{i}", [P, BANK], F32, tag=f"raw{i}_0") for i in range(4)]
-        step = [sbuf(f"step{i}", [P, BANK], F32, tag=f"product{i}") for i in range(5)]
-        for i in range(len(units)):
+        rest = [sbuf(f"rest{i}", [P, BANK], F32, tag=f"w1_raw{i}_0") for i in range(RESTS)]
+        step = [sbuf(f"step{i}", [P, BANK], F32, tag=f"recent{i}") for i in range(STEPS)]
+        for i in range(len(pieces)):
             for one_pass in (fresh_pass, gate_pass):
                 for g in range(1 if i == 0 else 0, PASSES):
                     one_pass(i, g)
             blend_begin(i)
-            if i >= 2:
-                blend_end(i - 2)
-        blend_end(len(units) - 2)
-        blend_end(len(units) - 1)
+            if i >= END_LAG:
+                blend_end(i - END_LAG)
+        for i in range(len(pieces) - END_LAG, len(pieces)):
+            blend_end(i)

@@ -33,6 +33,7 @@ CHUNK_VALUES = CHUNK * PACK
 FIRST_TABLE_LOADS = 4
 RESTS = 4
 STEPS = 5
+W3_LAST_AT = 2
 END_LAG = 2
 
 
@@ -255,13 +256,13 @@ def tile_list_shelf_suggester_kernel(
             words = out_2[g].rearrange("p m t -> p (m t)").bitcast(I32)
             nc.sync.dma_start(out=words[:, cols], in_=page_codes[g, h][:].bitcast(I32))
 
-        pieces = [(n, h) for c in range(W3_CHUNKS) for h in range(HALVES) for n in (2 * c, 2 * c + 1)]
+        pieces = [(n, h) for c in range(W3_CHUNKS) for n, h in ((2 * c, 0), (2 * c, 1), (2 * c + 1, 1), (2 * c + 1, 0))]
 
         def gate_bank(i):
-            return banks[(2, 0, 4)[i % 3]]
+            return banks[(0, 2, 4)[i % 3]]
 
         def fresh_bank(i):
-            return banks[(3, 1, 5, 6, 7)[i % STEPS]]
+            return banks[(1, 3, 5, 7, 6)[i % STEPS]]
 
         def gate_pass(i, g):
             n, h = pieces[i]
@@ -287,11 +288,14 @@ def tile_list_shelf_suggester_kernel(
             n, h = pieces[i]
             return old[n // 2][:, n % 2, h * BANK : (h + 1) * BANK]
 
+        def rest_of(i):
+            return rest_once if i == W3_LAST_AT else rest[i % RESTS]
+
         def blend_begin(i):
-            nc.scalar.activation(out=rest[i % RESTS][:], in_=gate_bank(i)[:], func=SIGMOID, scale=-1.0)
+            nc.scalar.activation(out=rest_of(i)[:], in_=gate_bank(i)[:], func=SIGMOID, scale=-1.0)
             nc.vector.tensor_tensor(out=step[i % STEPS][:], in0=fresh_bank(i)[:], in1=scores(i), op=SUB)
-            engine = nc.vector if i in (1, len(pieces) - 1) else nc.gpsimd
-            engine.tensor_tensor(out=step[i % STEPS][:], in0=step[i % STEPS][:], in1=rest[i % RESTS][:], op=MULT)
+            engine = nc.vector if i in (2, len(pieces) - 1) else nc.gpsimd
+            engine.tensor_tensor(out=step[i % STEPS][:], in0=step[i % STEPS][:], in1=rest_of(i)[:], op=MULT)
 
         def blend_end(i):
             n, h = pieces[i]
@@ -348,26 +352,21 @@ def tile_list_shelf_suggester_kernel(
         for b in (6, 7):
             scatter(b)
             turn_page(b - 1)
-        w3_middle = [sbuf("w3_middle0", [P, CHUNK_VALUES], BF16, tag=taste_tag[last - 1])]
-        stage_w3(w3_middle[0][:], 1, 0, nc.scalar.copy)
 
         quantize_w3(0, [w3_first[:]], taste_tag[last])
         quantize_page(0, 0, f"recent{last}")
         turn_page(last)
-        gate_pass(0, 0)
-        fresh_pass(0, 0)
-        quantize_page(0, 1, "table_words1")
         regroup_page(1, 0, shared)
         quantize_page(1, 0)
+        quantize_page(0, 1, grouped_tag[1, 0])
         regroup_page(1, 1, on_scalar)
         quantize_page(1, 1)
-        w3_middle.append(sbuf("w3_middle1", [P, CHUNK_VALUES], BF16, tag=grouped_tag[0, 0]))
-        stage_w3(w3_middle[1][:], 1, 1, nc.vector.tensor_copy)
-        quantize_w3(1, [t[:] for t in w3_middle], grouped_tag[0, 1])
-        w3_last = sbuf("w3_last", [P, PASSES * CHUNK_VALUES], BF16)
+        w3_middle = sbuf("w3_middle", [P, PASSES * CHUNK_VALUES], BF16, tag=grouped_tag[0, 0])
         for a in range(PASSES):
-            stage_w3(pass_part(w3_last, a), 2, a, nc.scalar.copy)
-        quantize_w3(2, [w3_last[:]], grouped_tag[1, 0])
+            stage_w3(pass_part(w3_middle, a), 1, a, nc.vector.tensor_copy)
+        quantize_w3(1, [w3_middle[:]], None)
+        w3_last = [sbuf("w3_last0", [P, CHUNK_VALUES], BF16, tag="turned1_1")]
+        stage_w3(w3_last[0][:], 2, 0, nc.scalar.copy)
         scale_rows = out_3.bitcast(I32)
         for q in range(4):
             nc.sync.dma_start(
@@ -376,12 +375,17 @@ def tile_list_shelf_suggester_kernel(
             )
 
         rest = [sbuf(f"rest{i}", [P, BANK], F32, tag=f"w1_raw{i}_0") for i in range(RESTS)]
+        rest_once = sbuf("rest_once", [P, BANK], F32)
         step = [sbuf(f"step{i}", [P, BANK], F32, tag=f"recent{i}") for i in range(STEPS)]
         for i in range(len(pieces)):
             for one_pass in (fresh_pass, gate_pass):
-                for g in range(1 if i == 0 else 0, PASSES):
+                for g in range(PASSES):
                     one_pass(i, g)
             blend_begin(i)
+            if i == W3_LAST_AT:
+                w3_last.append(sbuf("w3_last1", [P, CHUNK_VALUES], BF16, tag="rest_once"))
+                stage_w3(w3_last[1][:], 2, 1, nc.scalar.copy)
+                quantize_w3(2, [t[:] for t in w3_last], grouped_tag[1, 1])
             if i >= END_LAG:
                 blend_end(i - END_LAG)
         for i in range(len(pieces) - END_LAG, len(pieces)):

@@ -31,9 +31,9 @@ W1_CHUNKS = H // CHUNK
 W3_CHUNKS = N // CHUNK
 CHUNK_VALUES = CHUNK * PACK
 FIRST_TABLE_LOADS = 4
+AHEAD = 2
 RESTS = 4
 STEPS = 5
-W3_LAST_AT = 2
 END_LAG = 2
 
 
@@ -69,15 +69,18 @@ def tile_list_shelf_suggester_kernel(
         old = [sbuf(f"old{c}", [P, CHUNK // P, T2], F32) for c in range(W3_CHUNKS - 1)]
         w1_staged = [sbuf(f"w1_staged{i}", [P, PASSES * CHUNK_VALUES], BF16) for i in range(2)]
         w1_plane = [sbuf(f"w1_plane{c}", [P, PASSES * CHUNK], U8) for c in range(W1_CHUNKS)]
-        w3_plane = [sbuf(f"w3_plane{c}", [P, PASSES * CHUNK], U8) for c in range(W3_CHUNKS)]
+        w3_codes = sbuf("w3_codes", [P, PASSES, N], U32)
         recent = [sbuf(f"recent{b}", [P, S], F32) for b in range(ROW_TILES)]
-        turned = [[sbuf(f"turned{g}_{h}", [P, PACK * K_PASS], BF16) for h in range(HALVES)] for g in range(PASSES)]
+        turned = {
+            (g, h, s): sbuf(f"turned{g}_{h}_{s}", [P, 2 * K_PASS], BF16)
+            for g in range(PASSES) for h in range(HALVES) for s in range(2)
+        }
         page_plane = sbuf("page_plane", [P, PASSES, T2], U8)
-        w1_codes, w3_codes, page_codes, taste, grouped = {}, {}, {}, {}, {}
+        w1_codes, page_codes, taste, grouped = {}, {}, {}, {}
 
         taste_tag = {b: f"taste{b}" for b in range(ROW_TILES)}
-        taste_tag.update({1: "w1_raw1_1", 3: "w1_raw3_1", 4: "w1_raw3_0"})
-        grouped_tag = {(0, 0): "w1_raw0_1", (0, 1): taste_tag[1], (1, 0): taste_tag[2], (1, 1): taste_tag[3]}
+        taste_tag.update({1: "w1_raw1_1", 2: "w1_raw2_1", 4: "w1_raw3_1", 7: "w3_raw0"})
+        grouped_tag = {(0, 0): "w1_raw0_1", (0, 1): taste_tag[1], (1, 0): taste_tag[2], (1, 1): taste_tag[4]}
 
         nc.vector.memset(table_scales[:].bitcast(I32), 0)
         nc.vector.memset(w2_plane[:].bitcast(I32), 0)
@@ -89,11 +92,8 @@ def tile_list_shelf_suggester_kernel(
 
         def load_plane(plane, scales):
             rows = scales.bitcast(I32)
-            for q in range(4):
-                nc.sync.dma_start(
-                    out=plane[32 * q : 32 * q + 4].bitcast(I32),
-                    in_=rows[:, 4 * q : 4 * q + 4, :].rearrange("a r n -> r a n"),
-                )
+            for r in range(4):
+                nc.sync.dma_start(out=plane[r:P:32].bitcast(I32), in_=rows[:, r:16:4, :].rearrange("a q n -> q a n"))
 
         def load_pass(tile, w, a, first):
             rows = w[a * K_PASS : (a + 1) * K_PASS, first : first + tile.shape[2]]
@@ -134,23 +134,18 @@ def tile_list_shelf_suggester_kernel(
         load_w1(0, 1)
         nc.sync.dma_start(put_list[:], offs2)
         load_page(0)
-        load_w1(1, 0)
-        load_w1(1, 1)
-        load_w1(2, 0)
-        load_page(1)
-        load_w1(2, 1)
-        load_w1(3, 0)
-        load_w1(3, 1)
-        load_page(2)
-        load_page(3)
-        load_page(4)
+        for c in range(1, W1_CHUNKS):
+            for a in range(PASSES):
+                load_w1(c, a)
+            load_page(c)
         load_w3(0)
+        load_page(4)
         load_page(5)
-        load_w3(1)
         load_page(6)
-        load_page(7)
+        load_w3(1)
         nc.sync.dma_start(out=w4_codes[:].bitcast(I32), in_=w4_words.bitcast(I32).rearrange("a p n -> p a n"))
         load_plane(w4_plane, w4_scales)
+        load_page(7)
         load_old(0)
         load_old(1)
 
@@ -160,8 +155,8 @@ def tile_list_shelf_suggester_kernel(
         def pass_part(staged, a):
             return staged[:, a * CHUNK_VALUES : (a + 1) * CHUNK_VALUES]
 
-        def stage_w1(c):
-            for a in range(PASSES):
+        def stage_w1(c, passes=(0, 1)):
+            for a in passes:
                 stage(pass_part(w1_staged[c % 2], a), w1_raw[c][a][:], nc.scalar.copy)
 
         def stage_w3(dst, c, a, copy):
@@ -177,9 +172,9 @@ def tile_list_shelf_suggester_kernel(
             w1_codes[c] = sbuf(f"w1_codes{c}", [P, PASSES * CHUNK], U32)
             quantize_chunk(w1_codes[c], w1_plane[c], parts)
 
-        def quantize_w3(c, parts, tag):
-            w3_codes[c] = sbuf(f"w3_codes{c}", [P, PASSES * CHUNK], U32, tag=tag)
-            quantize_chunk(w3_codes[c], w3_plane[c], parts)
+        def quantize_w3(staged, a, first):
+            cols = slice(first, first + staged.shape[1] // PACK)
+            nc.vector.quantize_mx(out=w3_codes[:, a, cols].bitcast(FP8X4), scales=w3_plane[:, a, cols], in_=staged[:])
 
         def chunk_columns(tile, a):
             first = a * CHUNK + tile % 2 * P
@@ -189,7 +184,7 @@ def tile_list_shelf_suggester_kernel(
             nc.vector.tensor_tensor(out=dst[:], in0=bank[:], in1=weights[:], op=MULT)
 
         def recent_product(b):
-            bank = banks[(0, 1, 4, 5)[b % 4]]
+            bank = banks[4 + b % 4]
             g, col = divmod(b * P, K_PASS)
             for a in range(PASSES):
                 nc.tensor.matmul_mx(
@@ -204,72 +199,93 @@ def tile_list_shelf_suggester_kernel(
             else:
                 weigh(recent[b], bank)
 
-        def taste_product(b):
+        def taste_product(b, homes):
             taste[b] = sbuf(f"taste{b}", [P, S], F32, tag=taste_tag[b])
-            bank = banks[(6, 7, 2, 3, 0, 1, 6, 7)[b]]
-            for a in range(PASSES):
-                cols = chunk_columns(b, a)
-                nc.tensor.matmul_mx(
-                    out=bank[:],
-                    lhsT=w1_codes[b // 2][:, cols].bitcast(FP8X4), lhsT_scale=w1_plane[b // 2][:, cols],
-                    rhs=picked_words[a][:].bitcast(FP8X4), rhs_scale=picked_scales[a][:],
-                    start=(a == 0), stop=(a == PASSES - 1),
-                )
-            if b == 0:
-                weigh(taste[b], bank)
-            else:
-                nc.scalar.copy(out=taste[b][:], in_=bank[:])
+            parts = len(homes)
+            for i in range(parts):
+                picks = slice(i * S // parts, (i + 1) * S // parts)
+                sums = homes[i][:, : S // parts]
+                for a in range(PASSES):
+                    cols = chunk_columns(b, a)
+                    nc.tensor.matmul_mx(
+                        out=sums,
+                        lhsT=w1_codes[b // 2][:, cols].bitcast(FP8X4), lhsT_scale=w1_plane[b // 2][:, cols],
+                        rhs=picked_words[a][:, picks].bitcast(FP8X4), rhs_scale=picked_scales[a][:, picks],
+                        start=(a == 0), stop=(a == PASSES - 1),
+                    )
+                if b == 0:
+                    weigh(taste[b], homes[i])
+                else:
+                    nc.scalar.copy(out=taste[b][:, picks], in_=sums)
 
         def scatter(b):
             nc.vector.tensor_tensor(page[b][:].indirect(put_list[:]), recent[b][:], taste[b][:], MULT)
             nc.sync.dma_start(out=out_1[b * P : (b + 1) * P, :], in_=page[b][:])
 
-        def turn_banks(b):
-            first = 2 - 2 * (b % 2)
-            return banks[first : first + 2]
-
-        def turn_page(b):
+        def turn_half(b, h, homes):
             g, q = divmod(b, TILES_PER_PASS)
-            for h in range(HALVES):
-                bank = turn_banks(b)[h]
-                for j in range(4):
-                    col = h * BANK + j * P
-                    nc.tensor.transpose(bank[:, j * P : (j + 1) * P], page[b][:, col : col + P], identity[:])
-                dst = turned[g][h][:].rearrange("m (j u p e) -> m j u p e", j=4, u=2, e=2)[:, :, :, 32 * q : 32 * (q + 1), :]
-                nc.scalar.copy(out=dst, in_=bank[:].rearrange("m (j p u e) -> m j u p e", j=4, u=2, e=2))
-
-        def regroup_page(g, h, copies):
-            words = turned[g][h][:].bitcast(F32)
-            grouped[g, h] = sbuf(f"grouped{g}_{h}", [P, BANK * PACK], BF16, tag=grouped_tag[g, h])
+            blocks = 4 // len(homes)
+            for k in range(4):
+                col = h * BANK + k * P
+                at = k % blocks * P
+                nc.tensor.transpose(homes[k // blocks][:, at : at + P], page[b][:, col : col + P], identity[:])
             for s in range(2):
-                bank = banks[4 + 2 * h + s]
-                for i in range(4):
-                    col = (4 * s + i) * P
-                    nc.tensor.transpose(bank[:, i * P : (i + 1) * P], words[:, col : col + P], identity[:])
-                dst = grouped[g, h][:].bitcast(F32)[:, s * BANK : (s + 1) * BANK].rearrange("p (j m u) -> p j m u", j=2, u=2)
-                copies[s](out=dst, in_=bank[:].rearrange("p (j u m) -> p j m u", j=2, u=2))
+                at = 2 * s % blocks * P
+                src = homes[2 * s // blocks][:, at : at + 2 * P]
+                dst = turned[g, h, s][:].rearrange("m (j u p e) -> m j u p e", j=2, u=2, e=2)[:, :, :, 32 * q : 32 * (q + 1), :]
+                nc.scalar.copy(out=dst, in_=src.rearrange("m (j p u e) -> m j u p e", j=2, u=2, e=2))
 
-        def quantize_page(g, h, tag=None):
+        def turn_page(b, two_banks):
+            for h in range(HALVES):
+                turn_half(b, h, two_banks[h : h + 1])
+
+        def regroup_part(g, h, s, homes):
+            words = turned[g, h, s][:].bitcast(F32)
+            blocks = 2 // len(homes)
+            for j in range(2):
+                for u in range(2):
+                    at = (j % blocks * 2 + u) * P
+                    col = (2 * j + u) * P
+                    nc.tensor.transpose(homes[j // blocks][:, at : at + P], words[:, col : col + P], identity[:])
+            for i, bank in enumerate(homes):
+                width = blocks * 2 * P
+                first = s * BANK + i * width
+                dst = grouped[g, h][:].bitcast(F32)[:, first : first + width].rearrange("p (j m u) -> p j m u", j=blocks, u=2)
+                nc.scalar.copy(out=dst, in_=bank[:, :width].rearrange("p (j u m) -> p j m u", j=blocks, u=2))
+
+        def regroup_page(g, h, homes):
+            grouped[g, h] = sbuf(f"grouped{g}_{h}", [P, BANK * PACK], BF16, tag=grouped_tag[g, h])
+            regroup_part(g, h, 0, homes[:1])
+            regroup_part(g, h, 1, homes[1:])
+
+        def quantize_page(g, h, tag=None, parts=1):
             cols = slice(h * BANK, (h + 1) * BANK)
             page_codes[g, h] = sbuf(f"page_codes{g}_{h}", [P, BANK], U32, tag=tag)
-            nc.vector.quantize_mx(out=page_codes[g, h][:].bitcast(FP8X4), scales=page_plane[:, g, cols], in_=grouped[g, h][:])
+            width = BANK // parts
+            for first in range(0, BANK, width):
+                nc.vector.quantize_mx(
+                    out=page_codes[g, h][:, first : first + width].bitcast(FP8X4),
+                    scales=page_plane[:, g, h * BANK + first : h * BANK + first + width],
+                    in_=grouped[g, h][:, PACK * first : PACK * (first + width)],
+                )
             words = out_2[g].rearrange("p m t -> p (m t)").bitcast(I32)
             nc.sync.dma_start(out=words[:, cols], in_=page_codes[g, h][:].bitcast(I32))
 
-        pieces = [(n, h) for c in range(W3_CHUNKS) for n, h in ((2 * c, 0), (2 * c, 1), (2 * c + 1, 1), (2 * c + 1, 0))]
+        pieces = [(0, 0), (1, 0), (0, 1), (1, 1)]
+        pieces.extend((n, h) for n in range(2, N // P) for h in (1, 0))
 
         def gate_bank(i):
-            return banks[(0, 2, 4)[i % 3]]
+            return gate_ring[i % 3]
 
         def fresh_bank(i):
-            return banks[(1, 3, 5, 7, 6)[i % STEPS]]
+            return fresh_ring[i % STEPS]
 
         def gate_pass(i, g):
             n, h = pieces[i]
-            cols = chunk_columns(n, g)
+            cols = slice(n * P, (n + 1) * P)
             nc.tensor.matmul_mx(
                 out=gate_bank(i)[:],
-                lhsT=w3_codes[n // 2][:, cols].bitcast(FP8X4), lhsT_scale=w3_plane[n // 2][:, cols],
+                lhsT=w3_codes[:, g, cols].bitcast(FP8X4), lhsT_scale=w3_plane[:, g, cols],
                 rhs=page_codes[g, h][:].bitcast(FP8X4), rhs_scale=page_plane[:, g, h * BANK : (h + 1) * BANK],
                 start=(g == 0), stop=(g == PASSES - 1),
             )
@@ -288,22 +304,17 @@ def tile_list_shelf_suggester_kernel(
             n, h = pieces[i]
             return old[n // 2][:, n % 2, h * BANK : (h + 1) * BANK]
 
-        def rest_of(i):
-            return rest_once if i == W3_LAST_AT else rest[i % RESTS]
-
         def blend_begin(i):
-            nc.scalar.activation(out=rest_of(i)[:], in_=gate_bank(i)[:], func=SIGMOID, scale=-1.0)
+            nc.scalar.activation(out=rest[i % RESTS][:], in_=gate_bank(i)[:], func=SIGMOID, scale=-1.0)
             nc.vector.tensor_tensor(out=step[i % STEPS][:], in0=fresh_bank(i)[:], in1=scores(i), op=SUB)
-            engine = nc.vector if i in (2, len(pieces) - 1) else nc.gpsimd
-            engine.tensor_tensor(out=step[i % STEPS][:], in0=step[i % STEPS][:], in1=rest_of(i)[:], op=MULT)
+            engine = nc.vector if i in (0, len(pieces) // 2, len(pieces) - 1) else nc.gpsimd
+            engine.tensor_tensor(out=step[i % STEPS][:], in0=step[i % STEPS][:], in1=rest[i % RESTS][:], op=MULT)
 
         def blend_end(i):
             n, h = pieces[i]
             nc.vector.tensor_tensor(out=scores(i), in0=fresh_bank(i)[:], in1=step[i % STEPS][:], op=SUB)
             nc.sync.dma_start(out=out_0[n * P : (n + 1) * P, h * BANK : (h + 1) * BANK], in_=scores(i))
 
-        on_scalar = (nc.scalar.copy, nc.scalar.copy)
-        shared = (nc.vector.tensor_copy, nc.scalar.copy)
         last = ROW_TILES - 1
 
         nc.vector.tensor_copy(picked_words[0][:], table_words[0][:].bitcast(U32).indirect(pick_list[:]))
@@ -315,77 +326,83 @@ def tile_list_shelf_suggester_kernel(
         w3_first = sbuf("w3_first", [P, PASSES * CHUNK_VALUES], BF16, tag="table_words1")
         stage_w1(0)
         quantize_w1(0, [pass_part(w1_staged[0], a) for a in range(PASSES)])
-        taste_product(0)
+        taste_product(0, banks[0:1])
         for b in range(TILES_PER_PASS):
             recent_product(b)
         stage_w1(1)
-        taste_product(1)
+        taste_product(1, banks[2:3])
         scatter(0)
         for b in range(TILES_PER_PASS, ROW_TILES):
             recent_product(b)
 
         quantize_w1(1, [w1_staged[1][:]])
         stage_w1(2)
-        taste_product(2)
+        taste_product(2, banks[0:4])
         scatter(1)
         quantize_w1(2, [w1_staged[0][:]])
-        stage_w1(3)
-        for b in (3, 4, 5):
-            taste_product(b)
+        w3_second = sbuf("w3_second", [P, CHUNK_VALUES], BF16, tag="w1_staged0")
+        taste_product(3, banks[2:4])
+        stage_w1(3, (0,))
+        turn_page(0, banks[0:2])
+        stage_w1(3, (1,))
         scatter(2)
-        turn_page(0)
-        turn_page(1)
         quantize_w1(3, [w1_staged[1][:]])
-        for b in (6, 7):
-            taste_product(b)
+        turn_page(1, banks[2:4])
+        taste_product(4, banks[6:8])
+        taste_product(5, banks[4:6])
         scatter(3)
-        turn_page(2)
-
-        scatter(4)
+        turn_page(2, banks[6:8])
         stage_w3(pass_part(w3_first, 0), 0, 0, nc.scalar.copy)
-        turn_page(3)
+        taste_product(6, banks[6:8])
+        scatter(4)
+        turn_page(3, banks[4:6])
+        stage_w3(pass_part(w3_first, 1), 1, 0, nc.scalar.copy)
+        regroup_page(0, 0, banks[2:4])
         scatter(5)
-        for h in range(HALVES):
-            regroup_page(0, h, on_scalar)
-        stage_w3(pass_part(w3_first, 1), 0, 1, nc.scalar.copy)
-        turn_page(4)
-        for b in (6, 7):
-            scatter(b)
-            turn_page(b - 1)
+        turn_page(4, banks[4:6])
+        stage_w3(w3_second[:], 2, 0, nc.scalar.copy)
+        taste_product(7, banks[6:8] + banks[2:4])
+        regroup_page(0, 1, banks[0:2])
+        scatter(6)
+        quantize_page(0, 0)
+        turn_page(5, banks[4:6])
+        turn_page(6, banks[6:8])
+        fresh_ring = [banks[i] for i in (2, 3, 6, 7, 4)]
+        gate_ring = [banks[i] for i in (0, 1, 5)]
+        for i in range(AHEAD):
+            fresh_pass(i, 0)
+        scatter(7)
 
-        quantize_w3(0, [w3_first[:]], taste_tag[last])
-        quantize_page(0, 0, f"recent{last}")
-        turn_page(last)
-        regroup_page(1, 0, shared)
-        quantize_page(1, 0)
+        w3_plane = sbuf("w3_plane", [P, PASSES, N], U8, tag=taste_tag[last])
+        w3_third = sbuf("w3_third", [P, W3_CHUNKS * CHUNK_VALUES], BF16, tag=f"recent{last}")
+        quantize_w3(w3_first, 0, 0)
+        turn_half(last, 0, banks[4:6])
+        turn_half(last, 1, banks[0:2])
+        regroup_page(1, 0, banks[6:8])
+        quantize_page(1, 0, parts=2)
+        for i in range(AHEAD):
+            gate_pass(i, 0)
+        regroup_page(1, 1, banks[4:6])
         quantize_page(0, 1, grouped_tag[1, 0])
-        regroup_page(1, 1, on_scalar)
         quantize_page(1, 1)
-        w3_middle = sbuf("w3_middle", [P, PASSES * CHUNK_VALUES], BF16, tag=grouped_tag[0, 0])
-        for a in range(PASSES):
-            stage_w3(pass_part(w3_middle, a), 1, a, nc.vector.tensor_copy)
-        quantize_w3(1, [w3_middle[:]], None)
-        w3_last = [sbuf("w3_last0", [P, CHUNK_VALUES], BF16, tag="turned1_1")]
-        stage_w3(w3_last[0][:], 2, 0, nc.scalar.copy)
+        for c in range(W3_CHUNKS):
+            stage_w3(pass_part(w3_third, c), c, 1, nc.vector.tensor_copy)
+        quantize_w3(w3_second, 0, 2 * CHUNK)
+        quantize_w3(w3_third[:, : 2 * CHUNK_VALUES], 1, 0)
+        quantize_w3(w3_third[:, 2 * CHUNK_VALUES :], 1, 2 * CHUNK)
         scale_rows = out_3.bitcast(I32)
-        for q in range(4):
+        for r in range(4):
             nc.sync.dma_start(
-                out=scale_rows[:, 4 * q : 4 * q + 4, :].rearrange("g r m -> r g m"),
-                in_=page_plane[32 * q : 32 * q + 4].bitcast(I32),
+                out=scale_rows[:, r:16:4, :].rearrange("g q m -> q g m"), in_=page_plane[r:P:32].bitcast(I32)
             )
 
         rest = [sbuf(f"rest{i}", [P, BANK], F32, tag=f"w1_raw{i}_0") for i in range(RESTS)]
-        rest_once = sbuf("rest_once", [P, BANK], F32)
         step = [sbuf(f"step{i}", [P, BANK], F32, tag=f"recent{i}") for i in range(STEPS)]
         for i in range(len(pieces)):
             for one_pass in (fresh_pass, gate_pass):
-                for g in range(PASSES):
+                for g in range(1 if i < AHEAD else 0, PASSES):
                     one_pass(i, g)
             blend_begin(i)
-            if i == W3_LAST_AT:
-                w3_last.append(sbuf("w3_last1", [P, CHUNK_VALUES], BF16, tag="rest_once"))
-                stage_w3(w3_last[1][:], 2, 1, nc.scalar.copy)
-                quantize_w3(2, [t[:] for t in w3_last], grouped_tag[1, 1])
             if i >= END_LAG:
                 blend_end(i - END_LAG)
         for i in range(len(pieces) - END_LAG, len(pieces)):

@@ -32,6 +32,7 @@ W3_CHUNKS = N // CHUNK
 CHUNK_VALUES = CHUNK * PACK
 FIRST_TABLE_LOADS = 4
 AHEAD = 2
+WHOLE_ROWS = 4
 RESTS = 4
 STEPS = 5
 END_LAG = 2
@@ -69,18 +70,17 @@ def tile_list_shelf_suggester_kernel(
         old = [sbuf(f"old{c}", [P, CHUNK // P, T2], F32) for c in range(W3_CHUNKS - 1)]
         w1_staged = [sbuf(f"w1_staged{i}", [P, PASSES * CHUNK_VALUES], BF16) for i in range(2)]
         w1_plane = [sbuf(f"w1_plane{c}", [P, PASSES * CHUNK], U8) for c in range(W1_CHUNKS)]
-        w3_codes = sbuf("w3_codes", [P, PASSES, N], U32)
         recent = [sbuf(f"recent{b}", [P, S], F32) for b in range(ROW_TILES)]
         turned = {
             (g, h, s): sbuf(f"turned{g}_{h}_{s}", [P, 2 * K_PASS], BF16)
             for g in range(PASSES) for h in range(HALVES) for s in range(2)
         }
         page_plane = sbuf("page_plane", [P, PASSES, T2], U8)
-        w1_codes, page_codes, taste, grouped = {}, {}, {}, {}
+        w1_codes, w3_staged, w3_codes, page_codes, taste, grouped = {}, {}, {}, {}, {}, {}
 
         taste_tag = {b: f"taste{b}" for b in range(ROW_TILES)}
         taste_tag.update({1: "w1_raw1_1", 2: "w1_raw2_1", 4: "w1_raw3_1", 7: "w3_raw0"})
-        grouped_tag = {(0, 0): "w1_raw0_1", (0, 1): taste_tag[1], (1, 0): taste_tag[2], (1, 1): taste_tag[4]}
+        grouped_tag = dict(zip(sorted(turned), ("w1_raw0_1", "w1_raw1_1", "w1_raw2_1", "w1_raw3_1", "taste0", "taste3", "taste5", "recent5")))
 
         nc.vector.memset(table_scales[:].bitcast(I32), 0)
         nc.vector.memset(w2_plane[:].bitcast(I32), 0)
@@ -159,8 +159,12 @@ def tile_list_shelf_suggester_kernel(
             for a in passes:
                 stage(pass_part(w1_staged[c % 2], a), w1_raw[c][a][:], nc.scalar.copy)
 
-        def stage_w3(dst, c, a, copy):
+        def stage_w3(c, a, dst, copy):
+            w3_staged[c, a] = dst
             stage(dst, w3_raw[a][:, :, c * CHUNK : (c + 1) * CHUNK], copy)
+
+        def stage_w3_on_scalar(c, a, tag):
+            stage_w3(c, a, sbuf(f"w3_staged{c}_{a}", [P, CHUNK_VALUES], BF16, tag=tag)[:], nc.scalar.copy)
 
         def quantize_chunk(codes, plane, parts):
             words = PASSES * CHUNK // len(parts)
@@ -172,9 +176,10 @@ def tile_list_shelf_suggester_kernel(
             w1_codes[c] = sbuf(f"w1_codes{c}", [P, PASSES * CHUNK], U32)
             quantize_chunk(w1_codes[c], w1_plane[c], parts)
 
-        def quantize_w3(staged, a, first):
-            cols = slice(first, first + staged.shape[1] // PACK)
-            nc.vector.quantize_mx(out=w3_codes[:, a, cols].bitcast(FP8X4), scales=w3_plane[:, a, cols], in_=staged[:])
+        def quantize_w3(c, a, tag=None):
+            w3_codes[c, a] = sbuf(f"w3_codes{c}_{a}", [P, CHUNK], U32, tag=tag)
+            plane = w3_plane[:, a, c * CHUNK : (c + 1) * CHUNK]
+            nc.vector.quantize_mx(out=w3_codes[c, a][:].bitcast(FP8X4), scales=plane, in_=w3_staged[c, a])
 
         def chunk_columns(tile, a):
             first = a * CHUNK + tile % 2 * P
@@ -184,7 +189,7 @@ def tile_list_shelf_suggester_kernel(
             nc.vector.tensor_tensor(out=dst[:], in0=bank[:], in1=weights[:], op=MULT)
 
         def recent_product(b):
-            bank = banks[4 + b % 4]
+            bank = banks[(7, 4, 5, 6, 1, 3, 4, 5)[b]]
             g, col = divmod(b * P, K_PASS)
             for a in range(PASSES):
                 nc.tensor.matmul_mx(
@@ -249,24 +254,25 @@ def tile_list_shelf_suggester_kernel(
                     nc.tensor.transpose(homes[j // blocks][:, at : at + P], words[:, col : col + P], identity[:])
             for i, bank in enumerate(homes):
                 width = blocks * 2 * P
-                first = s * BANK + i * width
-                dst = grouped[g, h][:].bitcast(F32)[:, first : first + width].rearrange("p (j m u) -> p j m u", j=blocks, u=2)
+                first = i * width
+                dst = grouped[g, h, s][:].bitcast(F32)[:, first : first + width].rearrange("p (j m u) -> p j m u", j=blocks, u=2)
                 nc.scalar.copy(out=dst, in_=bank[:, :width].rearrange("p (j u m) -> p j m u", j=blocks, u=2))
 
         def regroup_page(g, h, homes):
-            grouped[g, h] = sbuf(f"grouped{g}_{h}", [P, BANK * PACK], BF16, tag=grouped_tag[g, h])
+            for s in range(2):
+                grouped[g, h, s] = sbuf(f"grouped{g}_{h}_{s}", [P, 2 * BANK], BF16, tag=grouped_tag[g, h, s])
             regroup_part(g, h, 0, homes[:1])
             regroup_part(g, h, 1, homes[1:])
 
-        def quantize_page(g, h, tag=None, parts=1):
+        def quantize_page(g, h, tag=None):
             cols = slice(h * BANK, (h + 1) * BANK)
             page_codes[g, h] = sbuf(f"page_codes{g}_{h}", [P, BANK], U32, tag=tag)
-            width = BANK // parts
-            for first in range(0, BANK, width):
+            for s in range(2):
+                first = s * BANK // 2
                 nc.vector.quantize_mx(
-                    out=page_codes[g, h][:, first : first + width].bitcast(FP8X4),
-                    scales=page_plane[:, g, h * BANK + first : h * BANK + first + width],
-                    in_=grouped[g, h][:, PACK * first : PACK * (first + width)],
+                    out=page_codes[g, h][:, first : first + BANK // 2].bitcast(FP8X4),
+                    scales=page_plane[:, g, h * BANK + first : h * BANK + first + BANK // 2],
+                    in_=grouped[g, h, s][:],
                 )
             words = out_2[g].rearrange("p m t -> p (m t)").bitcast(I32)
             nc.sync.dma_start(out=words[:, cols], in_=page_codes[g, h][:].bitcast(I32))
@@ -275,17 +281,17 @@ def tile_list_shelf_suggester_kernel(
         pieces.extend((n, h) for n in range(2, N // P) for h in (1, 0))
 
         def gate_bank(i):
-            return gate_ring[i % 3]
+            return banks[(0, 1, 5)[i % 3]]
 
         def fresh_bank(i):
-            return fresh_ring[i % STEPS]
+            return banks[(2, 3, 6, 7, 4)[i % STEPS]]
 
         def gate_pass(i, g):
             n, h = pieces[i]
             cols = slice(n * P, (n + 1) * P)
             nc.tensor.matmul_mx(
                 out=gate_bank(i)[:],
-                lhsT=w3_codes[:, g, cols].bitcast(FP8X4), lhsT_scale=w3_plane[:, g, cols],
+                lhsT=w3_codes[n // 2, g][:, n % 2 * P : (n % 2 + 1) * P].bitcast(FP8X4), lhsT_scale=w3_plane[:, g, cols],
                 rhs=page_codes[g, h][:].bitcast(FP8X4), rhs_scale=page_plane[:, g, h * BANK : (h + 1) * BANK],
                 start=(g == 0), stop=(g == PASSES - 1),
             )
@@ -300,6 +306,12 @@ def tile_list_shelf_suggester_kernel(
                 start=(g == 0), stop=(g == PASSES - 1),
             )
 
+        def warm_pass(bank):
+            nc.tensor.matmul_mx(
+                out=bank[:], lhsT=w4_codes[:, 0, : 2 * P].bitcast(FP4X4), lhsT_scale=w4_plane[:, 0, :P],
+                rhs=page_codes[0, 0][:].bitcast(FP8X4), rhs_scale=page_plane[:, 0, :BANK], start=True, stop=True,
+            )
+
         def scores(i):
             n, h = pieces[i]
             return old[n // 2][:, n % 2, h * BANK : (h + 1) * BANK]
@@ -307,13 +319,16 @@ def tile_list_shelf_suggester_kernel(
         def blend_begin(i):
             nc.scalar.activation(out=rest[i % RESTS][:], in_=gate_bank(i)[:], func=SIGMOID, scale=-1.0)
             nc.vector.tensor_tensor(out=step[i % STEPS][:], in0=fresh_bank(i)[:], in1=scores(i), op=SUB)
-            engine = nc.vector if i in (0, len(pieces) // 2, len(pieces) - 1) else nc.gpsimd
+            engine = nc.vector if i in (0, 1, 11) else nc.gpsimd
             engine.tensor_tensor(out=step[i % STEPS][:], in0=step[i % STEPS][:], in1=rest[i % RESTS][:], op=MULT)
 
         def blend_end(i):
             n, h = pieces[i]
             nc.vector.tensor_tensor(out=scores(i), in0=fresh_bank(i)[:], in1=step[i % STEPS][:], op=SUB)
-            nc.sync.dma_start(out=out_0[n * P : (n + 1) * P, h * BANK : (h + 1) * BANK], in_=scores(i))
+            if n >= WHOLE_ROWS:
+                nc.sync.dma_start(out=out_0[n * P : (n + 1) * P, h * BANK : (h + 1) * BANK], in_=scores(i))
+            elif (n, 1 - h) in pieces[:i]:
+                nc.sync.dma_start(out=out_0[n * P : (n + 1) * P, :], in_=old[n // 2][:, n % 2, :])
 
         last = ROW_TILES - 1
 
@@ -323,11 +338,16 @@ def tile_list_shelf_suggester_kernel(
         nc.vector.tensor_copy(picked_words[1][:], table_words[1][:].bitcast(U32).indirect(pick_list[:]))
         old.append(sbuf("old2", [P, CHUNK // P, T2], F32, tag="table_words0"))
         load_old(2)
-        w3_first = sbuf("w3_first", [P, PASSES * CHUNK_VALUES], BF16, tag="table_words1")
-        stage_w1(0)
-        quantize_w1(0, [pass_part(w1_staged[0], a) for a in range(PASSES)])
+        w1_codes[0] = sbuf("w1_codes0", [P, PASSES * CHUNK], U32)
+        for a, first, width in ((0, 0, CHUNK), (1, 0, P), (1, P, P)):
+            at = a * CHUNK + first
+            values = w1_staged[0][:, PACK * at : PACK * (at + width)]
+            stage(values, w1_raw[0][a][:, :, first : first + width], nc.scalar.copy)
+            nc.vector.quantize_mx(
+                out=w1_codes[0][:, at : at + width].bitcast(FP8X4), scales=w1_plane[0][:, at : at + width], in_=values
+            )
         taste_product(0, banks[0:1])
-        for b in range(TILES_PER_PASS):
+        for b in (1, 2, 3, 0):
             recent_product(b)
         stage_w1(1)
         taste_product(1, banks[2:3])
@@ -340,7 +360,6 @@ def tile_list_shelf_suggester_kernel(
         taste_product(2, banks[0:4])
         scatter(1)
         quantize_w1(2, [w1_staged[0][:]])
-        w3_second = sbuf("w3_second", [P, CHUNK_VALUES], BF16, tag="w1_staged0")
         taste_product(3, banks[2:4])
         stage_w1(3, (0,))
         turn_page(0, banks[0:2])
@@ -352,50 +371,56 @@ def tile_list_shelf_suggester_kernel(
         taste_product(5, banks[4:6])
         scatter(3)
         turn_page(2, banks[6:8])
-        stage_w3(pass_part(w3_first, 0), 0, 0, nc.scalar.copy)
+        stage_w3_on_scalar(0, 0, "table_words1")
         taste_product(6, banks[6:8])
         scatter(4)
         turn_page(3, banks[4:6])
-        stage_w3(pass_part(w3_first, 1), 1, 0, nc.scalar.copy)
+        stage_w3_on_scalar(1, 0, "w1_staged0")
         regroup_page(0, 0, banks[2:4])
         scatter(5)
         turn_page(4, banks[4:6])
-        stage_w3(w3_second[:], 2, 0, nc.scalar.copy)
+        stage_w3_on_scalar(2, 0, "w1_staged1")
         taste_product(7, banks[6:8] + banks[2:4])
         regroup_page(0, 1, banks[0:2])
         scatter(6)
         quantize_page(0, 0)
         turn_page(5, banks[4:6])
         turn_page(6, banks[6:8])
-        fresh_ring = [banks[i] for i in (2, 3, 6, 7, 4)]
-        gate_ring = [banks[i] for i in (0, 1, 5)]
         for i in range(AHEAD):
+            warm_pass(fresh_bank(i))
             fresh_pass(i, 0)
+        for c in range(W3_CHUNKS - 1):
+            stage_w3_on_scalar(c, 1, f"turned0_1_{c}")
         scatter(7)
 
         w3_plane = sbuf("w3_plane", [P, PASSES, N], U8, tag=taste_tag[last])
-        w3_third = sbuf("w3_third", [P, W3_CHUNKS * CHUNK_VALUES], BF16, tag=f"recent{last}")
-        quantize_w3(w3_first, 0, 0)
+        w3_end = sbuf("w3_end", [P, CHUNK_VALUES], BF16, tag=f"recent{last}")
+        quantize_w3(0, 0)
         turn_half(last, 0, banks[4:6])
         turn_half(last, 1, banks[0:2])
+        for bank in banks[6:8]:
+            warm_pass(bank)
         regroup_page(1, 0, banks[6:8])
-        quantize_page(1, 0, parts=2)
+        quantize_page(1, 0)
         for i in range(AHEAD):
             gate_pass(i, 0)
         regroup_page(1, 1, banks[4:6])
-        quantize_page(0, 1, grouped_tag[1, 0])
         quantize_page(1, 1)
+        quantize_w3(1, 0)
+        stage_w3(W3_CHUNKS - 1, 1, w3_end[:], nc.vector.tensor_copy)
+        quantize_page(0, 1, "table_words1")
         for c in range(W3_CHUNKS):
-            stage_w3(pass_part(w3_third, c), c, 1, nc.vector.tensor_copy)
-        quantize_w3(w3_second, 0, 2 * CHUNK)
-        quantize_w3(w3_third[:, : 2 * CHUNK_VALUES], 1, 0)
-        quantize_w3(w3_third[:, 2 * CHUNK_VALUES :], 1, 2 * CHUNK)
-        scale_rows = out_3.bitcast(I32)
-        for r in range(4):
-            nc.sync.dma_start(
-                out=scale_rows[:, r:16:4, :].rearrange("g q m -> q g m"), in_=page_plane[r:P:32].bitcast(I32)
-            )
+            quantize_w3(c, 1)
+        quantize_w3(2, 0)
 
+        def store_page_scales():
+            scale_rows = out_3.bitcast(I32)
+            for r in range(4):
+                nc.sync.dma_start(
+                    out=scale_rows[:, r:16:4, :].rearrange("g q m -> q g m"), in_=page_plane[r:P:32].bitcast(I32)
+                )
+
+        store_page_scales()
         rest = [sbuf(f"rest{i}", [P, BANK], F32, tag=f"w1_raw{i}_0") for i in range(RESTS)]
         step = [sbuf(f"step{i}", [P, BANK], F32, tag=f"recent{i}") for i in range(STEPS)]
         for i in range(len(pieces)):

@@ -71,16 +71,14 @@ def tile_list_shelf_suggester_kernel(
         w1_staged = [sbuf(f"w1_staged{i}", [P, PASSES * CHUNK_VALUES], BF16) for i in range(2)]
         w1_plane = [sbuf(f"w1_plane{c}", [P, PASSES * CHUNK], U8) for c in range(W1_CHUNKS)]
         recent = [sbuf(f"recent{b}", [P, S], F32) for b in range(ROW_TILES)]
-        turned = {
-            (g, h, s): sbuf(f"turned{g}_{h}_{s}", [P, 2 * K_PASS], BF16)
-            for g in range(PASSES) for h in range(HALVES) for s in range(2)
-        }
+        turned = {(g, h): [sbuf(f"turned{g}_{h}", [P, 4 * K_PASS], BF16)] for g, h in ((0, 0), (0, 1), (1, 1))}
+        turned[1, 0] = [sbuf(f"turned1_0_{s}", [P, 2 * K_PASS], BF16) for s in range(2)]
         page_plane = sbuf("page_plane", [P, PASSES, T2], U8)
         w1_codes, w3_staged, w3_codes, page_codes, taste, grouped = {}, {}, {}, {}, {}, {}
 
         taste_tag = {b: f"taste{b}" for b in range(ROW_TILES)}
         taste_tag.update({1: "w1_raw1_1", 2: "w1_raw2_1", 4: "w1_raw3_1", 7: "w3_raw0"})
-        grouped_tag = dict(zip(sorted(turned), ("w1_raw0_1", "w1_raw1_1", "w1_raw2_1", "w1_raw3_1", "taste0", "taste3", "taste5", "recent5")))
+        grouped_tag = dict(zip(((g, h, s) for g, h in sorted(turned) for s in range(2)), ("w1_raw0_1", "w1_raw1_1", "w1_raw2_1", "w1_raw3_1", "taste0", "taste3", "taste5", "recent5")))
 
         nc.vector.memset(table_scales[:].bitcast(I32), 0)
         nc.vector.memset(w2_plane[:].bitcast(I32), 0)
@@ -234,18 +232,22 @@ def tile_list_shelf_suggester_kernel(
                 col = h * BANK + k * P
                 at = k % blocks * P
                 nc.tensor.transpose(homes[k // blocks][:, at : at + P], page[b][:, col : col + P], identity[:])
-            for s in range(2):
-                at = 2 * s % blocks * P
-                src = homes[2 * s // blocks][:, at : at + 2 * P]
-                dst = turned[g, h, s][:].rearrange("m (j u p e) -> m j u p e", j=2, u=2, e=2)[:, :, :, 32 * q : 32 * (q + 1), :]
-                nc.scalar.copy(out=dst, in_=src.rearrange("m (j p u e) -> m j u p e", j=2, u=2, e=2))
+            tiles = turned[g, h]
+            run = 4 // max(len(homes), len(tiles))
+            for k in range(0, 4, run):
+                at = k % blocks * P
+                src = homes[k // blocks][:, at : at + run * P]
+                tile, first = tiles[k * len(tiles) // 4], k % (4 // len(tiles))
+                dst = tile[:].rearrange("m (j u p e) -> m j u p e", u=2, p=P, e=2)[:, first : first + run, :, 32 * q : 32 * (q + 1), :]
+                nc.scalar.copy(out=dst, in_=src.rearrange("m (j p u e) -> m j u p e", j=run, u=2, e=2))
 
         def turn_page(b, two_banks):
             for h in range(HALVES):
                 turn_half(b, h, two_banks[h : h + 1])
 
         def regroup_part(g, h, s, homes):
-            words = turned[g, h, s][:].bitcast(F32)
+            tiles = turned[g, h]
+            words = tiles[s][:].bitcast(F32) if len(tiles) == 2 else tiles[0][:].bitcast(F32)[:, s * BANK : (s + 1) * BANK]
             blocks = 2 // len(homes)
             for j in range(2):
                 for u in range(2):
@@ -264,9 +266,11 @@ def tile_list_shelf_suggester_kernel(
             regroup_part(g, h, 0, homes[:1])
             regroup_part(g, h, 1, homes[1:])
 
+        last_words = sbuf("last_words", [P, T2], U32)
+
         def quantize_page(g, h, tag=None):
             cols = slice(h * BANK, (h + 1) * BANK)
-            page_codes[g, h] = sbuf(f"page_codes{g}_{h}", [P, BANK], U32, tag=tag)
+            page_codes[g, h] = last_words[:, cols] if g else sbuf(f"page_codes{g}_{h}", [P, BANK], U32, tag=tag)
             for s in range(2):
                 first = s * BANK // 2
                 nc.vector.quantize_mx(
@@ -275,7 +279,10 @@ def tile_list_shelf_suggester_kernel(
                     in_=grouped[g, h, s][:],
                 )
             words = out_2[g].rearrange("p m t -> p (m t)").bitcast(I32)
-            nc.sync.dma_start(out=words[:, cols], in_=page_codes[g, h][:].bitcast(I32))
+            if g == 0:
+                nc.sync.dma_start(out=words[:, cols], in_=page_codes[g, h][:].bitcast(I32))
+            elif h == HALVES - 1:
+                nc.sync.dma_start(out=words, in_=last_words[:].bitcast(I32))
 
         pieces = [(0, 0), (1, 0), (0, 1), (1, 1)]
         pieces.extend((n, h) for n in range(2, N // P) for h in (1, 0))
@@ -389,8 +396,9 @@ def tile_list_shelf_suggester_kernel(
         for i in range(AHEAD):
             warm_pass(fresh_bank(i))
             fresh_pass(i, 0)
+        w3_late = sbuf("w3_late", [P, 2 * CHUNK_VALUES], BF16, tag="turned0_1")
         for c in range(W3_CHUNKS - 1):
-            stage_w3_on_scalar(c, 1, f"turned0_1_{c}")
+            stage_w3(c, 1, pass_part(w3_late, c), nc.scalar.copy)
         scatter(7)
 
         w3_plane = sbuf("w3_plane", [P, PASSES, N], U8, tag=taste_tag[last])

@@ -26,6 +26,7 @@ BANK = 512
 ROW_TILES = H // P
 TILES_PER_PASS = K_PASS // P
 HALVES = T2 // BANK
+QUARTER = BANK // 2
 CHUNK = 256
 W1_CHUNKS = H // CHUNK
 W3_CHUNKS = N // CHUNK
@@ -74,11 +75,12 @@ def tile_list_shelf_suggester_kernel(
         turned = {(g, h): [sbuf(f"turned{g}_{h}", [P, 4 * K_PASS], BF16)] for g, h in ((0, 0), (0, 1), (1, 1))}
         turned[1, 0] = [sbuf(f"turned1_0_{s}", [P, 2 * K_PASS], BF16) for s in range(2)]
         page_plane = sbuf("page_plane", [P, PASSES, T2], U8)
-        w1_codes, w3_staged, w3_codes, page_codes, taste, grouped = {}, {}, {}, {}, {}, {}
+        w3_codes = sbuf("w3_codes", [P, PASSES, N], U32)
+        w1_codes, page_codes, taste, grouped = {}, {}, {}, {}
 
         taste_tag = {b: f"taste{b}" for b in range(ROW_TILES)}
         taste_tag.update({1: "w1_raw1_1", 2: "w1_raw2_1", 4: "w1_raw3_1", 7: "w3_raw0"})
-        grouped_tag = dict(zip(((g, h, s) for g, h in sorted(turned) for s in range(2)), ("w1_raw0_1", "w1_raw1_1", "w1_raw2_1", "w1_raw3_1", "taste0", "taste3", "taste5", "recent5")))
+        grouped_tag = dict(zip(((g, h, s) for g, h in sorted(turned) for s in range(2)), ("w1_raw0_1", "", "w1_raw2_1", "", "taste0", "taste3", "taste5", "recent5")))
 
         nc.vector.memset(table_scales[:].bitcast(I32), 0)
         nc.vector.memset(w2_plane[:].bitcast(I32), 0)
@@ -127,8 +129,8 @@ def tile_list_shelf_suggester_kernel(
         load_plane(w2_plane, w2_scales)
         load_table_words(1, 1)
         nc.sync.dma_start(out=weights[:], in_=wgs)
-        load_w1(0, 0)
         load_w2(1)
+        load_w1(0, 0)
         load_w1(0, 1)
         nc.sync.dma_start(put_list[:], offs2)
         load_page(0)
@@ -158,11 +160,7 @@ def tile_list_shelf_suggester_kernel(
                 stage(pass_part(w1_staged[c % 2], a), w1_raw[c][a][:], nc.scalar.copy)
 
         def stage_w3(c, a, dst, copy):
-            w3_staged[c, a] = dst
             stage(dst, w3_raw[a][:, :, c * CHUNK : (c + 1) * CHUNK], copy)
-
-        def stage_w3_on_scalar(c, a, tag):
-            stage_w3(c, a, sbuf(f"w3_staged{c}_{a}", [P, CHUNK_VALUES], BF16, tag=tag)[:], nc.scalar.copy)
 
         def quantize_chunk(codes, plane, parts):
             words = PASSES * CHUNK // len(parts)
@@ -174,10 +172,9 @@ def tile_list_shelf_suggester_kernel(
             w1_codes[c] = sbuf(f"w1_codes{c}", [P, PASSES * CHUNK], U32)
             quantize_chunk(w1_codes[c], w1_plane[c], parts)
 
-        def quantize_w3(c, a, tag=None):
-            w3_codes[c, a] = sbuf(f"w3_codes{c}_{a}", [P, CHUNK], U32, tag=tag)
-            plane = w3_plane[:, a, c * CHUNK : (c + 1) * CHUNK]
-            nc.vector.quantize_mx(out=w3_codes[c, a][:].bitcast(FP8X4), scales=plane, in_=w3_staged[c, a])
+        def quantize_w3(a, first, values):
+            cols = slice(first * CHUNK, first * CHUNK + values.shape[1] // PACK)
+            nc.vector.quantize_mx(out=w3_codes[:, a, cols].bitcast(FP8X4), scales=w3_plane[:, a, cols], in_=values)
 
         def chunk_columns(tile, a):
             first = a * CHUNK + tile % 2 * P
@@ -186,21 +183,21 @@ def tile_list_shelf_suggester_kernel(
         def weigh(dst, bank):
             nc.vector.tensor_tensor(out=dst[:], in0=bank[:], in1=weights[:], op=MULT)
 
-        def recent_product(b):
-            bank = banks[(7, 4, 5, 6, 1, 3, 4, 5)[b]]
+        def recent_product(b, bank, picks=slice(0, S)):
             g, col = divmod(b * P, K_PASS)
+            sums = bank[:, : picks.stop - picks.start]
             for a in range(PASSES):
                 nc.tensor.matmul_mx(
-                    out=bank[:],
+                    out=sums,
                     lhsT=w2_codes[g][:, a, 2 * col : 2 * (col + P)].bitcast(FP4X4),
                     lhsT_scale=w2_plane[:, a, b * P : (b + 1) * P],
-                    rhs=picked_words[a][:].bitcast(FP8X4), rhs_scale=picked_scales[a][:],
+                    rhs=picked_words[a][:, picks].bitcast(FP8X4), rhs_scale=picked_scales[a][:, picks],
                     start=(a == 0), stop=(a == PASSES - 1),
                 )
             if b == 0:
-                nc.scalar.copy(out=recent[b][:], in_=bank[:])
+                nc.scalar.copy(out=recent[b][:], in_=sums)
             else:
-                weigh(recent[b], bank)
+                nc.vector.tensor_tensor(out=recent[b][:, picks], in0=sums, in1=weights[:, picks], op=MULT)
 
         def taste_product(b, homes):
             taste[b] = sbuf(f"taste{b}", [P, S], F32, tag=taste_tag[b])
@@ -257,12 +254,18 @@ def tile_list_shelf_suggester_kernel(
             for i, bank in enumerate(homes):
                 width = blocks * 2 * P
                 first = i * width
-                dst = grouped[g, h, s][:].bitcast(F32)[:, first : first + width].rearrange("p (j m u) -> p j m u", j=blocks, u=2)
+                dst = grouped[g, h, s].bitcast(F32)[:, first : first + width].rearrange("p (j m u) -> p j m u", j=blocks, u=2)
                 nc.scalar.copy(out=dst, in_=bank[:, :width].rearrange("p (j u m) -> p j m u", j=blocks, u=2))
 
         def regroup_page(g, h, homes):
+            if g == 0:
+                both = sbuf(f"grouped{g}_{h}", [P, 4 * BANK], BF16, tag=grouped_tag[g, h, 0])
+                grouped[g, h] = both[:]
             for s in range(2):
-                grouped[g, h, s] = sbuf(f"grouped{g}_{h}_{s}", [P, 2 * BANK], BF16, tag=grouped_tag[g, h, s])
+                if g == 0:
+                    grouped[g, h, s] = both[:, s * 2 * BANK : (s + 1) * 2 * BANK]
+                else:
+                    grouped[g, h, s] = sbuf(f"grouped{g}_{h}_{s}", [P, 2 * BANK], BF16, tag=grouped_tag[g, h, s])[:]
             regroup_part(g, h, 0, homes[:1])
             regroup_part(g, h, 1, homes[1:])
 
@@ -271,12 +274,14 @@ def tile_list_shelf_suggester_kernel(
         def quantize_page(g, h, tag=None):
             cols = slice(h * BANK, (h + 1) * BANK)
             page_codes[g, h] = last_words[:, cols] if g else sbuf(f"page_codes{g}_{h}", [P, BANK], U32, tag=tag)
-            for s in range(2):
-                first = s * BANK // 2
+            parts = [grouped[g, h, s] for s in range(2)] if g else [grouped[g, h]]
+            width = BANK // len(parts)
+            for s, part in enumerate(parts):
+                first = s * width
                 nc.vector.quantize_mx(
-                    out=page_codes[g, h][:, first : first + BANK // 2].bitcast(FP8X4),
-                    scales=page_plane[:, g, h * BANK + first : h * BANK + first + BANK // 2],
-                    in_=grouped[g, h, s][:],
+                    out=page_codes[g, h][:, first : first + width].bitcast(FP8X4),
+                    scales=page_plane[:, g, h * BANK + first : h * BANK + first + width],
+                    in_=part,
                 )
             words = out_2[g].rearrange("p m t -> p (m t)").bitcast(I32)
             if g == 0:
@@ -284,8 +289,8 @@ def tile_list_shelf_suggester_kernel(
             elif h == HALVES - 1:
                 nc.sync.dma_start(out=words, in_=last_words[:].bitcast(I32))
 
-        pieces = [(0, 0), (1, 0), (0, 1), (1, 1)]
-        pieces.extend((n, h) for n in range(2, N // P) for h in (1, 0))
+        pieces = [(0, 2, q * QUARTER, QUARTER) for q in range(T2 // QUARTER)]
+        pieces.extend((n, 1, h * BANK, BANK) for n in range(2, N // P) for h in (1, 0))
 
         def gate_bank(i):
             return banks[(0, 1, 5)[i % 3]]
@@ -293,25 +298,22 @@ def tile_list_shelf_suggester_kernel(
         def fresh_bank(i):
             return banks[(2, 3, 6, 7, 4)[i % STEPS]]
 
+        def piece_pass(i, g, bank, stationary):
+            first, tiles, col, width = pieces[i]
+            h, at = divmod(col, BANK)
+            for k in range(tiles):
+                codes, plane = stationary(first + k)
+                nc.tensor.matmul_mx(
+                    out=bank[:, k * width : (k + 1) * width], lhsT=codes, lhsT_scale=plane,
+                    rhs=page_codes[g, h][:, at : at + width].bitcast(FP8X4), rhs_scale=page_plane[:, g, col : col + width],
+                    start=(g == 0 and k == 0), stop=(g == PASSES - 1 and k == tiles - 1),
+                )
+
         def gate_pass(i, g):
-            n, h = pieces[i]
-            cols = slice(n * P, (n + 1) * P)
-            nc.tensor.matmul_mx(
-                out=gate_bank(i)[:],
-                lhsT=w3_codes[n // 2, g][:, n % 2 * P : (n % 2 + 1) * P].bitcast(FP8X4), lhsT_scale=w3_plane[:, g, cols],
-                rhs=page_codes[g, h][:].bitcast(FP8X4), rhs_scale=page_plane[:, g, h * BANK : (h + 1) * BANK],
-                start=(g == 0), stop=(g == PASSES - 1),
-            )
+            piece_pass(i, g, gate_bank(i), lambda n: (w3_codes[:, g, n * P : (n + 1) * P].bitcast(FP8X4), w3_plane[:, g, n * P : (n + 1) * P]))
 
         def fresh_pass(i, g):
-            n, h = pieces[i]
-            nc.tensor.matmul_mx(
-                out=fresh_bank(i)[:],
-                lhsT=w4_codes[:, g, 2 * n * P : 2 * (n + 1) * P].bitcast(FP4X4),
-                lhsT_scale=w4_plane[:, g, n * P : (n + 1) * P],
-                rhs=page_codes[g, h][:].bitcast(FP8X4), rhs_scale=page_plane[:, g, h * BANK : (h + 1) * BANK],
-                start=(g == 0), stop=(g == PASSES - 1),
-            )
+            piece_pass(i, g, fresh_bank(i), lambda n: (w4_codes[:, g, 2 * n * P : 2 * (n + 1) * P].bitcast(FP4X4), w4_plane[:, g, n * P : (n + 1) * P]))
 
         def warm_pass(bank):
             nc.tensor.matmul_mx(
@@ -320,31 +322,42 @@ def tile_list_shelf_suggester_kernel(
             )
 
         def scores(i):
-            n, h = pieces[i]
-            return old[n // 2][:, n % 2, h * BANK : (h + 1) * BANK]
+            first, tiles, col, width = pieces[i]
+            return old[first // 2][:, first % 2 : first % 2 + tiles, col : col + width]
+
+        def by_tiles(i, tile):
+            return tile[:].rearrange("p (k m) -> p k m", k=pieces[i][1])
 
         def blend_begin(i):
             nc.scalar.activation(out=rest[i % RESTS][:], in_=gate_bank(i)[:], func=SIGMOID, scale=-1.0)
-            nc.vector.tensor_tensor(out=step[i % STEPS][:], in0=fresh_bank(i)[:], in1=scores(i), op=SUB)
-            engine = nc.vector if i in (0, 1, 11) else nc.gpsimd
+            nc.vector.tensor_tensor(out=by_tiles(i, step[i % STEPS]), in0=by_tiles(i, fresh_bank(i)), in1=scores(i), op=SUB)
+            engine = nc.vector if i in (0, 10) else nc.gpsimd
             engine.tensor_tensor(out=step[i % STEPS][:], in0=step[i % STEPS][:], in1=rest[i % RESTS][:], op=MULT)
 
         def blend_end(i):
-            n, h = pieces[i]
-            nc.vector.tensor_tensor(out=scores(i), in0=fresh_bank(i)[:], in1=step[i % STEPS][:], op=SUB)
-            if n >= WHOLE_ROWS:
-                nc.sync.dma_start(out=out_0[n * P : (n + 1) * P, h * BANK : (h + 1) * BANK], in_=scores(i))
-            elif (n, 1 - h) in pieces[:i]:
-                nc.sync.dma_start(out=out_0[n * P : (n + 1) * P, :], in_=old[n // 2][:, n % 2, :])
+            first, tiles, col, width = pieces[i]
+            nc.vector.tensor_tensor(out=scores(i), in0=by_tiles(i, fresh_bank(i)), in1=by_tiles(i, step[i % STEPS]), op=SUB)
+            if first >= WHOLE_ROWS:
+                nc.sync.dma_start(out=out_0[first * P : (first + 1) * P, col : col + width], in_=old[first // 2][:, first % 2, col : col + width])
+            elif i + 1 == len(pieces) or pieces[i + 1][0] != first:
+                for n in range(first, first + tiles):
+                    nc.sync.dma_start(out=out_0[n * P : (n + 1) * P, :], in_=old[n // 2][:, n % 2, :])
 
         last = ROW_TILES - 1
 
         nc.vector.tensor_copy(picked_words[0][:], table_words[0][:].bitcast(U32).indirect(pick_list[:]))
         for a in range(PASSES):
             nc.vector.tensor_copy(picked_scales[a][:], table_scales[:, a, :].indirect(pick_list[:]))
-        nc.vector.tensor_copy(picked_words[1][:], table_words[1][:].bitcast(U32).indirect(pick_list[:]))
+        for half in range(2):
+            picks = slice(half * S // 2, (half + 1) * S // 2)
+            offsets = pick_list[:, half * S // 32 : (half + 1) * S // 32]
+            nc.vector.tensor_copy(picked_words[1][:, picks], table_words[1][:].bitcast(U32).indirect(offsets))
         old.append(sbuf("old2", [P, CHUNK // P, T2], F32, tag="table_words0"))
         load_old(2)
+        for half in range(2):
+            for b in (1, 2, 3):
+                recent_product(b, banks[b + 3 * (1 - half)], slice(half * S // 2, (half + 1) * S // 2))
+        recent_product(0, banks[7])
         w1_codes[0] = sbuf("w1_codes0", [P, PASSES * CHUNK], U32)
         for a, first, width in ((0, 0, CHUNK), (1, 0, P), (1, P, P)):
             at = a * CHUNK + first
@@ -354,13 +367,11 @@ def tile_list_shelf_suggester_kernel(
                 out=w1_codes[0][:, at : at + width].bitcast(FP8X4), scales=w1_plane[0][:, at : at + width], in_=values
             )
         taste_product(0, banks[0:1])
-        for b in (1, 2, 3, 0):
-            recent_product(b)
+        for b, bank in zip(range(TILES_PER_PASS, ROW_TILES), (4, 5, 6, 1)):
+            recent_product(b, banks[bank])
         stage_w1(1)
         taste_product(1, banks[2:3])
         scatter(0)
-        for b in range(TILES_PER_PASS, ROW_TILES):
-            recent_product(b)
 
         quantize_w1(1, [w1_staged[1][:]])
         stage_w1(2)
@@ -378,15 +389,16 @@ def tile_list_shelf_suggester_kernel(
         taste_product(5, banks[4:6])
         scatter(3)
         turn_page(2, banks[6:8])
-        stage_w3_on_scalar(0, 0, "table_words1")
+        w3_early = sbuf("w3_early", [P, W3_CHUNKS * CHUNK_VALUES], BF16, tag="table_words1")
+        stage_w3(0, 0, pass_part(w3_early, 0), nc.scalar.copy)
         taste_product(6, banks[6:8])
         scatter(4)
         turn_page(3, banks[4:6])
-        stage_w3_on_scalar(1, 0, "w1_staged0")
+        stage_w3(1, 0, pass_part(w3_early, 1), nc.scalar.copy)
         regroup_page(0, 0, banks[2:4])
         scatter(5)
         turn_page(4, banks[4:6])
-        stage_w3_on_scalar(2, 0, "w1_staged1")
+        stage_w3(2, 0, pass_part(w3_early, 2), nc.scalar.copy)
         taste_product(7, banks[6:8] + banks[2:4])
         regroup_page(0, 1, banks[0:2])
         scatter(6)
@@ -403,7 +415,7 @@ def tile_list_shelf_suggester_kernel(
 
         w3_plane = sbuf("w3_plane", [P, PASSES, N], U8, tag=taste_tag[last])
         w3_end = sbuf("w3_end", [P, CHUNK_VALUES], BF16, tag=f"recent{last}")
-        quantize_w3(0, 0)
+        quantize_w3(0, 0, w3_early[:, :CHUNK_VALUES])
         turn_half(last, 0, banks[4:6])
         turn_half(last, 1, banks[0:2])
         for bank in banks[6:8]:
@@ -414,12 +426,11 @@ def tile_list_shelf_suggester_kernel(
             gate_pass(i, 0)
         regroup_page(1, 1, banks[4:6])
         quantize_page(1, 1)
-        quantize_w3(1, 0)
+        quantize_w3(0, 1, w3_early[:, CHUNK_VALUES:])
         stage_w3(W3_CHUNKS - 1, 1, w3_end[:], nc.vector.tensor_copy)
         quantize_page(0, 1, "table_words1")
-        for c in range(W3_CHUNKS):
-            quantize_w3(c, 1)
-        quantize_w3(2, 0)
+        quantize_w3(1, 0, w3_late[:])
+        quantize_w3(1, W3_CHUNKS - 1, w3_end[:])
 
         def store_page_scales():
             scale_rows = out_3.bitcast(I32)

@@ -33,6 +33,7 @@ W3_CHUNKS = N // CHUNK
 CHUNK_VALUES = CHUNK * PACK
 FIRST_TABLE_LOADS = 4
 AHEAD = 2
+ON_GPSIMD = 3
 WHOLE_ROWS = 4
 RESTS = 4
 STEPS = 5
@@ -71,16 +72,15 @@ def tile_list_shelf_suggester_kernel(
         old = [sbuf(f"old{c}", [P, CHUNK // P, T2], F32) for c in range(W3_CHUNKS - 1)]
         w1_staged = [sbuf(f"w1_staged{i}", [P, PASSES * CHUNK_VALUES], BF16) for i in range(2)]
         w1_plane = [sbuf(f"w1_plane{c}", [P, PASSES * CHUNK], U8) for c in range(W1_CHUNKS)]
-        recent = [sbuf(f"recent{b}", [P, S], F32) for b in range(ROW_TILES)]
-        turned = {(g, h): [sbuf(f"turned{g}_{h}", [P, 4 * K_PASS], BF16)] for g, h in ((0, 0), (0, 1), (1, 1))}
-        turned[1, 0] = [sbuf(f"turned1_0_{s}", [P, 2 * K_PASS], BF16) for s in range(2)]
+        recent = {b: sbuf(f"recent{b}", [P, S], F32) for b in range(1, ROW_TILES)}
+        turned = {(g, h): [sbuf(f"turned{g}_{h}", [P, 4 * K_PASS], BF16)] for g in range(PASSES) for h in range(HALVES)}
         page_plane = sbuf("page_plane", [P, PASSES, T2], U8)
         w3_codes = sbuf("w3_codes", [P, PASSES, N], U32)
-        w1_codes, page_codes, taste, grouped = {}, {}, {}, {}
+        w1_codes, second_pass, page_codes, taste, grouped = {}, {}, {}, {}, {}
 
         taste_tag = {b: f"taste{b}" for b in range(ROW_TILES)}
         taste_tag.update({1: "w1_raw1_1", 2: "w1_raw2_1", 4: "w1_raw3_1", 7: "w3_raw0"})
-        grouped_tag = dict(zip(((g, h, s) for g, h in sorted(turned) for s in range(2)), ("w1_raw0_1", "", "w1_raw2_1", "", "taste0", "taste3", "taste5", "recent5")))
+        grouped_tag = dict(zip(((g, h, s) for g, h in sorted(turned) for s in range(2)), ("w1_raw0_1", "", "w1_raw2_1", "", "taste0", "taste3", "taste5", "recent6")))
 
         nc.vector.memset(table_scales[:].bitcast(I32), 0)
         nc.vector.memset(w2_plane[:].bitcast(I32), 0)
@@ -194,9 +194,9 @@ def tile_list_shelf_suggester_kernel(
                     rhs=picked_words[a][:, picks].bitcast(FP8X4), rhs_scale=picked_scales[a][:, picks],
                     start=(a == 0), stop=(a == PASSES - 1),
                 )
-            if b == 0:
-                nc.scalar.copy(out=recent[b][:], in_=sums)
-            else:
+            if b == ON_GPSIMD:
+                nc.scalar.copy(out=recent[b][:, picks], in_=sums)
+            elif b:
                 nc.vector.tensor_tensor(out=recent[b][:, picks], in0=sums, in1=weights[:, picks], op=MULT)
 
         def taste_product(b, homes):
@@ -209,7 +209,7 @@ def tile_list_shelf_suggester_kernel(
                     cols = chunk_columns(b, a)
                     nc.tensor.matmul_mx(
                         out=sums,
-                        lhsT=w1_codes[b // 2][:, cols].bitcast(FP8X4), lhsT_scale=w1_plane[b // 2][:, cols],
+                        lhsT=(second_pass[b][:] if a and b in second_pass else w1_codes[b // 2][:, cols]).bitcast(FP8X4), lhsT_scale=w1_plane[b // 2][:, cols],
                         rhs=picked_words[a][:, picks].bitcast(FP8X4), rhs_scale=picked_scales[a][:, picks],
                         start=(a == 0), stop=(a == PASSES - 1),
                     )
@@ -357,17 +357,32 @@ def tile_list_shelf_suggester_kernel(
         for half in range(2):
             for b in (1, 2, 3):
                 recent_product(b, banks[b + 3 * (1 - half)], slice(half * S // 2, (half + 1) * S // 2))
+        nc.gpsimd.tensor_tensor(out=recent[ON_GPSIMD][:], in0=recent[ON_GPSIMD][:], in1=weights[:], op=MULT)
+        recent_product(4, banks[0])
+        recent_product(5, banks[4])
         recent_product(0, banks[7])
-        w1_codes[0] = sbuf("w1_codes0", [P, PASSES * CHUNK], U32)
-        for a, first, width in ((0, 0, CHUNK), (1, 0, P), (1, P, P)):
+        def first_values(a, first, width):
             at = a * CHUNK + first
-            values = w1_staged[0][:, PACK * at : PACK * (at + width)]
-            stage(values, w1_raw[0][a][:, :, first : first + width], nc.scalar.copy)
-            nc.vector.quantize_mx(
-                out=w1_codes[0][:, at : at + width].bitcast(FP8X4), scales=w1_plane[0][:, at : at + width], in_=values
-            )
+            return w1_staged[0][:, PACK * at : PACK * (at + width)]
+
+        def quantize_first(a, first, width, codes):
+            at = a * CHUNK + first
+            nc.vector.quantize_mx(out=codes[:].bitcast(FP8X4), scales=w1_plane[0][:, at : at + width], in_=first_values(a, first, width))
+
+        w1_codes[0] = sbuf("w1_codes0", [P, CHUNK], U32)
+        stage(first_values(0, 0, CHUNK), w1_raw[0][0][:], nc.scalar.copy)
+        quantize_first(0, 0, CHUNK, w1_codes[0])
+        for b in range(2):
+            stage(first_values(1, b * P, P), w1_raw[0][1][:, :, b * P : (b + 1) * P], nc.scalar.copy)
+            if b == 0:
+                recent[0] = sbuf("recent0", [P, S], F32, tag="w1_raw0_0")
+                nc.scalar.copy(out=recent[0][:], in_=banks[7][:])
+        second_pass[0] = sbuf("second_pass0", [P, P], U32, tag="second_pass")
+        quantize_first(1, 0, P, second_pass[0])
         taste_product(0, banks[0:1])
-        for b, bank in zip(range(TILES_PER_PASS, ROW_TILES), (4, 5, 6, 1)):
+        second_pass[1] = sbuf("second_pass1", [P, P], U32, tag="second_pass")
+        quantize_first(1, P, P, second_pass[1])
+        for b, bank in ((6, 5), (7, 1)):
             recent_product(b, banks[bank])
         stage_w1(1)
         taste_product(1, banks[2:3])
@@ -441,7 +456,7 @@ def tile_list_shelf_suggester_kernel(
 
         store_page_scales()
         rest = [sbuf(f"rest{i}", [P, BANK], F32, tag=f"w1_raw{i}_0") for i in range(RESTS)]
-        step = [sbuf(f"step{i}", [P, BANK], F32, tag=f"recent{i}") for i in range(STEPS)]
+        step = [sbuf(f"step{i}", [P, BANK], F32, tag=f"recent{i + 1}") for i in range(STEPS)]
         for i in range(len(pieces)):
             for one_pass in (fresh_pass, gate_pass):
                 for g in range(1 if i < AHEAD else 0, PASSES):

@@ -34,6 +34,7 @@ CHUNK_VALUES = CHUNK * PACK
 FIRST_TABLE_LOADS = 4
 AHEAD = 2
 ON_GPSIMD = 3
+LATE_ON_SCALAR = 384
 WHOLE_ROWS = 4
 RESTS = 4
 STEPS = 5
@@ -173,7 +174,7 @@ def tile_list_shelf_suggester_kernel(
             quantize_chunk(w1_codes[c], w1_plane[c], parts)
 
         def quantize_w3(a, first, values):
-            cols = slice(first * CHUNK, first * CHUNK + values.shape[1] // PACK)
+            cols = slice(first, first + values.shape[1] // PACK)
             nc.vector.quantize_mx(out=w3_codes[:, a, cols].bitcast(FP8X4), scales=w3_plane[:, a, cols], in_=values)
 
         def chunk_columns(tile, a):
@@ -328,18 +329,27 @@ def tile_list_shelf_suggester_kernel(
         def by_tiles(i, tile):
             return tile[:].rearrange("p (k m) -> p k m", k=pieces[i][1])
 
+        def parts(i):
+            cuts = (0, QUARTER, BANK) if i == len(pieces) - 1 else (0, BANK)
+            return [slice(a, b) for a, b in zip(cuts, cuts[1:])]
+
         def blend_begin(i):
             nc.scalar.activation(out=rest[i % RESTS][:], in_=gate_bank(i)[:], func=SIGMOID, scale=-1.0)
             nc.vector.tensor_tensor(out=by_tiles(i, step[i % STEPS]), in0=by_tiles(i, fresh_bank(i)), in1=scores(i), op=SUB)
             engine = nc.vector if i in (0, 10) else nc.gpsimd
-            engine.tensor_tensor(out=step[i % STEPS][:], in0=step[i % STEPS][:], in1=rest[i % RESTS][:], op=MULT)
+            for cols in parts(i):
+                engine.tensor_tensor(out=step[i % STEPS][:, cols], in0=step[i % STEPS][:, cols], in1=rest[i % RESTS][:, cols], op=MULT)
 
         def blend_end(i):
             first, tiles, col, width = pieces[i]
-            nc.vector.tensor_tensor(out=scores(i), in0=by_tiles(i, fresh_bank(i)), in1=by_tiles(i, step[i % STEPS]), op=SUB)
             if first >= WHOLE_ROWS:
-                nc.sync.dma_start(out=out_0[first * P : (first + 1) * P, col : col + width], in_=old[first // 2][:, first % 2, col : col + width])
-            elif i + 1 == len(pieces) or pieces[i + 1][0] != first:
+                for cols in parts(i):
+                    new = old[first // 2][:, first % 2, col + cols.start : col + cols.stop]
+                    nc.vector.tensor_tensor(out=new, in0=fresh_bank(i)[:, cols], in1=step[i % STEPS][:, cols], op=SUB)
+                    nc.sync.dma_start(out=out_0[first * P : (first + 1) * P, col + cols.start : col + cols.stop], in_=new)
+                return
+            nc.vector.tensor_tensor(out=scores(i), in0=by_tiles(i, fresh_bank(i)), in1=by_tiles(i, step[i % STEPS]), op=SUB)
+            if i + 1 == len(pieces) or pieces[i + 1][0] != first:
                 for n in range(first, first + tiles):
                     nc.sync.dma_start(out=out_0[n * P : (n + 1) * P, :], in_=old[n // 2][:, n % 2, :])
 
@@ -423,13 +433,12 @@ def tile_list_shelf_suggester_kernel(
         for i in range(AHEAD):
             warm_pass(fresh_bank(i))
             fresh_pass(i, 0)
-        w3_late = sbuf("w3_late", [P, 2 * CHUNK_VALUES], BF16, tag="turned0_1")
-        for c in range(W3_CHUNKS - 1):
-            stage_w3(c, 1, pass_part(w3_late, c), nc.scalar.copy)
+        w3_late = sbuf("w3_late", [P, PACK * LATE_ON_SCALAR], BF16, tag="turned0_1")
+        stage(w3_late[:], w3_raw[1][:, :, :LATE_ON_SCALAR], nc.scalar.copy)
         scatter(7)
 
         w3_plane = sbuf("w3_plane", [P, PASSES, N], U8, tag=taste_tag[last])
-        w3_end = sbuf("w3_end", [P, CHUNK_VALUES], BF16, tag=f"recent{last}")
+        w3_end = sbuf("w3_end", [P, PACK * (N - LATE_ON_SCALAR)], BF16, tag=f"recent{last}")
         quantize_w3(0, 0, w3_early[:, :CHUNK_VALUES])
         turn_half(last, 0, banks[4:6])
         turn_half(last, 1, banks[0:2])
@@ -441,11 +450,11 @@ def tile_list_shelf_suggester_kernel(
             gate_pass(i, 0)
         regroup_page(1, 1, banks[4:6])
         quantize_page(1, 1)
-        quantize_w3(0, 1, w3_early[:, CHUNK_VALUES:])
-        stage_w3(W3_CHUNKS - 1, 1, w3_end[:], nc.vector.tensor_copy)
+        quantize_w3(0, CHUNK, w3_early[:, CHUNK_VALUES:])
+        stage(w3_end[:], w3_raw[1][:, :, LATE_ON_SCALAR:], nc.vector.tensor_copy)
         quantize_page(0, 1, "table_words1")
         quantize_w3(1, 0, w3_late[:])
-        quantize_w3(1, W3_CHUNKS - 1, w3_end[:])
+        quantize_w3(1, LATE_ON_SCALAR, w3_end[:])
 
         def store_page_scales():
             scale_rows = out_3.bitcast(I32)

@@ -73,7 +73,7 @@ def tile_list_shelf_suggester_kernel(
         old = [sbuf(f"old{c}", [P, CHUNK // P, T2], F32) for c in range(W3_CHUNKS - 1)]
         w1_staged = [sbuf(f"w1_staged{i}", [P, PASSES * CHUNK_VALUES], BF16) for i in range(2)]
         w1_plane = [sbuf(f"w1_plane{c}", [P, PASSES * CHUNK], U8) for c in range(W1_CHUNKS)]
-        recent = {b: sbuf(f"recent{b}", [P, S], F32) for b in range(1, ROW_TILES)}
+        recent = {b: sbuf(f"recent{b}", [P, S], F32) for b in range(1, ROW_TILES - 1)}
         turned = {(g, h): [sbuf(f"turned{g}_{h}", [P, 4 * K_PASS], BF16)] for g in range(PASSES) for h in range(HALVES)}
         page_plane = sbuf("page_plane", [P, PASSES, T2], U8)
         w3_codes = sbuf("w3_codes", [P, PASSES, N], U32)
@@ -356,11 +356,11 @@ def tile_list_shelf_suggester_kernel(
         last = ROW_TILES - 1
 
         nc.vector.tensor_copy(picked_words[0][:], table_words[0][:].bitcast(U32).indirect(pick_list[:]))
-        for a in range(PASSES):
-            nc.vector.tensor_copy(picked_scales[a][:], table_scales[:, a, :].indirect(pick_list[:]))
-        for half in range(2):
-            picks = slice(half * S // 2, (half + 1) * S // 2)
-            offsets = pick_list[:, half * S // 32 : (half + 1) * S // 32]
+        halves = [(slice(h * S // 2, (h + 1) * S // 2), pick_list[:, h * S // 32 : (h + 1) * S // 32]) for h in range(2)]
+        for picks, offsets in halves:
+            nc.vector.tensor_copy(picked_scales[0][:, picks], table_scales[:, 0, :].indirect(offsets))
+        nc.vector.tensor_copy(picked_scales[1][:], table_scales[:, 1, :].indirect(pick_list[:]))
+        for picks, offsets in halves:
             nc.vector.tensor_copy(picked_words[1][:, picks], table_words[1][:].bitcast(U32).indirect(offsets))
         old.append(sbuf("old2", [P, CHUNK // P, T2], F32, tag="table_words0"))
         load_old(2)
@@ -371,9 +371,11 @@ def tile_list_shelf_suggester_kernel(
         recent_product(4, banks[0])
         recent_product(5, banks[4])
         recent_product(0, banks[7])
+        first_staged = sbuf("first_staged", [P, PACK * P], BF16)
+
         def first_values(a, first, width):
             at = a * CHUNK + first
-            return w1_staged[0][:, PACK * at : PACK * (at + width)]
+            return first_staged[:] if (a, first) == (1, 0) else w1_staged[0][:, PACK * at : PACK * (at + width)]
 
         def quantize_first(a, first, width, codes):
             at = a * CHUNK + first
@@ -392,10 +394,11 @@ def tile_list_shelf_suggester_kernel(
         taste_product(0, banks[0:1])
         second_pass[1] = sbuf("second_pass1", [P, P], U32, tag="second_pass")
         quantize_first(1, P, P, second_pass[1])
+        recent[last] = sbuf(f"recent{last}", [P, S], F32, tag="first_staged")
         for b, bank in ((6, 5), (7, 1)):
             recent_product(b, banks[bank])
         stage_w1(1)
-        taste_product(1, banks[2:3])
+        taste_product(1, banks[7:8])
         scatter(0)
 
         quantize_w1(1, [w1_staged[1][:]])
@@ -438,7 +441,7 @@ def tile_list_shelf_suggester_kernel(
         scatter(7)
 
         w3_plane = sbuf("w3_plane", [P, PASSES, N], U8, tag=taste_tag[last])
-        w3_end = sbuf("w3_end", [P, PACK * (N - LATE_ON_SCALAR)], BF16, tag=f"recent{last}")
+        w3_end = sbuf("w3_end", [P, PACK * (N - LATE_ON_SCALAR)], BF16, tag="first_staged")
         quantize_w3(0, 0, w3_early[:, :CHUNK_VALUES])
         turn_half(last, 0, banks[4:6])
         turn_half(last, 1, banks[0:2])

@@ -34,7 +34,7 @@ CHUNK_VALUES = CHUNK * PACK
 FIRST_TABLE_LOADS = 4
 AHEAD = 2
 ON_GPSIMD = 3
-LATE_ON_SCALAR = 384
+LATE_ON_SCALAR = 256
 WHOLE_ROWS = 4
 RESTS = 4
 STEPS = 5
@@ -71,7 +71,7 @@ def tile_list_shelf_suggester_kernel(
         w1_raw = [[sbuf(f"w1_raw{c}_{a}", [P, PACK, CHUNK], F32) for a in range(PASSES)] for c in range(W1_CHUNKS)]
         w3_raw = [sbuf(f"w3_raw{a}", [P, PACK, N], F32) for a in range(PASSES)]
         old = [sbuf(f"old{c}", [P, CHUNK // P, T2], F32) for c in range(W3_CHUNKS - 1)]
-        w1_staged = [sbuf(f"w1_staged{i}", [P, PASSES * CHUNK_VALUES], BF16) for i in range(2)]
+        w1_staged = {c: sbuf(f"w1_staged{c}", [P, PASSES * CHUNK_VALUES], BF16) for c in range(2)}
         w1_plane = [sbuf(f"w1_plane{c}", [P, PASSES * CHUNK], U8) for c in range(W1_CHUNKS)]
         recent = {b: sbuf(f"recent{b}", [P, S], F32) for b in range(1, ROW_TILES - 1)}
         turned = {(g, h): [sbuf(f"turned{g}_{h}", [P, 4 * K_PASS], BF16)] for g in range(PASSES) for h in range(HALVES)}
@@ -80,7 +80,7 @@ def tile_list_shelf_suggester_kernel(
         w1_codes, second_pass, page_codes, taste, grouped = {}, {}, {}, {}, {}
 
         taste_tag = {b: f"taste{b}" for b in range(ROW_TILES)}
-        taste_tag.update({1: "w1_raw1_1", 2: "w1_raw2_1", 4: "w1_raw3_1", 7: "w3_raw0"})
+        taste_tag.update({1: "w1_raw1_1", 2: "w1_raw2_1", 4: "w1_raw3_1"})
         grouped_tag = dict(zip(((g, h, s) for g, h in sorted(turned) for s in range(2)), ("w1_raw0_1", "", "w1_raw2_1", "", "taste0", "taste3", "taste5", "recent6")))
 
         nc.vector.memset(table_scales[:].bitcast(I32), 0)
@@ -158,7 +158,7 @@ def tile_list_shelf_suggester_kernel(
 
         def stage_w1(c, passes=(0, 1)):
             for a in passes:
-                stage(pass_part(w1_staged[c % 2], a), w1_raw[c][a][:], nc.scalar.copy)
+                stage(pass_part(w1_staged[c], a), w1_raw[c][a][:], nc.scalar.copy)
 
         def stage_w3(c, a, dst, copy):
             stage(dst, w3_raw[a][:, :, c * CHUNK : (c + 1) * CHUNK], copy)
@@ -402,16 +402,18 @@ def tile_list_shelf_suggester_kernel(
         scatter(0)
 
         quantize_w1(1, [w1_staged[1][:]])
+        w1_staged[2] = sbuf("w1_staged2", [P, PASSES * CHUNK_VALUES], BF16, tag="w1_staged1")
         stage_w1(2)
         taste_product(2, banks[0:4])
         scatter(1)
-        quantize_w1(2, [w1_staged[0][:]])
+        quantize_w1(2, [w1_staged[2][:]])
         taste_product(3, banks[2:4])
+        w1_staged[3] = sbuf("w1_staged3", [P, PASSES * CHUNK_VALUES], BF16, tag="w1_staged1")
         stage_w1(3, (0,))
         turn_page(0, banks[0:2])
         stage_w1(3, (1,))
         scatter(2)
-        quantize_w1(3, [w1_staged[1][:]])
+        quantize_w1(3, [w1_staged[3][:]])
         turn_page(1, banks[2:4])
         taste_product(4, banks[6:8])
         taste_product(5, banks[4:6])
@@ -426,8 +428,8 @@ def tile_list_shelf_suggester_kernel(
         regroup_page(0, 0, banks[2:4])
         scatter(5)
         turn_page(4, banks[4:6])
-        stage_w3(2, 0, pass_part(w3_early, 2), nc.scalar.copy)
         taste_product(7, banks[6:8] + banks[2:4])
+        stage_w3(2, 0, pass_part(w3_early, 2), nc.scalar.copy)
         regroup_page(0, 1, banks[0:2])
         scatter(6)
         quantize_page(0, 0)

@@ -336,7 +336,7 @@ def tile_list_shelf_suggester_kernel(
         def blend_begin(i):
             nc.scalar.activation(out=rest[i % RESTS][:], in_=gate_bank(i)[:], func=SIGMOID, scale=-1.0)
             nc.vector.tensor_tensor(out=by_tiles(i, step[i % STEPS]), in0=by_tiles(i, fresh_bank(i)), in1=scores(i), op=SUB)
-            engine = nc.vector if i in (0, 10) else nc.gpsimd
+            engine = nc.vector if i in (1, 10) else nc.gpsimd
             for cols in parts(i):
                 engine.tensor_tensor(out=step[i % STEPS][:, cols], in0=step[i % STEPS][:, cols], in1=rest[i % RESTS][:, cols], op=MULT)
 

@@ -34,7 +34,7 @@ CHUNK_VALUES = CHUNK * PACK
 FIRST_TABLE_LOADS = 4
 AHEAD = 2
 ON_GPSIMD = 3
-LATE_ON_SCALAR = 256
+LATE_ON_SCALAR = 512
 WHOLE_ROWS = 4
 RESTS = 4
 STEPS = 5
@@ -434,12 +434,12 @@ def tile_list_shelf_suggester_kernel(
         scatter(6)
         quantize_page(0, 0)
         turn_page(5, banks[4:6])
+        w3_late = sbuf("w3_late", [P, PACK * LATE_ON_SCALAR], BF16, tag="turned0_1")
+        stage(w3_late[:], w3_raw[1][:, :, :LATE_ON_SCALAR], nc.scalar.copy)
         turn_page(6, banks[6:8])
         for i in range(AHEAD):
             warm_pass(fresh_bank(i))
             fresh_pass(i, 0)
-        w3_late = sbuf("w3_late", [P, PACK * LATE_ON_SCALAR], BF16, tag="turned0_1")
-        stage(w3_late[:], w3_raw[1][:, :, :LATE_ON_SCALAR], nc.scalar.copy)
         scatter(7)
 
         w3_plane = sbuf("w3_plane", [P, PASSES, N], U8, tag=taste_tag[last])

@@ -31,7 +31,6 @@ CHUNK = 256
 W1_CHUNKS = H // CHUNK
 W3_CHUNKS = N // CHUNK
 CHUNK_VALUES = CHUNK * PACK
-FIRST_TABLE_LOADS = 4
 AHEAD = 2
 ON_GPSIMD = 3
 LATE_ON_SCALAR = 512
@@ -59,7 +58,7 @@ def tile_list_shelf_suggester_kernel(
         put_list = keep.tile([P, S // 16], U16, name="put_list")
         identity = sbuf("identity", [P, P], F32)
         table_words = [sbuf(f"table_words{a}", [P, T], I32) for a in range(PASSES)]
-        table_scales = sbuf("table_scales", [P, PASSES, T], U8)
+        table_rows = sbuf("table_rows", [P, T], U8)
         picked_words = [sbuf(f"picked_words{a}", [P, S], U32) for a in range(PASSES)]
         picked_scales = [sbuf(f"picked_scales{a}", [P, S], U8) for a in range(PASSES)]
         w2_codes = [sbuf(f"w2_codes{g}", [P, PASSES, 2 * K_PASS], U8) for g in range(PASSES)]
@@ -83,8 +82,9 @@ def tile_list_shelf_suggester_kernel(
         taste_tag.update({1: "w1_raw1_1", 2: "w1_raw2_1", 4: "w1_raw3_1"})
         grouped_tag = dict(zip(((g, h, s) for g, h in sorted(turned) for s in range(2)), ("w1_raw0_1", "", "w1_raw2_1", "", "taste0", "taste3", "taste5", "recent6")))
 
-        nc.vector.memset(table_scales[:].bitcast(I32), 0)
+        nc.gpsimd.memset(table_rows[:].bitcast(I32), 0)
         nc.vector.memset(w2_plane[:].bitcast(I32), 0)
+        nc.vector.memset(picked_scales[1][:].bitcast(I32), 0)
         nc.gpsimd.memset(w4_plane[:].bitcast(I32), 0)
         make_identity(nc, identity[:])
 
@@ -96,6 +96,17 @@ def tile_list_shelf_suggester_kernel(
             for r in range(4):
                 nc.sync.dma_start(out=plane[r:P:32].bitcast(I32), in_=rows[:, r:16:4, :].rearrange("a q n -> q a n"))
 
+        def load_table_rows():
+            rows = tab_scales.bitcast(I32)
+            for r in range(4):
+                nc.sync.dma_start(out=table_rows[r:P:32].bitcast(I32), in_=rows[0, r:16:4, :])
+            nc.sync.dma_start(out=table_rows[4:P:8].bitcast(I32), in_=rows[1].rearrange("(q r) t -> r q t", r=4))
+
+        def pick_scales():
+            nc.vector.tensor_copy(picked_scales[0][:], table_rows[:].indirect(pick_list[:]))
+            for r in range(4):
+                nc.sync.dma_start(out=picked_scales[1][r:P:32].bitcast(I32), in_=picked_scales[0][32 * r + 4 : 32 * (r + 1) : 8].bitcast(I32))
+
         def load_pass(tile, w, a, first):
             rows = w[a * K_PASS : (a + 1) * K_PASS, first : first + tile.shape[2]]
             nc.sync.dma_start(out=tile[:], in_=rows.rearrange("(p j) c -> p j c", j=PACK))
@@ -106,15 +117,14 @@ def tile_list_shelf_suggester_kernel(
         def load_w3(a):
             load_pass(w3_raw[a], w3, a, 0)
 
-        def load_table_words(a, loads):
+        def load_table_words(a, *cuts):
             words = tab_words[a].rearrange("p t i -> p (t i)").bitcast(I32)
-            for i in range(loads):
-                cols = slice(i * T // loads, (i + 1) * T // loads)
-                nc.sync.dma_start(out=table_words[a][:, cols], in_=words[:, cols])
+            for first, end in zip(cuts, cuts[1:]):
+                nc.sync.dma_start(out=table_words[a][:, first:end], in_=words[:, first:end])
 
-        def load_w2(g):
-            words = w2_words.bitcast(I32)[:, :, g * K_PASS // 2 : (g + 1) * K_PASS // 2]
-            nc.sync.dma_start(out=w2_codes[g][:].bitcast(I32), in_=words.rearrange("a p n -> p a n"))
+        def load_w2(g, passes=slice(0, PASSES)):
+            words = w2_words.bitcast(I32)[passes, :, g * K_PASS // 2 : (g + 1) * K_PASS // 2]
+            nc.sync.dma_start(out=w2_codes[g][:, passes, :].bitcast(I32), in_=words.rearrange("a p n -> p a n"))
 
         def load_page(b):
             nc.sync.dma_start(out=page[b][:], in_=page0[b * P : (b + 1) * P, :])
@@ -124,16 +134,19 @@ def tile_list_shelf_suggester_kernel(
             nc.sync.dma_start(out=old[c][:], in_=rows.rearrange("(i p) m -> p i m", p=P))
 
         nc.sync.dma_start(pick_list[:], offs)
-        load_table_words(0, FIRST_TABLE_LOADS)
-        load_plane(table_scales, tab_scales)
-        load_w2(0)
+        nc.sync.dma_start(put_list[:], offs2)
+        load_w2(0, slice(0, 1))
+        load_w2(0, slice(1, 2))
+        load_table_words(0, 0, T // 2)
+        load_table_rows()
+        load_table_words(0, T // 2, T)
         load_plane(w2_plane, w2_scales)
-        load_table_words(1, 1)
+        load_table_words(1, 0, T // 4, T // 2, 3 * T // 4, T)
+        pick_scales()
         nc.sync.dma_start(out=weights[:], in_=wgs)
         load_w2(1)
         load_w1(0, 0)
         load_w1(0, 1)
-        nc.sync.dma_start(put_list[:], offs2)
         load_page(0)
         for c in range(1, W1_CHUNKS):
             for a in range(PASSES):
@@ -357,9 +370,6 @@ def tile_list_shelf_suggester_kernel(
 
         nc.vector.tensor_copy(picked_words[0][:], table_words[0][:].bitcast(U32).indirect(pick_list[:]))
         halves = [(slice(h * S // 2, (h + 1) * S // 2), pick_list[:, h * S // 32 : (h + 1) * S // 32]) for h in range(2)]
-        for picks, offsets in halves:
-            nc.vector.tensor_copy(picked_scales[0][:, picks], table_scales[:, 0, :].indirect(offsets))
-        nc.vector.tensor_copy(picked_scales[1][:], table_scales[:, 1, :].indirect(pick_list[:]))
         for picks, offsets in halves:
             nc.vector.tensor_copy(picked_words[1][:, picks], table_words[1][:].bitcast(U32).indirect(offsets))
         old.append(sbuf("old2", [P, CHUNK // P, T2], F32, tag="table_words0"))

@@ -141,7 +141,7 @@ def tile_list_shelf_suggester_kernel(
         load_table_rows()
         load_table_words(0, T // 2, T)
         load_plane(w2_plane, w2_scales)
-        load_table_words(1, 0, T // 4, T // 2, 3 * T // 4, T)
+        load_table_words(1, 0, T)
         pick_scales()
         nc.sync.dma_start(out=weights[:], in_=wgs)
         load_w2(1)

@@ -102,8 +102,12 @@ def tile_list_shelf_suggester_kernel(
                 nc.sync.dma_start(out=table_rows[r:P:32].bitcast(I32), in_=rows[0, r:16:4, :])
             nc.sync.dma_start(out=table_rows[4:P:8].bitcast(I32), in_=rows[1].rearrange("(q r) t -> r q t", r=4))
 
+        halves = [(slice(h * S // 2, (h + 1) * S // 2), pick_list[:, h * S // 32 : (h + 1) * S // 32]) for h in range(2)]
+
         def pick_scales():
-            nc.vector.tensor_copy(picked_scales[0][:], table_rows[:].indirect(pick_list[:]))
+            for picks, offsets in halves:
+                nc.vector.tensor_copy(picked_scales[0][:, picks], table_rows[:].indirect(offsets))
+                nc.vector.tensor_copy(picked_words[0][:, picks], table_words[0][:].bitcast(U32).indirect(offsets))
             for r in range(4):
                 nc.sync.dma_start(out=picked_scales[1][r:P:32].bitcast(I32), in_=picked_scales[0][32 * r + 4 : 32 * (r + 1) : 8].bitcast(I32))
 
@@ -135,11 +139,10 @@ def tile_list_shelf_suggester_kernel(
 
         nc.sync.dma_start(pick_list[:], offs)
         nc.sync.dma_start(put_list[:], offs2)
-        load_w2(0, slice(0, 1))
-        load_w2(0, slice(1, 2))
-        load_table_words(0, 0, T // 2)
+        load_table_words(0, 0, T // 4, T // 2)
         load_table_rows()
         load_table_words(0, T // 2, T)
+        load_w2(0)
         load_plane(w2_plane, w2_scales)
         load_table_words(1, 0, T)
         pick_scales()
@@ -368,8 +371,6 @@ def tile_list_shelf_suggester_kernel(
 
         last = ROW_TILES - 1
 
-        nc.vector.tensor_copy(picked_words[0][:], table_words[0][:].bitcast(U32).indirect(pick_list[:]))
-        halves = [(slice(h * S // 2, (h + 1) * S // 2), pick_list[:, h * S // 32 : (h + 1) * S // 32]) for h in range(2)]
         for picks, offsets in halves:
             nc.vector.tensor_copy(picked_words[1][:, picks], table_words[1][:].bitcast(U32).indirect(offsets))
         old.append(sbuf("old2", [P, CHUNK // P, T2], F32, tag="table_words0"))

@@ -138,18 +138,19 @@ def tile_list_shelf_suggester_kernel(
             nc.sync.dma_start(out=old[c][:], in_=rows.rearrange("(i p) m -> p i m", p=P))
 
         nc.sync.dma_start(pick_list[:], offs)
-        nc.sync.dma_start(put_list[:], offs2)
-        load_table_words(0, 0, T // 4, T // 2)
+        load_table_words(0, 0, T // 2)
         load_table_rows()
         load_table_words(0, T // 2, T)
-        load_w2(0)
+        load_w2(0, slice(0, 1))
         load_plane(w2_plane, w2_scales)
         load_table_words(1, 0, T)
         pick_scales()
+        load_w2(0, slice(1, 2))
         nc.sync.dma_start(out=weights[:], in_=wgs)
         load_w2(1)
         load_w1(0, 0)
         load_w1(0, 1)
+        nc.sync.dma_start(put_list[:], offs2)
         load_page(0)
         for c in range(1, W1_CHUNKS):
             for a in range(PASSES):

@@ -138,9 +138,9 @@ def tile_list_shelf_suggester_kernel(
             nc.sync.dma_start(out=old[c][:], in_=rows.rearrange("(i p) m -> p i m", p=P))
 
         nc.sync.dma_start(pick_list[:], offs)
-        load_table_words(0, 0, T // 2)
+        load_table_words(0, 0, T // 4)
         load_table_rows()
-        load_table_words(0, T // 2, T)
+        load_table_words(0, T // 4, T)
         load_w2(0, slice(0, 1))
         load_plane(w2_plane, w2_scales)
         load_table_words(1, 0, T)

from contextlib import ExitStack

import concourse.mybir as mybir
from concourse.masks import make_identity

K, H, N, T, S, T2 = 1024, 1024, 768, 2048, 512, 1024
FLOPS = 2 * (2 * K * H * S) + 2 * (2 * H * N * T2)

F32 = mybir.dt.float32
BF16 = mybir.dt.bfloat16
I32 = mybir.dt.int32
U32 = mybir.dt.uint32
U16 = mybir.dt.uint16
U8 = mybir.dt.uint8
FP8X4 = mybir.dt.float8_e4m3fn_x4
FP4X4 = mybir.dt.float4_e2m1fn_x4
MULT = mybir.AluOpType.mult
SUB = mybir.AluOpType.subtract
SIGMOID = mybir.ActivationFunctionType.Sigmoid

P = 128
PACK = 4
K_PASS = P * PACK
PASSES = K // K_PASS
BANK = 512
ROW_TILES = H // P
TILES_PER_PASS = K_PASS // P
HALVES = T2 // BANK
QUARTER = BANK // 2
CHUNK = 256
W1_CHUNKS = H // CHUNK
W3_CHUNKS = N // CHUNK
CHUNK_VALUES = CHUNK * PACK
AHEAD = 2
ON_GPSIMD = 3
LATE_ON_SCALAR = 512
WHOLE_ROWS = 4
RESTS = 4
STEPS = 5
END_LAG = 2


def tile_list_shelf_suggester_kernel(
    tc, tab_words, tab_scales, offs, offs2, w1, w2_words, w2_scales, wgs, page0, w3, w4_words, w4_scales, prev,
    out_0, out_1, out_2, out_3,
):
    nc = tc.nc
    with ExitStack() as ctx:
        keep = ctx.enter_context(tc.tile_pool(name="keep", bufs=1))
        psum = ctx.enter_context(tc.psum_pool(name="psum", bufs=1))

        def sbuf(name, shape, dtype, tag=None):
            return keep.tile(shape, dtype, name=name, tag=tag or name, align_bytes=64)

        banks = [psum.tile([P, BANK], F32, name=f"bank{i}") for i in range(8)]

        pick_list = keep.tile([P, S // 16], U16, name="pick_list")
        put_list = keep.tile([P, S // 16], U16, name="put_list")
        identity = sbuf("identity", [P, P], F32)
        table_words = [sbuf(f"table_words{a}", [P, T], I32) for a in range(PASSES)]
        table_rows = sbuf("table_rows", [P, T], U8)
        picked_words = [sbuf(f"picked_words{a}", [P, S], U32) for a in range(PASSES)]
        picked_scales = [sbuf(f"picked_scales{a}", [P, S], U8) for a in range(PASSES)]
        w2_codes = [sbuf(f"w2_codes{g}", [P, PASSES, 2 * K_PASS], U8) for g in range(PASSES)]
        w2_plane = sbuf("w2_plane", [P, PASSES, H], U8)
        w4_codes = sbuf("w4_codes", [P, PASSES, 2 * N], U8)
        w4_plane = sbuf("w4_plane", [P, PASSES, N], U8)
        weights = sbuf("weights", [P, S], F32)
        page = [sbuf(f"page{b}", [P, T2], F32) for b in range(ROW_TILES)]
        w1_raw = [[sbuf(f"w1_raw{c}_{a}", [P, PACK, CHUNK], F32) for a in range(PASSES)] for c in range(W1_CHUNKS)]
        w3_raw = [sbuf(f"w3_raw{a}", [P, PACK, N], F32) for a in range(PASSES)]
        old = [sbuf(f"old{c}", [P, CHUNK // P, T2], F32) for c in range(W3_CHUNKS - 1)]
        w1_staged = {c: sbuf(f"w1_staged{c}", [P, PASSES * CHUNK_VALUES], BF16) for c in range(2)}
        w1_plane = [sbuf(f"w1_plane{c}", [P, PASSES * CHUNK], U8) for c in range(W1_CHUNKS)]
        recent = {b: sbuf(f"recent{b}", [P, S], F32) for b in range(1, ROW_TILES - 1)}
        turned = {(g, h): [sbuf(f"turned{g}_{h}", [P, 4 * K_PASS], BF16)] for g in range(PASSES) for h in range(HALVES)}
        page_plane = sbuf("page_plane", [P, PASSES, T2], U8)
        w3_codes = sbuf("w3_codes", [P, PASSES, N], U32)
        w1_codes, second_pass, page_codes, taste, grouped = {}, {}, {}, {}, {}

        taste_tag = {b: f"taste{b}" for b in range(ROW_TILES)}
        taste_tag.update({1: "w1_raw1_1", 2: "w1_raw2_1", 4: "w1_raw3_1"})
        grouped_tag = dict(zip(((g, h, s) for g, h in sorted(turned) for s in range(2)), ("w1_raw0_1", "", "w1_raw2_1", "", "taste0", "taste3", "taste5", "recent6")))

        nc.gpsimd.memset(table_rows[:].bitcast(I32), 0)
        nc.vector.memset(w2_plane[:].bitcast(I32), 0)
        nc.vector.memset(picked_scales[1][:].bitcast(I32), 0)
        nc.gpsimd.memset(w4_plane[:].bitcast(I32), 0)
        make_identity(nc, identity[:])

        warm = sbuf("warm", [P, 1], F32)
        nc.scalar.activation(out=warm[:], in_=identity[:, 0:1], func=SIGMOID)

        def load_plane(plane, scales):
            rows = scales.bitcast(I32)
            for r in range(4):
                nc.sync.dma_start(out=plane[r:P:32].bitcast(I32), in_=rows[:, r:16:4, :].rearrange("a q n -> q a n"))

        def load_table_rows():
            rows = tab_scales.bitcast(I32)
            for r in range(4):
                nc.sync.dma_start(out=table_rows[r:P:32].bitcast(I32), in_=rows[0, r:16:4, :])
            nc.sync.dma_start(out=table_rows[4:P:8].bitcast(I32), in_=rows[1].rearrange("(q r) t -> r q t", r=4))

        halves = [(slice(h * S // 2, (h + 1) * S // 2), pick_list[:, h * S // 32 : (h + 1) * S // 32]) for h in range(2)]

        def pick_scales():
            for picks, offsets in halves:
                nc.vector.tensor_copy(picked_scales[0][:, picks], table_rows[:].indirect(offsets))
                nc.vector.tensor_copy(picked_words[0][:, picks], table_words[0][:].bitcast(U32).indirect(offsets))
            for r in range(4):
                nc.sync.dma_start(out=picked_scales[1][r:P:32].bitcast(I32), in_=picked_scales[0][32 * r + 4 : 32 * (r + 1) : 8].bitcast(I32))

        def load_pass(tile, w, a, first):
            rows = w[a * K_PASS : (a + 1) * K_PASS, first : first + tile.shape[2]]
            nc.sync.dma_start(out=tile[:], in_=rows.rearrange("(p j) c -> p j c", j=PACK))

        def load_w1(c, a):
            load_pass(w1_raw[c][a], w1, a, c * CHUNK)

        def load_w3(a):
            load_pass(w3_raw[a], w3, a, 0)

        def load_table_words(a, *cuts):
            words = tab_words[a].rearrange("p t i -> p (t i)").bitcast(I32)
            for first, end in zip(cuts, cuts[1:]):
                nc.sync.dma_start(out=table_words[a][:, first:end], in_=words[:, first:end])

        def load_w2(g, passes=slice(0, PASSES)):
            words = w2_words.bitcast(I32)[passes, :, g * K_PASS // 2 : (g + 1) * K_PASS // 2]
            nc.sync.dma_start(out=w2_codes[g][:, passes, :].bitcast(I32), in_=words.rearrange("a p n -> p a n"))

        def load_page(b):
            nc.sync.dma_start(out=page[b][:], in_=page0[b * P : (b + 1) * P, :])

        def load_old(c):
            rows = prev[c * CHUNK : (c + 1) * CHUNK, :]
            nc.sync.dma_start(out=old[c][:], in_=rows.rearrange("(i p) m -> p i m", p=P))

        nc.sync.dma_start(pick_list[:], offs)
        load_table_words(0, 0, T // 4)
        load_table_rows()
        load_table_words(0, T // 4, T)
        load_w2(0, slice(0, 1))
        load_plane(w2_plane, w2_scales)
        load_table_words(1, 0, T)
        pick_scales()
        load_w2(0, slice(1, 2))
        nc.sync.dma_start(out=weights[:], in_=wgs)
        load_w2(1)
        load_w1(0, 0)
        load_w1(0, 1)
        nc.sync.dma_start(put_list[:], offs2)
        load_page(0)
        for c in range(1, W1_CHUNKS):
            for a in range(PASSES):
                load_w1(c, a)
            load_page(c)
        load_w3(0)
        load_page(4)
        load_page(5)
        load_page(6)
        load_w3(1)
        nc.sync.dma_start(out=w4_codes[:].bitcast(I32), in_=w4_words.bitcast(I32).rearrange("a p n -> p a n"))
        load_plane(w4_plane, w4_scales)
        load_page(7)
        load_old(0)
        load_old(1)

        def stage(dst, src, copy):
            copy(out=dst.rearrange("p (c i j) -> p c j i", i=4, j=PACK), in_=src.rearrange("p j (c i) -> p c j i", i=4))

        def pass_part(staged, a):
            return staged[:, a * CHUNK_VALUES : (a + 1) * CHUNK_VALUES]

        def stage_w1(c, passes=(0, 1)):
            for a in passes:
                stage(pass_part(w1_staged[c], a), w1_raw[c][a][:], nc.scalar.copy)

        def stage_w3(c, a, dst, copy):
            stage(dst, w3_raw[a][:, :, c * CHUNK : (c + 1) * CHUNK], copy)

        def quantize_chunk(codes, plane, parts):
            words = PASSES * CHUNK // len(parts)
            for i, part in enumerate(parts):
                cols = slice(i * words, (i + 1) * words)
                nc.vector.quantize_mx(out=codes[:, cols].bitcast(FP8X4), scales=plane[:, cols], in_=part)

        def quantize_w1(c, parts):
            w1_codes[c] = sbuf(f"w1_codes{c}", [P, PASSES * CHUNK], U32)
            quantize_chunk(w1_codes[c], w1_plane[c], parts)

        def quantize_w3(a, first, values):
            cols = slice(first, first + values.shape[1] // PACK)
            nc.vector.quantize_mx(out=w3_codes[:, a, cols].bitcast(FP8X4), scales=w3_plane[:, a, cols], in_=values)

        def chunk_columns(tile, a):
            first = a * CHUNK + tile % 2 * P
            return slice(first, first + P)

        def weigh(dst, bank):
            nc.vector.tensor_tensor(out=dst[:], in0=bank[:], in1=weights[:], op=MULT)

        def recent_product(b, bank, picks=slice(0, S)):
            g, col = divmod(b * P, K_PASS)
            sums = bank[:, : picks.stop - picks.start]
            for a in range(PASSES):
                nc.tensor.matmul_mx(
                    out=sums,
                    lhsT=w2_codes[g][:, a, 2 * col : 2 * (col + P)].bitcast(FP4X4),
                    lhsT_scale=w2_plane[:, a, b * P : (b + 1) * P],
                    rhs=picked_words[a][:, picks].bitcast(FP8X4), rhs_scale=picked_scales[a][:, picks],
                    start=(a == 0), stop=(a == PASSES - 1),
                )
            if b == ON_GPSIMD:
                nc.scalar.copy(out=recent[b][:, picks], in_=sums)
            elif b:
                nc.vector.tensor_tensor(out=recent[b][:, picks], in0=sums, in1=weights[:, picks], op=MULT)

        def taste_product(b, homes):
            taste[b] = sbuf(f"taste{b}", [P, S], F32, tag=taste_tag[b])
            parts = len(homes)
            for i in range(parts):
                picks = slice(i * S // parts, (i + 1) * S // parts)
                sums = homes[i][:, : S // parts]
                for a in range(PASSES):
                    cols = chunk_columns(b, a)
                    nc.tensor.matmul_mx(
                        out=sums,
                        lhsT=(second_pass[b][:] if a and b in second_pass else w1_codes[b // 2][:, cols]).bitcast(FP8X4), lhsT_scale=w1_plane[b // 2][:, cols],
                        rhs=picked_words[a][:, picks].bitcast(FP8X4), rhs_scale=picked_scales[a][:, picks],
                        start=(a == 0), stop=(a == PASSES - 1),
                    )
                if b == 0:
                    weigh(taste[b], homes[i])
                else:
                    nc.scalar.copy(out=taste[b][:, picks], in_=sums)

        def scatter(b):
            nc.vector.tensor_tensor(page[b][:].indirect(put_list[:]), recent[b][:], taste[b][:], MULT)
            nc.sync.dma_start(out=out_1[b * P : (b + 1) * P, :], in_=page[b][:])

        def turn_half(b, h, homes):
            g, q = divmod(b, TILES_PER_PASS)
            blocks = 4 // len(homes)
            for k in range(4):
                col = h * BANK + k * P
                at = k % blocks * P
                nc.tensor.transpose(homes[k // blocks][:, at : at + P], page[b][:, col : col + P], identity[:])
            tiles = turned[g, h]
            run = 4 // max(len(homes), len(tiles))
            for k in range(0, 4, run):
                at = k % blocks * P
                src = homes[k // blocks][:, at : at + run * P]
                tile, first = tiles[k * len(tiles) // 4], k % (4 // len(tiles))
                dst = tile[:].rearrange("m (j u p e) -> m j u p e", u=2, p=P, e=2)[:, first : first + run, :, 32 * q : 32 * (q + 1), :]
                nc.scalar.copy(out=dst, in_=src.rearrange("m (j p u e) -> m j u p e", j=run, u=2, e=2))

        def turn_page(b, two_banks):
            for h in range(HALVES):
                turn_half(b, h, two_banks[h : h + 1])

        def regroup_part(g, h, s, homes):
            tiles = turned[g, h]
            words = tiles[s][:].bitcast(F32) if len(tiles) == 2 else tiles[0][:].bitcast(F32)[:, s * BANK : (s + 1) * BANK]
            blocks = 2 // len(homes)
            for j in range(2):
                for u in range(2):
                    at = (j % blocks * 2 + u) * P
                    col = (2 * j + u) * P
                    nc.tensor.transpose(homes[j // blocks][:, at : at + P], words[:, col : col + P], identity[:])
            for i, bank in enumerate(homes):
                width = blocks * 2 * P
                first = i * width
                dst = grouped[g, h, s].bitcast(F32)[:, first : first + width].rearrange("p (j m u) -> p j m u", j=blocks, u=2)
                nc.scalar.copy(out=dst, in_=bank[:, :width].rearrange("p (j u m) -> p j m u", j=blocks, u=2))

        def regroup_page(g, h, homes):
            if g == 0:
                both = sbuf(f"grouped{g}_{h}", [P, 4 * BANK], BF16, tag=grouped_tag[g, h, 0])
                grouped[g, h] = both[:]
            for s in range(2):
                if g == 0:
                    grouped[g, h, s] = both[:, s * 2 * BANK : (s + 1) * 2 * BANK]
                else:
                    grouped[g, h, s] = sbuf(f"grouped{g}_{h}_{s}", [P, 2 * BANK], BF16, tag=grouped_tag[g, h, s])[:]
            regroup_part(g, h, 0, homes[:1])
            regroup_part(g, h, 1, homes[1:])

        last_words = sbuf("last_words", [P, T2], U32)

        def quantize_page(g, h, tag=None):
            cols = slice(h * BANK, (h + 1) * BANK)
            page_codes[g, h] = last_words[:, cols] if g else sbuf(f"page_codes{g}_{h}", [P, BANK], U32, tag=tag)
            parts = [grouped[g, h, s] for s in range(2)] if g else [grouped[g, h]]
            width = BANK // len(parts)
            for s, part in enumerate(parts):
                first = s * width
                nc.vector.quantize_mx(
                    out=page_codes[g, h][:, first : first + width].bitcast(FP8X4),
                    scales=page_plane[:, g, h * BANK + first : h * BANK + first + width],
                    in_=part,
                )
            words = out_2[g].rearrange("p m t -> p (m t)").bitcast(I32)
            if g == 0:
                nc.sync.dma_start(out=words[:, cols], in_=page_codes[g, h][:].bitcast(I32))
            elif h == HALVES - 1:
                nc.sync.dma_start(out=words, in_=last_words[:].bitcast(I32))

        pieces = [(0, 2, q * QUARTER, QUARTER) for q in range(T2 // QUARTER)]
        pieces.extend((n, 1, h * BANK, BANK) for n in range(2, N // P) for h in (1, 0))

        def gate_bank(i):
            return banks[(0, 1, 5)[i % 3]]

        def fresh_bank(i):
            return banks[(2, 3, 6, 7, 4)[i % STEPS]]

        def piece_pass(i, g, bank, stationary):
            first, tiles, col, width = pieces[i]
            h, at = divmod(col, BANK)
            for k in range(tiles):
                codes, plane = stationary(first + k)
                nc.tensor.matmul_mx(
                    out=bank[:, k * width : (k + 1) * width], lhsT=codes, lhsT_scale=plane,
                    rhs=page_codes[g, h][:, at : at + width].bitcast(FP8X4), rhs_scale=page_plane[:, g, col : col + width],
                    start=(g == 0 and k == 0), stop=(g == PASSES - 1 and k == tiles - 1),
                )

        def gate_pass(i, g):
            piece_pass(i, g, gate_bank(i), lambda n: (w3_codes[:, g, n * P : (n + 1) * P].bitcast(FP8X4), w3_plane[:, g, n * P : (n + 1) * P]))

        def fresh_pass(i, g):
            piece_pass(i, g, fresh_bank(i), lambda n: (w4_codes[:, g, 2 * n * P : 2 * (n + 1) * P].bitcast(FP4X4), w4_plane[:, g, n * P : (n + 1) * P]))

        def warm_pass(bank):
            nc.tensor.matmul_mx(
                out=bank[:], lhsT=w4_codes[:, 0, : 2 * P].bitcast(FP4X4), lhsT_scale=w4_plane[:, 0, :P],
                rhs=page_codes[0, 0][:].bitcast(FP8X4), rhs_scale=page_plane[:, 0, :BANK], start=True, stop=True,
            )

        def scores(i):
            first, tiles, col, width = pieces[i]
            return old[first // 2][:, first % 2 : first % 2 + tiles, col : col + width]

        def by_tiles(i, tile):
            return tile[:].rearrange("p (k m) -> p k m", k=pieces[i][1])

        def parts(i):
            cuts = (0, QUARTER, BANK) if i == len(pieces) - 1 else (0, BANK)
            return [slice(a, b) for a, b in zip(cuts, cuts[1:])]

        def blend_begin(i):
            nc.scalar.activation(out=rest[i % RESTS][:], in_=gate_bank(i)[:], func=SIGMOID, scale=-1.0)
            nc.vector.tensor_tensor(out=by_tiles(i, step[i % STEPS]), in0=by_tiles(i, fresh_bank(i)), in1=scores(i), op=SUB)
            engine = nc.vector if i in (1, 10) else nc.gpsimd
            for cols in parts(i):
                engine.tensor_tensor(out=step[i % STEPS][:, cols], in0=step[i % STEPS][:, cols], in1=rest[i % RESTS][:, cols], op=MULT)

        def blend_end(i):
            first, tiles, col, width = pieces[i]
            if first >= WHOLE_ROWS:
                for cols in parts(i):
                    new = old[first // 2][:, first % 2, col + cols.start : col + cols.stop]
                    nc.vector.tensor_tensor(out=new, in0=fresh_bank(i)[:, cols], in1=step[i % STEPS][:, cols], op=SUB)
                    nc.sync.dma_start(out=out_0[first * P : (first + 1) * P, col + cols.start : col + cols.stop], in_=new)
                return
            nc.vector.tensor_tensor(out=scores(i), in0=by_tiles(i, fresh_bank(i)), in1=by_tiles(i, step[i % STEPS]), op=SUB)
            if i + 1 == len(pieces) or pieces[i + 1][0] != first:
                for n in range(first, first + tiles):
                    nc.sync.dma_start(out=out_0[n * P : (n + 1) * P, :], in_=old[n // 2][:, n % 2, :])

        last = ROW_TILES - 1

        for picks, offsets in halves:
            nc.vector.tensor_copy(picked_words[1][:, picks], table_words[1][:].bitcast(U32).indirect(offsets))
        old.append(sbuf("old2", [P, CHUNK // P, T2], F32, tag="table_words0"))
        load_old(2)
        for half in range(2):
            for b in (1, 2, 3):
                recent_product(b, banks[b + 3 * (1 - half)], slice(half * S // 2, (half + 1) * S // 2))
        nc.gpsimd.tensor_tensor(out=recent[ON_GPSIMD][:], in0=recent[ON_GPSIMD][:], in1=weights[:], op=MULT)
        recent_product(4, banks[0])
        recent_product(5, banks[4])
        recent_product(0, banks[7])
        first_staged = sbuf("first_staged", [P, PACK * P], BF16)

        def first_values(a, first, width):
            at = a * CHUNK + first
            return first_staged[:] if (a, first) == (1, 0) else w1_staged[0][:, PACK * at : PACK * (at + width)]

        def quantize_first(a, first, width, codes):
            at = a * CHUNK + first
            nc.vector.quantize_mx(out=codes[:].bitcast(FP8X4), scales=w1_plane[0][:, at : at + width], in_=first_values(a, first, width))

        w1_codes[0] = sbuf("w1_codes0", [P, CHUNK], U32)
        stage(first_values(0, 0, CHUNK), w1_raw[0][0][:], nc.scalar.copy)
        quantize_first(0, 0, CHUNK, w1_codes[0])
        for b in range(2):
            stage(first_values(1, b * P, P), w1_raw[0][1][:, :, b * P : (b + 1) * P], nc.scalar.copy)
            if b == 0:
                recent[0] = sbuf("recent0", [P, S], F32, tag="w1_raw0_0")
                nc.scalar.copy(out=recent[0][:], in_=banks[7][:])
        second_pass[0] = sbuf("second_pass0", [P, P], U32, tag="second_pass")
        quantize_first(1, 0, P, second_pass[0])
        taste_product(0, banks[0:1])
        second_pass[1] = sbuf("second_pass1", [P, P], U32, tag="second_pass")
        quantize_first(1, P, P, second_pass[1])
        recent[last] = sbuf(f"recent{last}", [P, S], F32, tag="first_staged")
        for b, bank in ((6, 5), (7, 1)):
            recent_product(b, banks[bank])
        stage_w1(1)
        taste_product(1, banks[7:8])
        scatter(0)

        quantize_w1(1, [w1_staged[1][:]])
        w1_staged[2] = sbuf("w1_staged2", [P, PASSES * CHUNK_VALUES], BF16, tag="w1_staged1")
        stage_w1(2)
        taste_product(2, banks[0:4])
        scatter(1)
        quantize_w1(2, [w1_staged[2][:]])
        taste_product(3, banks[2:4])
        w1_staged[3] = sbuf("w1_staged3", [P, PASSES * CHUNK_VALUES], BF16, tag="w1_staged1")
        stage_w1(3, (0,))
        turn_page(0, banks[0:2])
        stage_w1(3, (1,))
        scatter(2)
        quantize_w1(3, [w1_staged[3][:]])
        turn_page(1, banks[2:4])
        taste_product(4, banks[6:8])
        taste_product(5, banks[4:6])
        scatter(3)
        turn_page(2, banks[6:8])
        w3_early = sbuf("w3_early", [P, W3_CHUNKS * CHUNK_VALUES], BF16, tag="table_words1")
        stage_w3(0, 0, pass_part(w3_early, 0), nc.scalar.copy)
        taste_product(6, banks[6:8])
        scatter(4)
        turn_page(3, banks[4:6])
        stage_w3(1, 0, pass_part(w3_early, 1), nc.scalar.copy)
        regroup_page(0, 0, banks[2:4])
        scatter(5)
        turn_page(4, banks[4:6])
        taste_product(7, banks[6:8] + banks[2:4])
        stage_w3(2, 0, pass_part(w3_early, 2), nc.scalar.copy)
        regroup_page(0, 1, banks[0:2])
        scatter(6)
        quantize_page(0, 0)
        turn_page(5, banks[4:6])
        w3_late = sbuf("w3_late", [P, PACK * LATE_ON_SCALAR], BF16, tag="turned0_1")
        stage(w3_late[:], w3_raw[1][:, :, :LATE_ON_SCALAR], nc.scalar.copy)
        turn_page(6, banks[6:8])
        for i in range(AHEAD):
            warm_pass(fresh_bank(i))
            fresh_pass(i, 0)
        scatter(7)

        w3_plane = sbuf("w3_plane", [P, PASSES, N], U8, tag=taste_tag[last])
        w3_end = sbuf("w3_end", [P, PACK * (N - LATE_ON_SCALAR)], BF16, tag="first_staged")
        quantize_w3(0, 0, w3_early[:, :CHUNK_VALUES])
        turn_half(last, 0, banks[4:6])
        turn_half(last, 1, banks[0:2])
        for bank in banks[6:8]:
            warm_pass(bank)
        regroup_page(1, 0, banks[6:8])
        quantize_page(1, 0)
        for i in range(AHEAD):
            gate_pass(i, 0)
        regroup_page(1, 1, banks[4:6])
        quantize_page(1, 1)
        quantize_w3(0, CHUNK, w3_early[:, CHUNK_VALUES:])
        stage(w3_end[:], w3_raw[1][:, :, LATE_ON_SCALAR:], nc.vector.tensor_copy)
        quantize_page(0, 1, "table_words1")
        quantize_w3(1, 0, w3_late[:])
        quantize_w3(1, LATE_ON_SCALAR, w3_end[:])

        def store_page_scales():
            scale_rows = out_3.bitcast(I32)
            for r in range(4):
                nc.sync.dma_start(
                    out=scale_rows[:, r:16:4, :].rearrange("g q m -> q g m"), in_=page_plane[r:P:32].bitcast(I32)
                )

        store_page_scales()
        rest = [sbuf(f"rest{i}", [P, BANK], F32, tag=f"w1_raw{i}_0") for i in range(RESTS)]
        step = [sbuf(f"step{i}", [P, BANK], F32, tag=f"recent{i + 1}") for i in range(STEPS)]
        for i in range(len(pieces)):
            for one_pass in (fresh_pass, gate_pass):
                for g in range(1 if i < AHEAD else 0, PASSES):
                    one_pass(i, g)
            blend_begin(i)
            if i >= END_LAG:
                blend_end(i - END_LAG)
        for i in range(len(pieces) - END_LAG, len(pieces)):
            blend_end(i)
